import numpy as np
import ml_dtypes


def mxq(x, axis, fmt="e4m3"):
    dtype, down = {"e4m3": (ml_dtypes.float8_e4m3fn, 7), "e5m2": (ml_dtypes.float8_e5m2, 14)}[fmt]
    v = np.moveaxis(np.asarray(x, np.float32).astype(ml_dtypes.bfloat16).astype(np.float64), axis, -1)
    blocks = v.reshape(v.shape[:-1] + (-1, 32))
    amax = np.abs(blocks).max(-1, keepdims=True)
    byte = np.maximum(np.where(amax > 0, np.frexp(amax)[1] - 1 + 127, 0) - down, 1)
    scale = np.exp2(byte - 127.0)
    codes = (blocks / scale).astype(np.float32).astype(dtype).astype(np.float64)
    return np.moveaxis((codes * scale).reshape(v.shape), -1, axis)


WIDE = False


def mx_kscale(k):
    if not WIDE:
        return np.ones(k)
    levels = np.array([10, -10, 5, -5, 0])
    if k % 512:
        return np.exp2(np.random.permutation(np.resize(levels, k // 32))).repeat(32)
    a = np.empty((k // 512, 16))
    for p in range(k // 512):
        a[p, :8] = np.random.permutation(np.resize(levels, 8))
        for g in range(8):
            far = levels[np.abs(levels - a[p, g]) >= 10]
            a[p, g + 8] = far[np.random.randint(len(far))]
    return np.exp2(a.ravel()).repeat(32)


def f64(x):
    return np.asarray(x).astype(np.float64)


def striped(idx):
    return np.tile(idx.reshape(-1, 16).T, (8, 1)).astype(np.uint16)


def unstriped(offs):
    return offs[:16].T.reshape(-1).astype(np.int64)


E2M1 = np.array([0.0, 0.5, 1.0, 1.5, 2.0, 3.0, 4.0, 6.0, -0.0, -0.5, -1.0, -1.5, -2.0, -3.0, -4.0, -6.0])


def pack_weight(w, fmt):
    k, n = w.shape
    w = f64(np.asarray(w, np.float32).astype(ml_dtypes.bfloat16)).reshape(k // 32, 32, n)
    amax = np.abs(w).max(1)
    if fmt == "e4m3":
        byte = np.frexp(amax)[1] - 1 + 127 - 7
    else:
        mant, ex = np.frexp(amax / 6.0)
        byte = np.where(mant > 0.5, ex, ex - 1) + 127
    byte = np.clip(np.where(amax > 0, byte, 1), 1, 254)
    scaled = (w * np.exp2(127.0 - byte)[:, None, :]).reshape(k, n).astype(np.float32)
    by_word = np.ascontiguousarray(scaled.reshape(k // 512, 128, 4, n).transpose(0, 1, 3, 2))
    if fmt == "e4m3":
        words = by_word.astype(ml_dtypes.float8_e4m3fn).view(np.uint8)
    else:
        c = by_word.astype(ml_dtypes.float4_e2m1fn).view(np.uint8) & 0xF
        words = (c[..., 0::2] | (c[..., 1::2] << 4)).reshape(k // 512, 128, 2 * n)
    return np.ascontiguousarray(words), np.ascontiguousarray(byte.astype(np.uint8).reshape(k // 512, 16, n))


def unpack_weight(words, scales, fmt):
    g, _, n = scales.shape
    words = np.ascontiguousarray(words).reshape(g, 128, n, -1)
    if fmt == "e4m3":
        vals = words.view(ml_dtypes.float8_e4m3fn).astype(np.float64)
    else:
        nib = np.empty((g, 128, n, 4), np.uint8)
        nib[..., 0::2] = words & 0xF
        nib[..., 1::2] = words >> 4
        vals = E2M1[nib]
    vals = vals * np.repeat(np.exp2(scales.astype(np.float64) - 127.0), 8, axis=1)[..., None]
    return vals.transpose(0, 1, 3, 2).reshape(g * 512, n)


K, T, E, C, N = 1536, 1536, 6, 256, 512
M = 256


def by_expert(wq, xq):
    return np.concatenate([wq[e].T @ xq[:, e * C:(e + 1) * C] for e in range(E)], axis=1)


def setup_inputs():
    n = np.random.standard_normal
    s = mx_kscale(K)[:, None]
    v = mx_kscale(N)
    x = pack_weight(n((K, T)) * s, "e4m3")
    return {
        "x_words": x[0],
        "x_scales": x[1],
        "w": (n((E, K, N)) / np.sqrt(K) / s[None] * v[None, None, :]).astype(np.float32),
        "b": (0.3 * n((N, E)) * v[:, None]).astype(np.float32),
        "wp": (n((N, M)) / np.sqrt(N) / v[:, None]).astype(np.float32),
        "gate": np.tile(np.random.uniform(0.2, 1.0, E * C), (N, 1)).astype(np.float32),
        "offs": striped(np.random.permutation(T)[:E * C]),
    }


def reference(x_words, x_scales, w, b, wp, gate, offs):
    idx = unstriped(offs)
    xq = unpack_weight(x_words, x_scales, "e4m3")[:, idx]
    y = by_expert(mxq(f64(w), 1, "e4m3"), xq)
    y = y + np.repeat(f64(b), C, axis=1)
    c = np.zeros((N, T))
    c[:, idx] = f64(gate) * y
    return mxq(f64(wp), 0, "e4m3").T @ mxq(c, 0, "e4m3")

@@ -1,0 +1,177 @@
+from contextlib import ExitStack
+
+import concourse.mybir as mybir
+
+K, T, E, C, N, M = 1536, 1536, 6, 256, 512, 256
+FLOPS = 2 * K * N * E * C + 2 * N * M * T
+BYTES = K * T + K * T // 32 + 4 * (E * K * N + N * E + N * M + 128 * E * C + M * T) + 2 * 128 * (T // 16)
+
+F32 = mybir.dt.float32
+BF16 = mybir.dt.bfloat16
+I32 = mybir.dt.int32
+U32 = mybir.dt.uint32
+U16 = mybir.dt.uint16
+U8 = mybir.dt.uint8
+FP8X4 = mybir.dt.float8_e4m3fn_x4
+IDENTITY = mybir.ActivationFunctionType.Identity
+MULT = mybir.AluOpType.mult
+
+P = 128
+PACK = 4
+KP = P * PACK
+PASSES = K // KP
+PAIR = 2
+LIST_COLS = C // 16
+GROUPS = N // (PACK * PAIR)
+
+VECTOR_PASSES = {(1, 2), (2, 2), (3, 2), (4, 2)}
+
+
+def tile_moe_nxt_lin_bias_kernel(tc, x_words, x_scales, w, b, wp, gate, offs, out):
+    nc = tc.nc
+    with ExitStack() as ctx:
+        keep = ctx.enter_context(tc.tile_pool(name="keep", bufs=1))
+        raws = ctx.enter_context(tc.tile_pool(name="raws", bufs=10))
+        halves = ctx.enter_context(tc.tile_pool(name="halves", bufs=1))
+        rounded = ctx.enter_context(tc.tile_pool(name="rounded", bufs=6))
+        codes = ctx.enter_context(tc.tile_pool(name="codes", bufs=6))
+        work = ctx.enter_context(tc.tile_pool(name="work", bufs=3))
+        picked = ctx.enter_context(tc.tile_pool(name="picked", bufs=E - 1))
+        ybanks = ctx.enter_context(tc.psum_pool(name="ybanks", bufs=6))
+        obanks = ctx.enter_context(tc.psum_pool(name="obanks", bufs=2))
+
+        offsets = keep.tile([P, T // 16], U16, name="offsets")
+        nc.sync.dma_start(offsets[:], offs)
+
+        xs = keep.tile([P, T // 4], I32, name="xs", align_bytes=64)
+        nc.gpsimd.memset(xs[:], 0)
+        b_raw = keep.tile([P, PACK, E], F32, name="b_raw")
+        b_rows = b.rearrange("(u j i) e -> i u j e", j=PACK, i=PAIR)
+        for i in range(PAIR):
+            nc.scalar.dma_start(out=b_raw[i:P:PAIR, :, :], in_=b_rows[i])
+        bias = keep.tile([P, PACK, E], F32, name="bias")
+        nc.scalar.activation(bias[:], b_raw[:], IDENTITY)
+
+        xw = [keep.tile([P, T], I32, name="xw%d" % a, align_bytes=64) for a in range(PASSES)]
+        gates = keep.tile([P, E * C], F32, name="gates")
+        wp_raw = keep.tile([P, PACK, M], F32, name="wp_raw")
+        result = [keep.tile([P, T], F32, name="result%d" % m) for m in range(M // P)]
+
+        def load_w(e, a):
+            rows = w[e, a * KP : (a + 1) * KP, :].rearrange("(p r) n -> p r n", r=PACK)
+            if (e, a) in ((0, 0), (E - 1, PASSES - 1)):
+                pieces = []
+                for h in range(2):
+                    raw = halves.tile([P, PACK, N // 2], F32, name="half%d_%d" % (e, h))
+                    nc.sync.dma_start(out=raw[:], in_=rows[:, :, h * N // 2 : (h + 1) * N // 2])
+                    on_vector = e > 0 and h == 1
+                    pieces.append((raw, h * GROUPS // 2, GROUPS // 2, on_vector))
+                return pieces
+            raw = raws.tile([P, PACK, N], F32, name="raw")
+            nc.sync.dma_start(out=raw[:], in_=rows)
+            return [(raw, 0, GROUPS, (e, a) in VECTOR_PASSES)]
+
+        def quantise_w(pieces):
+            wb = rounded.tile([P, N * PACK], BF16, name="wb", align_bytes=64)
+            view = wb[:].rearrange("p (j u i r) -> p u j r i", j=PACK, i=PAIR, r=PACK)
+            for raw, u0, count, on_vector in pieces:
+                src = raw[:].rearrange("p r (u j i) -> p u j r i", j=PACK, i=PAIR)
+                dst = view[:, u0 : u0 + count]
+                if on_vector:
+                    nc.vector.tensor_copy(out=dst, in_=src)
+                else:
+                    nc.scalar.copy(out=dst, in_=src)
+            wc = codes.tile([P, N], U32, name="wc", align_bytes=64)
+            ws = codes.tile([P, N], U8, name="ws", align_bytes=64)
+            nc.vector.quantize_mx(out=wc[:].bitcast(FP8X4), scales=ws[:], in_=wb[:])
+            return wc, ws
+
+        def load_x(a):
+            nc.sync.dma_start(out=xw[a][:], in_=x_words[a].rearrange("p t r -> p (t r)").bitcast(I32))
+
+        for a in range(PASSES):
+            load_x(a)
+        for q in range(4):
+            nc.sync.dma_start(
+                out=xs[32 * q : 32 * q + 4 * PASSES, :],
+                in_=x_scales[:, 4 * q : 4 * q + 4, :].bitcast(I32),
+            )
+        half_slots = E * C // 2
+        loaded = {}
+        for e in range(E):
+            for a in range(PASSES):
+                loaded[e, a] = load_w(e, a)
+                if (e, a) == (1, 0):
+                    nc.sync.dma_start(out=gates[:, :half_slots], in_=gate[:P, :half_slots])
+                    wp_rows = wp.rearrange("(u j i) f -> i u j f", j=PACK, i=PAIR)
+                    for i in range(PAIR):
+                        nc.sync.dma_start(out=wp_raw[i:P:PAIR, :, :], in_=wp_rows[i])
+                if (e, a) == (E // 2, 0):
+                    nc.sync.dma_start(out=gates[:, half_slots:], in_=gate[:P, half_slots:])
+
+        wp_codes = keep.tile([P, M], U32, name="wp_codes", align_bytes=64)
+        wp_scales = keep.tile([P, M], U8, name="wp_scales", align_bytes=64)
+
+        for e in range(E):
+            slots = slice(e * C, (e + 1) * C)
+            picks = offsets[:, e * LIST_COLS : (e + 1) * LIST_COLS]
+
+            gs = picked.tile([P, C], U8, name="gs", align_bytes=64)
+            nc.vector.tensor_copy(gs[:], xs[:].bitcast(U8).indirect(picks))
+            banks = [ybanks.tile([P, C], F32, name="ybank") for j in range(PACK)]
+            for a in range(PASSES):
+                gw = picked.tile([P, C], U32, name="gw%d" % a, align_bytes=64)
+                nc.vector.tensor_copy(gw[:], xw[a][:].bitcast(U32).indirect(picks))
+                wc, ws = quantise_w(loaded[e, a])
+                for j in range(PACK):
+                    cols = slice(j * P, (j + 1) * P)
+                    nc.tensor.matmul_mx(
+                        out=banks[j][:],
+                        lhsT=wc[:, cols].bitcast(FP8X4),
+                        lhsT_scale=ws[:, cols],
+                        rhs=gw[:].bitcast(FP8X4),
+                        rhs_scale=gs[4 * a : P, :],
+                        start=(a == 0),
+                        stop=(a == PASSES - 1),
+                    )
+
+            if e == 0:
+                wpb = keep.tile([P, M * PACK], BF16, name="wpb", align_bytes=64)
+                nc.vector.tensor_copy(
+                    out=wpb[:].rearrange("p (f i j) -> p f j i", i=PAIR, j=PACK),
+                    in_=wp_raw[:].rearrange("p j (f i) -> p f j i", i=PAIR),
+                )
+                nc.vector.quantize_mx(out=wp_codes[:].bitcast(FP8X4), scales=wp_scales[:], in_=wpb[:])
+
+            y = work.tile([P, PACK, C], F32, name="y")
+            for j in range(PACK):
+                nc.scalar.activation(y[:, j, :], banks[j][:], IDENTITY, bias=bias[:, j, e : e + 1])
+            cb = work.tile([P, C * PACK], BF16, name="cb", align_bytes=64)
+            nc.vector.tensor_tensor(
+                cb[:].rearrange("p (s i j) -> p s j i", i=PAIR, j=PACK),
+                y[:].rearrange("p j (s i) -> p s j i", i=PAIR),
+                gates[:, slots].rearrange("p (s i) -> p s i", i=PAIR).unsqueeze(2).to_broadcast([P, C // PAIR, PACK, PAIR]),
+                MULT,
+            )
+            cc = work.tile([P, C], U32, name="cc", align_bytes=64)
+            cs = work.tile([P, C], U8, name="cs", align_bytes=64)
+            nc.vector.quantize_mx(out=cc[:].bitcast(FP8X4), scales=cs[:], in_=cb[:])
+            obank = obanks.tile([P, M // P, C], F32, name="obank")
+            for m in range(M // P):
+                cols = slice(m * P, (m + 1) * P)
+                nc.tensor.matmul_mx(
+                    out=obank[:, m, :],
+                    lhsT=wp_codes[:, cols].bitcast(FP8X4),
+                    lhsT_scale=wp_scales[:, cols],
+                    rhs=cc[:].bitcast(FP8X4),
+                    rhs_scale=cs[:],
+                    start=True,
+                    stop=True,
+                )
+            o = work.tile([P, M // P, C], F32, name="o")
+            nc.scalar.copy(out=o[:], in_=obank[:])
+            for m in range(M // P):
+                nc.vector.tensor_copy(result[m][:].indirect(picks), o[:, m, :])
+
+        for m in range(M // P):
+            nc.sync.dma_start(out=out[m * P : (m + 1) * P, :], in_=result[m][:])

@@ -20,23 +20,29 @@ P = 128
 PACK = 4
 KP = P * PACK
 PASSES = K // KP
+STEPS = E * PASSES
 PAIR = 2
 LIST_COLS = C // 16
 GROUPS = N // (PACK * PAIR)
 
-VECTOR_PASSES = {(1, 2), (2, 2), (3, 2), (4, 2)}
+LOADS = "w00 x0 s w01 w02 x1 w10 x2 w11 w12 g0 p w20 w21 w22 w30 g1 w31 w32 w40 w41 w42 w50 w51 w52".split()
+SPLIT = {(0, 0), (5, 2)}
+CAST = {(5, 2): "SV"}
+BIAS_LAG = [2,2,2,2,2,2]
+OUT_LAG = [6,6,6,6,6,6]
+GW = 2
+GATE_ON_POOL = []
 
 
 def tile_moe_nxt_lin_bias_kernel(tc, x_words, x_scales, w, b, wp, gate, offs, out):
     nc = tc.nc
     with ExitStack() as ctx:
         keep = ctx.enter_context(tc.tile_pool(name="keep", bufs=1))
-        raws = ctx.enter_context(tc.tile_pool(name="raws", bufs=10))
-        halves = ctx.enter_context(tc.tile_pool(name="halves", bufs=1))
+        raws = ctx.enter_context(tc.tile_pool(name="raws", bufs=11))
         rounded = ctx.enter_context(tc.tile_pool(name="rounded", bufs=6))
-        codes = ctx.enter_context(tc.tile_pool(name="codes", bufs=6))
+        codes = ctx.enter_context(tc.tile_pool(name="codes", bufs=9))
         work = ctx.enter_context(tc.tile_pool(name="work", bufs=3))
-        picked = ctx.enter_context(tc.tile_pool(name="picked", bufs=E - 1))
+        picked = ctx.enter_context(tc.tile_pool(name="picked", bufs=2))
         ybanks = ctx.enter_context(tc.psum_pool(name="ybanks", bufs=6))
         obanks = ctx.enter_context(tc.psum_pool(name="obanks", bufs=2))
 
@@ -56,107 +62,115 @@ def tile_moe_nxt_lin_bias_kernel(tc, x_words, x_scales, w, b, wp, gate, offs, ou
         gates = keep.tile([P, E * C], F32, name="gates")
         wp_raw = keep.tile([P, PACK, M], F32, name="wp_raw")
         result = [keep.tile([P, T], F32, name="result%d" % m) for m in range(M // P)]
-
-        def load_w(e, a):
-            rows = w[e, a * KP : (a + 1) * KP, :].rearrange("(p r) n -> p r n", r=PACK)
-            if (e, a) in ((0, 0), (E - 1, PASSES - 1)):
-                pieces = []
-                for h in range(2):
-                    raw = halves.tile([P, PACK, N // 2], F32, name="half%d_%d" % (e, h))
-                    nc.sync.dma_start(out=raw[:], in_=rows[:, :, h * N // 2 : (h + 1) * N // 2])
-                    on_vector = e > 0 and h == 1
-                    pieces.append((raw, h * GROUPS // 2, GROUPS // 2, on_vector))
-                return pieces
-            raw = raws.tile([P, PACK, N], F32, name="raw")
-            nc.sync.dma_start(out=raw[:], in_=rows)
-            return [(raw, 0, GROUPS, (e, a) in VECTOR_PASSES)]
-
-        def quantise_w(pieces):
-            wb = rounded.tile([P, N * PACK], BF16, name="wb", align_bytes=64)
-            view = wb[:].rearrange("p (j u i r) -> p u j r i", j=PACK, i=PAIR, r=PACK)
-            for raw, u0, count, on_vector in pieces:
-                src = raw[:].rearrange("p r (u j i) -> p u j r i", j=PACK, i=PAIR)
-                dst = view[:, u0 : u0 + count]
-                if on_vector:
-                    nc.vector.tensor_copy(out=dst, in_=src)
-                else:
-                    nc.scalar.copy(out=dst, in_=src)
-            wc = codes.tile([P, N], U32, name="wc", align_bytes=64)
-            ws = codes.tile([P, N], U8, name="ws", align_bytes=64)
-            nc.vector.quantize_mx(out=wc[:].bitcast(FP8X4), scales=ws[:], in_=wb[:])
-            return wc, ws
-
-        def load_x(a):
-            nc.sync.dma_start(out=xw[a][:], in_=x_words[a].rearrange("p t r -> p (t r)").bitcast(I32))
-
-        for a in range(PASSES):
-            load_x(a)
-        for q in range(4):
-            nc.sync.dma_start(
-                out=xs[32 * q : 32 * q + 4 * PASSES, :],
-                in_=x_scales[:, 4 * q : 4 * q + 4, :].bitcast(I32),
-            )
         half_slots = E * C // 2
-        loaded = {}
-        for e in range(E):
-            for a in range(PASSES):
-                loaded[e, a] = load_w(e, a)
-                if (e, a) == (1, 0):
-                    nc.sync.dma_start(out=gates[:, :half_slots], in_=gate[:P, :half_slots])
-                    wp_rows = wp.rearrange("(u j i) f -> i u j f", j=PACK, i=PAIR)
-                    for i in range(PAIR):
-                        nc.sync.dma_start(out=wp_raw[i:P:PAIR, :, :], in_=wp_rows[i])
-                if (e, a) == (E // 2, 0):
-                    nc.sync.dma_start(out=gates[:, half_slots:], in_=gate[:P, half_slots:])
+
+        raw = {}
+        for item in LOADS:
+            if item[0] == "x":
+                a = int(item[1])
+                nc.sync.dma_start(out=xw[a][:], in_=x_words[a].rearrange("p t r -> p (t r)").bitcast(I32))
+            elif item == "s":
+                for q in range(4):
+                    nc.sync.dma_start(
+                        out=xs[32 * q : 32 * q + 4 * PASSES, :],
+                        in_=x_scales[:, 4 * q : 4 * q + 4, :].bitcast(I32),
+                    )
+            elif item[0] == "g":
+                cols = slice(int(item[1]) * half_slots, (int(item[1]) + 1) * half_slots)
+                nc.sync.dma_start(out=gates[:, cols], in_=gate[:P, cols])
+            elif item == "p":
+                wp_rows = wp.rearrange("(u j i) f -> i u j f", j=PACK, i=PAIR)
+                for i in range(PAIR):
+                    nc.sync.dma_start(out=wp_raw[i:P:PAIR, :, :], in_=wp_rows[i])
+            else:
+                e, a = int(item[1]), int(item[2])
+                rows = w[e, a * KP : (a + 1) * KP, :].rearrange("(p r) n -> p r n", r=PACK)
+                tile = raws.tile([P, PACK, N], F32, name="raw")
+                raw[e, a] = tile
+                parts = 2 if (e, a) in SPLIT else 1
+                for h in range(parts):
+                    cols = slice(h * N // parts, (h + 1) * N // parts)
+                    nc.sync.dma_start(out=tile[:, :, cols], in_=rows[:, :, cols])
 
         wp_codes = keep.tile([P, M], U32, name="wp_codes", align_bytes=64)
         wp_scales = keep.tile([P, M], U8, name="wp_scales", align_bytes=64)
+        words, planes, banks, projected = {}, {}, {}, {}
 
-        for e in range(E):
-            slots = slice(e * C, (e + 1) * C)
-            picks = offsets[:, e * LIST_COLS : (e + 1) * LIST_COLS]
+        def picks(e, count=1):
+            return offsets[:, e * LIST_COLS : (e + count) * LIST_COLS]
 
-            gs = picked.tile([P, C], U8, name="gs", align_bytes=64)
-            nc.vector.tensor_copy(gs[:], xs[:].bitcast(U8).indirect(picks))
-            banks = [ybanks.tile([P, C], F32, name="ybank") for j in range(PACK)]
-            for a in range(PASSES):
-                gw = picked.tile([P, C], U32, name="gw%d" % a, align_bytes=64)
-                nc.vector.tensor_copy(gw[:], xw[a][:].bitcast(U32).indirect(picks))
-                wc, ws = quantise_w(loaded[e, a])
-                for j in range(PACK):
-                    cols = slice(j * P, (j + 1) * P)
-                    nc.tensor.matmul_mx(
-                        out=banks[j][:],
-                        lhsT=wc[:, cols].bitcast(FP8X4),
-                        lhsT_scale=ws[:, cols],
-                        rhs=gw[:].bitcast(FP8X4),
-                        rhs_scale=gs[4 * a : P, :],
-                        start=(a == 0),
-                        stop=(a == PASSES - 1),
-                    )
+        def gather(e0):
+            gw = [picked.tile([P, GW * C], U32, name="gw%d" % a, align_bytes=64) for a in range(PASSES)]
+            gs = picked.tile([P, GW * C], U8, name="gs", align_bytes=64)
+            nc.vector.tensor_copy(gw[0][:], xw[0][:].bitcast(U32).indirect(picks(e0, GW)))
+            nc.vector.tensor_copy(gs[:], xs[:].bitcast(U8).indirect(picks(e0, GW)))
+            for a in range(1, PASSES):
+                nc.vector.tensor_copy(gw[a][:], xw[a][:].bitcast(U32).indirect(picks(e0, GW)))
+            for k in range(GW):
+                cols = slice(k * C, (k + 1) * C)
+                for a in range(PASSES):
+                    words[e0 + k, a] = gw[a][:, cols]
+                    planes[e0 + k, a] = gs[4 * a : P, cols]
 
-            if e == 0:
-                wpb = keep.tile([P, M * PACK], BF16, name="wpb", align_bytes=64)
-                nc.vector.tensor_copy(
-                    out=wpb[:].rearrange("p (f i j) -> p f j i", i=PAIR, j=PACK),
-                    in_=wp_raw[:].rearrange("p j (f i) -> p f j i", i=PAIR),
-                )
-                nc.vector.quantize_mx(out=wp_codes[:].bitcast(FP8X4), scales=wp_scales[:], in_=wpb[:])
-
-            y = work.tile([P, PACK, C], F32, name="y")
+        def expert_pass(e, a):
+            parts = 2 if (e, a) in SPLIT else 1
+            who = CAST.get((e, a), "S" * parts)
+            wb = rounded.tile([P, N * PACK], BF16, name="wb", align_bytes=64)
+            dst = wb[:].rearrange("p (j u i r) -> p u j r i", j=PACK, i=PAIR, r=PACK)
+            src = raw[e, a][:].rearrange("p r (u j i) -> p u j r i", j=PACK, i=PAIR)
+            for h in range(parts):
+                us = slice(h * GROUPS // parts, (h + 1) * GROUPS // parts)
+                if who[h] == "V":
+                    nc.vector.tensor_copy(out=dst[:, us], in_=src[:, us])
+                else:
+                    nc.scalar.copy(out=dst[:, us], in_=src[:, us])
+            wc = codes.tile([P, N], U32, name="wc", align_bytes=64)
+            ws = codes.tile([P, N], U8, name="ws", align_bytes=64)
+            nc.vector.quantize_mx(out=wc[:].bitcast(FP8X4), scales=ws[:], in_=wb[:])
+            if a == 0:
+                banks[e] = [ybanks.tile([P, C], F32, name="ybank") for j in range(PACK)]
             for j in range(PACK):
-                nc.scalar.activation(y[:, j, :], banks[j][:], IDENTITY, bias=bias[:, j, e : e + 1])
+                cols = slice(j * P, (j + 1) * P)
+                nc.tensor.matmul_mx(
+                    out=banks[e][j][:],
+                    lhsT=wc[:, cols].bitcast(FP8X4),
+                    lhsT_scale=ws[:, cols],
+                    rhs=words[e, a].bitcast(FP8X4),
+                    rhs_scale=planes[e, a],
+                    start=(a == 0),
+                    stop=(a == PASSES - 1),
+                )
+
+        def quantise_wp():
+            wpb = keep.tile([P, M * PACK], BF16, name="wpb", align_bytes=64)
+            nc.vector.tensor_copy(
+                out=wpb[:].rearrange("p (f i j) -> p f j i", i=2, j=PACK),
+                in_=wp_raw[:].rearrange("p j (f i) -> p f j i", i=2),
+            )
+            nc.vector.quantize_mx(out=wp_codes[:].bitcast(FP8X4), scales=wp_scales[:], in_=wpb[:])
+
+        def spent(step, name):
+            if step < STEPS:
+                return raw[divmod(step, PASSES)]
+            return work.tile([P, PACK, N], F32, name=name)
+
+        def project(e, step):
+            y = spent(step, "late")[:, :, :C]
+            for j in range(PACK):
+                nc.scalar.activation(y[:, j, :], banks[e][j][:], IDENTITY, bias=bias[:, j, e : e + 1])
             cb = work.tile([P, C * PACK], BF16, name="cb", align_bytes=64)
-            nc.vector.tensor_tensor(
-                cb[:].rearrange("p (s i j) -> p s j i", i=PAIR, j=PACK),
-                y[:].rearrange("p j (s i) -> p s j i", i=PAIR),
-                gates[:, slots].rearrange("p (s i) -> p s i", i=PAIR).unsqueeze(2).to_broadcast([P, C // PAIR, PACK, PAIR]),
+            engine = nc.gpsimd if e in GATE_ON_POOL else nc.vector
+            engine.tensor_tensor(
+                cb[:].rearrange("p (s i j) -> p s j i", i=2, j=PACK),
+                y.rearrange("p j (s i) -> p s j i", i=2),
+                gates[:, e * C : (e + 1) * C].rearrange("p (s i) -> p s i", i=2).unsqueeze(2).to_broadcast([P, C // 2, PACK, 2]),
                 MULT,
             )
             cc = work.tile([P, C], U32, name="cc", align_bytes=64)
             cs = work.tile([P, C], U8, name="cs", align_bytes=64)
             nc.vector.quantize_mx(out=cc[:].bitcast(FP8X4), scales=cs[:], in_=cb[:])
             obank = obanks.tile([P, M // P, C], F32, name="obank")
+            projected[e] = obank
             for m in range(M // P):
                 cols = slice(m * P, (m + 1) * P)
                 nc.tensor.matmul_mx(
@@ -168,10 +182,27 @@ def tile_moe_nxt_lin_bias_kernel(tc, x_words, x_scales, w, b, wp, gate, offs, ou
                     start=True,
                     stop=True,
                 )
-            o = work.tile([P, M // P, C], F32, name="o")
-            nc.scalar.copy(out=o[:], in_=obank[:])
+
+        def scatter(e, step):
+            o = spent(step, "late")[:, : M // P, C:]
+            nc.scalar.copy(out=o, in_=projected[e][:])
             for m in range(M // P):
-                nc.vector.tensor_copy(result[m][:].indirect(picks), o[:, m, :])
+                nc.vector.tensor_copy(result[m][:].indirect(picks(e)), o[:, m, :])
+
+        for step in range(STEPS + max(OUT_LAG)):
+            if step < STEPS:
+                e, a = divmod(step, PASSES)
+                if a == 0 and e % GW == 0:
+                    gather(e)
+                expert_pass(e, a)
+                if step == PASSES - 1:
+                    quantise_wp()
+            for e in range(E):
+                if step == PASSES * e + PASSES - 1 + OUT_LAG[e]:
+                    scatter(e, step)
+            for e in range(E):
+                if step == PASSES * e + PASSES - 1 + BIAS_LAG[e]:
+                    project(e, step)
 
         for m in range(M // P):
             nc.sync.dma_start(out=out[m * P : (m + 1) * P, :], in_=result[m][:])

@@ -15,6 +15,7 @@ U8 = mybir.dt.uint8
 FP8X4 = mybir.dt.float8_e4m3fn_x4
 IDENTITY = mybir.ActivationFunctionType.Identity
 MULT = mybir.AluOpType.mult
+ADD = mybir.AluOpType.add
 
 P = 128
 PACK = 4
@@ -25,11 +26,15 @@ PAIR = 2
 LIST_COLS = C // 16
 GROUPS = N // (PACK * PAIR)
 
-LOADS = "w00 x0 s w01 w02 x1 w10 x2 w11 w12 g0 p w20 w21 w22 w30 g1 w31 w32 w40 w41 w42 w50 w51 w52".split()
-SPLIT = {(0, 0), (5, 2)}
-CAST = {(5, 2): "SV"}
-BIAS_LAG = [2,2,2,2,2,2]
-OUT_LAG = [6,6,6,6,6,6]
+LOADS = "x1 x0 s w00 w01 w02 w10 w11 w12 x2 g01 w20 p w21 w22 w30 g5 w31 w32 g23 w40 w41 w42 w50 w51 w52 g4".split()
+SPLIT = {(5, 0), (0, 2), (2, 2), (4, 1), (1, 1), (2, 0)}
+CAST = {(1, 1): "SS", (2, 0): "VS", (2, 2): "VS", (4, 1): "SV", (5, 0): "SV", (0, 2): "SS", (0, 0): "V"}
+BIAS_LAG = [3,2,1,3,4,6]
+OUT_LAG = [6,5,6,8,15,23]
+OUT_SPLIT = [5,3]
+QPAIR = []
+TEAMS = [[0],[1],[2],[3],[4],[5]]
+GATE_LAG = [3,2,1,3,4,6]
 GW = 2
 GATE_ON_POOL = []
 
@@ -41,8 +46,10 @@ def tile_moe_nxt_lin_bias_kernel(tc, x_words, x_scales, w, b, wp, gate, offs, ou
         raws = ctx.enter_context(tc.tile_pool(name="raws", bufs=11))
         rounded = ctx.enter_context(tc.tile_pool(name="rounded", bufs=6))
         codes = ctx.enter_context(tc.tile_pool(name="codes", bufs=9))
+        rounded2 = ctx.enter_context(tc.tile_pool(name="rounded2", bufs=1))
+        codes2 = ctx.enter_context(tc.tile_pool(name="codes2", bufs=1))
         work = ctx.enter_context(tc.tile_pool(name="work", bufs=3))
-        picked = ctx.enter_context(tc.tile_pool(name="picked", bufs=2))
+        picked = ctx.enter_context(tc.tile_pool(name="picked", bufs=3))
         ybanks = ctx.enter_context(tc.psum_pool(name="ybanks", bufs=6))
         obanks = ctx.enter_context(tc.psum_pool(name="obanks", bufs=2))
 
@@ -62,7 +69,6 @@ def tile_moe_nxt_lin_bias_kernel(tc, x_words, x_scales, w, b, wp, gate, offs, ou
         gates = keep.tile([P, E * C], F32, name="gates")
         wp_raw = keep.tile([P, PACK, M], F32, name="wp_raw")
         result = [keep.tile([P, T], F32, name="result%d" % m) for m in range(M // P)]
-        half_slots = E * C // 2
 
         raw = {}
         for item in LOADS:
@@ -76,7 +82,7 @@ def tile_moe_nxt_lin_bias_kernel(tc, x_words, x_scales, w, b, wp, gate, offs, ou
                         in_=x_scales[:, 4 * q : 4 * q + 4, :].bitcast(I32),
                     )
             elif item[0] == "g":
-                cols = slice(int(item[1]) * half_slots, (int(item[1]) + 1) * half_slots)
+                cols = slice(int(item[1]) * C, (int(item[-1]) + 1) * C)
                 nc.sync.dma_start(out=gates[:, cols], in_=gate[:P, cols])
             elif item == "p":
                 wp_rows = wp.rearrange("(u j i) f -> i u j f", j=PACK, i=PAIR)
@@ -87,7 +93,7 @@ def tile_moe_nxt_lin_bias_kernel(tc, x_words, x_scales, w, b, wp, gate, offs, ou
                 rows = w[e, a * KP : (a + 1) * KP, :].rearrange("(p r) n -> p r n", r=PACK)
                 tile = raws.tile([P, PACK, N], F32, name="raw")
                 raw[e, a] = tile
-                parts = 2 if (e, a) in SPLIT else 1
+                parts = 2 if (e, a) in SPLIT and (e, a) in ((0, 0), (E - 1, PASSES - 1)) else 1
                 for h in range(parts):
                     cols = slice(h * N // parts, (h + 1) * N // parts)
                     nc.sync.dma_start(out=tile[:, :, cols], in_=rows[:, :, cols])
@@ -112,21 +118,10 @@ def tile_moe_nxt_lin_bias_kernel(tc, x_words, x_scales, w, b, wp, gate, offs, ou
                     words[e0 + k, a] = gw[a][:, cols]
                     planes[e0 + k, a] = gs[4 * a : P, cols]
 
-        def expert_pass(e, a):
-            parts = 2 if (e, a) in SPLIT else 1
-            who = CAST.get((e, a), "S" * parts)
-            wb = rounded.tile([P, N * PACK], BF16, name="wb", align_bytes=64)
-            dst = wb[:].rearrange("p (j u i r) -> p u j r i", j=PACK, i=PAIR, r=PACK)
-            src = raw[e, a][:].rearrange("p r (u j i) -> p u j r i", j=PACK, i=PAIR)
-            for h in range(parts):
-                us = slice(h * GROUPS // parts, (h + 1) * GROUPS // parts)
-                if who[h] == "V":
-                    nc.vector.tensor_copy(out=dst[:, us], in_=src[:, us])
-                else:
-                    nc.scalar.copy(out=dst[:, us], in_=src[:, us])
-            wc = codes.tile([P, N], U32, name="wc", align_bytes=64)
-            ws = codes.tile([P, N], U8, name="ws", align_bytes=64)
-            nc.vector.quantize_mx(out=wc[:].bitcast(FP8X4), scales=ws[:], in_=wb[:])
+        held, rounded_of = {}, {}
+
+        def multiply(step, wc, ws):
+            e, a = divmod(step, PASSES)
             if a == 0:
                 banks[e] = [ybanks.tile([P, C], F32, name="ybank") for j in range(PACK)]
             for j in range(PACK):
@@ -141,6 +136,42 @@ def tile_moe_nxt_lin_bias_kernel(tc, x_words, x_scales, w, b, wp, gate, offs, ou
                     stop=(a == PASSES - 1),
                 )
 
+        def expert_pass(step):
+            e, a = divmod(step, PASSES)
+            parts = 2 if (e, a) in SPLIT else 1
+            who = CAST.get((e, a), "S" * parts)
+            if step in QPAIR:
+                both = rounded2.tile([P, 2 * N * PACK], BF16, name="wb2", align_bytes=64)
+                held[step + 1] = both
+                wb = both[:, : N * PACK]
+            elif step in held:
+                wb = held[step][:, N * PACK :]
+            else:
+                one = rounded.tile([P, N * PACK], BF16, name="wb", align_bytes=64)
+                wb = one[:]
+            rounded_of[step] = wb
+            dst = wb.rearrange("p (j u i r) -> p u j r i", j=PACK, i=PAIR, r=PACK)
+            src = raw[e, a][:].rearrange("p r (u j i) -> p u j r i", j=PACK, i=PAIR)
+            for h in range(parts):
+                us = slice(h * GROUPS // parts, (h + 1) * GROUPS // parts)
+                if who[h] == "V":
+                    nc.vector.tensor_copy(out=dst[:, us], in_=src[:, us])
+                else:
+                    nc.scalar.copy(out=dst[:, us], in_=src[:, us])
+            if step in QPAIR:
+                return
+            if step in held:
+                wc = codes2.tile([P, 2 * N], U32, name="wc2", align_bytes=64)
+                ws = codes2.tile([P, 2 * N], U8, name="ws2", align_bytes=64)
+                nc.vector.quantize_mx(out=wc[:].bitcast(FP8X4), scales=ws[:], in_=held[step][:])
+                multiply(step - 1, wc[:, :N], ws[:, :N])
+                multiply(step, wc[:, N:], ws[:, N:])
+            else:
+                wc = codes.tile([P, N], U32, name="wc", align_bytes=64)
+                ws = codes.tile([P, N], U8, name="ws", align_bytes=64)
+                nc.vector.quantize_mx(out=wc[:].bitcast(FP8X4), scales=ws[:], in_=wb)
+                multiply(step, wc[:], ws[:])
+
         def quantise_wp():
             wpb = keep.tile([P, M * PACK], BF16, name="wpb", align_bytes=64)
             nc.vector.tensor_copy(
@@ -154,27 +185,51 @@ def tile_moe_nxt_lin_bias_kernel(tc, x_words, x_scales, w, b, wp, gate, offs, ou
                 return raw[divmod(step, PASSES)]
             return work.tile([P, PACK, N], F32, name=name)
 
+        team_of = {e: team for team in TEAMS for e in team}
+        sums = {}
+
         def project(e, step):
-            y = spent(step, "late")[:, :, :C]
+            team = team_of[e]
+            width = C * len(team)
+            if e == team[0]:
+                sums[e] = spent(step, "late")[:, :, :width]
+            y = sums[team[0]]
+            c0 = (e - team[0]) * C
             for j in range(PACK):
-                nc.scalar.activation(y[:, j, :], banks[e][j][:], IDENTITY, bias=bias[:, j, e : e + 1])
-            cb = work.tile([P, C * PACK], BF16, name="cb", align_bytes=64)
+                nc.scalar.activation(y[:, j, c0 : c0 + C], banks[e][j][:], IDENTITY, bias=bias[:, j, e : e + 1])
+
+        def gate_and_project(e, step):
+            team = team_of[e]
+            width = C * len(team)
+            if e != team[-1]:
+                return
+            y = sums[team[0]]
+            if e in GATE_ON_POOL and step < STEPS:
+                cb = rounded_of[step][:, : width * PACK]
+            else:
+                own = work.tile([P, width * PACK], BF16, name="cb", align_bytes=64)
+                cb = own[:]
             engine = nc.gpsimd if e in GATE_ON_POOL else nc.vector
+            gated = gates[:, team[0] * C : team[0] * C + width].rearrange("p (s i) -> p s i", i=2)
             engine.tensor_tensor(
-                cb[:].rearrange("p (s i j) -> p s j i", i=2, j=PACK),
+                cb.rearrange("p (s i j) -> p s j i", i=2, j=PACK),
                 y.rearrange("p j (s i) -> p s j i", i=2),
-                gates[:, e * C : (e + 1) * C].rearrange("p (s i) -> p s i", i=2).unsqueeze(2).to_broadcast([P, C // 2, PACK, 2]),
+                gated.unsqueeze(2).to_broadcast([P, width // 2, PACK, 2]),
                 MULT,
             )
-            cc = work.tile([P, C], U32, name="cc", align_bytes=64)
-            cs = work.tile([P, C], U8, name="cs", align_bytes=64)
-            nc.vector.quantize_mx(out=cc[:].bitcast(FP8X4), scales=cs[:], in_=cb[:])
-            obank = obanks.tile([P, M // P, C], F32, name="obank")
-            projected[e] = obank
+            cc = work.tile([P, width], U32, name="cc", align_bytes=64)
+            cs = work.tile([P, width], U8, name="cs", align_bytes=64)
+            nc.vector.quantize_mx(out=cc[:].bitcast(FP8X4), scales=cs[:], in_=cb)
+            if len(team) == 1:
+                obank = obanks.tile([P, M // P, C], F32, name="obank")
+                projected[e] = [obank[:, m, :] for m in range(M // P)] + [obank[:]]
+            else:
+                pair = [obanks.tile([P, width], F32, name="obank") for m in range(M // P)]
+                projected[e] = [bank[:] for bank in pair]
             for m in range(M // P):
                 cols = slice(m * P, (m + 1) * P)
                 nc.tensor.matmul_mx(
-                    out=obank[:, m, :],
+                    out=projected[e][m],
                     lhsT=wp_codes[:, cols].bitcast(FP8X4),
                     lhsT_scale=wp_scales[:, cols],
                     rhs=cc[:].bitcast(FP8X4),
@@ -184,17 +239,25 @@ def tile_moe_nxt_lin_bias_kernel(tc, x_words, x_scales, w, b, wp, gate, offs, ou
                 )
 
         def scatter(e, step):
-            o = spent(step, "late")[:, : M // P, C:]
-            nc.scalar.copy(out=o, in_=projected[e][:])
+            team = team_of[e]
+            if e != team[-1]:
+                return
+            width = C * len(team)
+            o = spent(step, "late")[:, : M // P, N - width :]
+            whole = len(team) == 1 and e not in OUT_SPLIT
+            if whole:
+                nc.scalar.copy(out=o, in_=projected[e][M // P])
             for m in range(M // P):
-                nc.vector.tensor_copy(result[m][:].indirect(picks(e)), o[:, m, :])
+                if not whole:
+                    nc.scalar.copy(out=o[:, m, :], in_=projected[e][m])
+                nc.vector.tensor_copy(result[m][:].indirect(picks(team[0], len(team))), o[:, m, :])
 
         for step in range(STEPS + max(OUT_LAG)):
             if step < STEPS:
                 e, a = divmod(step, PASSES)
                 if a == 0 and e % GW == 0:
                     gather(e)
-                expert_pass(e, a)
+                expert_pass(step)
                 if step == PASSES - 1:
                     quantise_wp()
             for e in range(E):
@@ -203,6 +266,8 @@ def tile_moe_nxt_lin_bias_kernel(tc, x_words, x_scales, w, b, wp, gate, offs, ou
             for e in range(E):
                 if step == PASSES * e + PASSES - 1 + BIAS_LAG[e]:
                     project(e, step)
+                if step == PASSES * e + PASSES - 1 + GATE_LAG[e]:
+                    gate_and_project(e, step)
 
         for m in range(M // P):
             nc.sync.dma_start(out=out[m * P : (m + 1) * P, :], in_=result[m][:])

@@ -22,7 +22,7 @@ PACK = 4
 KP = P * PACK
 PASSES = K // KP
 STEPS = E * PASSES
-PAIR = 2
+PAIR = 4
 LIST_COLS = C // 16
 GROUPS = N // (PACK * PAIR)
 

@@ -3,8 +3,9 @@ from contextlib import ExitStack
 import concourse.mybir as mybir
 
 K, T, E, C, N, M = 1536, 1536, 6, 256, 512, 256
+P = 128
 FLOPS = 2 * K * N * E * C + 2 * N * M * T
-BYTES = K * T + K * T // 32 + 4 * (E * K * N + N * E + N * M + 128 * E * C + M * T) + 2 * 128 * (T // 16)
+BYTES = K * T + K * T // 32 + 4 * (E * K * N + N * E + N * M + P * E * C + M * T) + 2 * P * (T // 16)
 
 F32 = mybir.dt.float32
 BF16 = mybir.dt.bfloat16
@@ -13,261 +14,218 @@ U32 = mybir.dt.uint32
 U16 = mybir.dt.uint16
 U8 = mybir.dt.uint8
 FP8X4 = mybir.dt.float8_e4m3fn_x4
+COPY = mybir.ActivationFunctionType.Copy
 IDENTITY = mybir.ActivationFunctionType.Identity
 MULT = mybir.AluOpType.mult
-ADD = mybir.AluOpType.add
 
-P = 128
 PACK = 4
+RUN = 4
+PAIR = 2
 KP = P * PACK
 PASSES = K // KP
 STEPS = E * PASSES
-PAIR = 4
+LAST = STEPS - 1
+GROUPS = N // (PACK * RUN)
+QUADRANTS = P // 32
+OUT_TILES = M // P
 LIST_COLS = C // 16
-GROUPS = N // (PACK * PAIR)
+HALF = E // 2
 
-LOADS = "x1 x0 s w00 w01 w02 w10 w11 w12 x2 g01 w20 p w21 w22 w30 g5 w31 w32 g23 w40 w41 w42 w50 w51 w52 g4".split()
-SPLIT = {(5, 0), (0, 2), (2, 2), (4, 1), (1, 1), (2, 0)}
-CAST = {(1, 1): "SS", (2, 0): "VS", (2, 2): "VS", (4, 1): "SV", (5, 0): "SV", (0, 2): "SS", (0, 0): "V"}
-BIAS_LAG = [3,2,1,3,4,6]
-OUT_LAG = [6,5,6,8,15,23]
-OUT_SPLIT = [5,3]
-QPAIR = []
-TEAMS = [[0],[1],[2],[3],[4],[5]]
-GATE_LAG = [3,2,1,3,4,6]
-GW = 2
-GATE_ON_POOL = []
+LOADS_BEHIND = {-1: ["x2"], 0: ["scales", "x0"], 3: ["x1"], 4: ["wp", "gate0"], 8: ["gate1"]}
+ROUNDED_BY = {5: "V", 8: "SV", 10: "SV", 11: "VV", 14: "SV", 16: "VS", 17: "SS"}
+PROJECT_STEP = [4, 6, 10, 13, 14, 18]
+SCATTER_STEP = [6, 9, 14, 17, 19, 25]
+COPIED_BY_TILE = (3, 4)
+
+RAW_BUFS = 11
+ROUNDED_BUFS = 6
+CODE_BUFS = 9
+C_BUFS = 3
+SUM_BANKS = 6
 
 
 def tile_moe_nxt_lin_bias_kernel(tc, x_words, x_scales, w, b, wp, gate, offs, out):
     nc = tc.nc
     with ExitStack() as ctx:
         keep = ctx.enter_context(tc.tile_pool(name="keep", bufs=1))
-        raws = ctx.enter_context(tc.tile_pool(name="raws", bufs=11))
-        rounded = ctx.enter_context(tc.tile_pool(name="rounded", bufs=6))
-        codes = ctx.enter_context(tc.tile_pool(name="codes", bufs=9))
-        rounded2 = ctx.enter_context(tc.tile_pool(name="rounded2", bufs=1))
-        codes2 = ctx.enter_context(tc.tile_pool(name="codes2", bufs=1))
-        work = ctx.enter_context(tc.tile_pool(name="work", bufs=3))
-        picked = ctx.enter_context(tc.tile_pool(name="picked", bufs=3))
-        ybanks = ctx.enter_context(tc.psum_pool(name="ybanks", bufs=6))
-        obanks = ctx.enter_context(tc.psum_pool(name="obanks", bufs=2))
+        raws = ctx.enter_context(tc.tile_pool(name="raws", bufs=RAW_BUFS))
+        rounded = ctx.enter_context(tc.tile_pool(name="rounded", bufs=ROUNDED_BUFS))
+        codes = ctx.enter_context(tc.tile_pool(name="codes", bufs=CODE_BUFS))
+        cwork = ctx.enter_context(tc.tile_pool(name="cwork", bufs=C_BUFS))
+        sum_banks = ctx.enter_context(tc.psum_pool(name="sum_banks", bufs=SUM_BANKS))
+        out_banks = ctx.enter_context(tc.psum_pool(name="out_banks", bufs=8 - SUM_BANKS))
 
         offsets = keep.tile([P, T // 16], U16, name="offsets")
         nc.sync.dma_start(offsets[:], offs)
 
-        xs = keep.tile([P, T // 4], I32, name="xs", align_bytes=64)
-        nc.gpsimd.memset(xs[:], 0)
-        b_raw = keep.tile([P, PACK, E], F32, name="b_raw")
-        b_rows = b.rearrange("(u j i) e -> i u j e", j=PACK, i=PAIR)
-        for i in range(PAIR):
-            nc.scalar.dma_start(out=b_raw[i:P:PAIR, :, :], in_=b_rows[i])
+        token_scales = keep.tile([P, T // 4], I32, name="token_scales", align_bytes=64)
+        nc.gpsimd.memset(token_scales[:], 0)
         bias = keep.tile([P, PACK, E], F32, name="bias")
-        nc.scalar.activation(bias[:], b_raw[:], IDENTITY)
+        b_rows = b.rearrange("(u j i) e -> i u j e", j=PACK, i=RUN)
+        for i in range(RUN):
+            nc.scalar.dma_start(out=bias[i:P:RUN, :, :], in_=b_rows[i])
 
-        xw = [keep.tile([P, T], I32, name="xw%d" % a, align_bytes=64) for a in range(PASSES)]
+        token_words = [keep.tile([P, T], I32, name="token_words%d" % a, align_bytes=64) for a in range(PASSES)]
         gates = keep.tile([P, E * C], F32, name="gates")
         wp_raw = keep.tile([P, PACK, M], F32, name="wp_raw")
-        result = [keep.tile([P, T], F32, name="result%d" % m) for m in range(M // P)]
+        result = [keep.tile([P, T], F32, name="result%d" % m) for m in range(OUT_TILES)]
 
-        raw = {}
-        for item in LOADS:
-            if item[0] == "x":
-                a = int(item[1])
-                nc.sync.dma_start(out=xw[a][:], in_=x_words[a].rearrange("p t r -> p (t r)").bitcast(I32))
-            elif item == "s":
-                for q in range(4):
+        def load_other(item):
+            if item == "scales":
+                for q in range(QUADRANTS):
                     nc.sync.dma_start(
-                        out=xs[32 * q : 32 * q + 4 * PASSES, :],
+                        out=token_scales[32 * q : 32 * q + 4 * PASSES, :],
                         in_=x_scales[:, 4 * q : 4 * q + 4, :].bitcast(I32),
                     )
-            elif item[0] == "g":
-                cols = slice(int(item[1]) * C, (int(item[-1]) + 1) * C)
+            elif item == "wp":
+                wp_rows = wp.rearrange("(u j i) f -> i u j f", j=PACK, i=RUN)
+                for i in range(RUN):
+                    nc.sync.dma_start(out=wp_raw[i:P:RUN, :, :], in_=wp_rows[i])
+            elif item.startswith("gate"):
+                cols = slice(int(item[-1]) * HALF * C, (int(item[-1]) + 1) * HALF * C)
                 nc.sync.dma_start(out=gates[:, cols], in_=gate[:P, cols])
-            elif item == "p":
-                wp_rows = wp.rearrange("(u j i) f -> i u j f", j=PACK, i=PAIR)
-                for i in range(PAIR):
-                    nc.sync.dma_start(out=wp_raw[i:P:PAIR, :, :], in_=wp_rows[i])
             else:
-                e, a = int(item[1]), int(item[2])
-                rows = w[e, a * KP : (a + 1) * KP, :].rearrange("(p r) n -> p r n", r=PACK)
-                tile = raws.tile([P, PACK, N], F32, name="raw")
-                raw[e, a] = tile
-                parts = 2 if (e, a) in SPLIT and (e, a) in ((0, 0), (E - 1, PASSES - 1)) else 1
-                for h in range(parts):
-                    cols = slice(h * N // parts, (h + 1) * N // parts)
-                    nc.sync.dma_start(out=tile[:, :, cols], in_=rows[:, :, cols])
+                a = int(item[-1])
+                nc.sync.dma_start(out=token_words[a][:], in_=x_words[a].rearrange("p t r -> p (t r)").bitcast(I32))
+
+        def load_weights(step):
+            e, a = divmod(step, PASSES)
+            rows = w[e, a * KP : (a + 1) * KP, :].rearrange("(p r) n -> p r n", r=PACK)
+            tile = raws.tile([P, PACK, N], F32, name="raw")
+            parts = 2 if step == LAST else 1
+            for h in range(parts):
+                cols = slice(h * N // parts, (h + 1) * N // parts)
+                nc.sync.dma_start(out=tile[:, :, cols], in_=rows[:, :, cols])
+            return tile
+
+        raw = []
+        for step in range(-1, STEPS):
+            if step >= 0:
+                raw.append(load_weights(step))
+            for item in LOADS_BEHIND.get(step, []):
+                load_other(item)
 
         wp_codes = keep.tile([P, M], U32, name="wp_codes", align_bytes=64)
         wp_scales = keep.tile([P, M], U8, name="wp_scales", align_bytes=64)
-        words, planes, banks, projected = {}, {}, {}, {}
+        slot_words, slot_scales, sums, biased, projected = {}, {}, {}, {}, {}
 
-        def picks(e, count=1):
+        def slots_of(e, count=1):
             return offsets[:, e * LIST_COLS : (e + count) * LIST_COLS]
 
-        def gather(e0):
-            gw = [picked.tile([P, GW * C], U32, name="gw%d" % a, align_bytes=64) for a in range(PASSES)]
-            gs = picked.tile([P, GW * C], U8, name="gs", align_bytes=64)
-            nc.vector.tensor_copy(gw[0][:], xw[0][:].bitcast(U32).indirect(picks(e0, GW)))
-            nc.vector.tensor_copy(gs[:], xs[:].bitcast(U8).indirect(picks(e0, GW)))
+        def gather_tokens(e0):
+            words = [
+                keep.tile([P, HALF * C], U32, name="slot_words%d_%d" % (e0, a), align_bytes=64) for a in range(PASSES)
+            ]
+            scales = keep.tile([P, HALF * C], U8, name="slot_scales%d" % e0, align_bytes=64)
+            picks = slots_of(e0, HALF)
+            nc.vector.tensor_copy(words[0][:], token_words[0][:].bitcast(U32).indirect(picks))
+            nc.vector.tensor_copy(scales[:], token_scales[:].bitcast(U8).indirect(picks))
             for a in range(1, PASSES):
-                nc.vector.tensor_copy(gw[a][:], xw[a][:].bitcast(U32).indirect(picks(e0, GW)))
-            for k in range(GW):
-                cols = slice(k * C, (k + 1) * C)
+                nc.vector.tensor_copy(words[a][:], token_words[a][:].bitcast(U32).indirect(picks))
+            for e in range(e0, e0 + HALF):
+                cols = slice((e - e0) * C, (e - e0 + 1) * C)
                 for a in range(PASSES):
-                    words[e0 + k, a] = gw[a][:, cols]
-                    planes[e0 + k, a] = gs[4 * a : P, cols]
+                    slot_words[e, a] = words[a][:, cols]
+                    slot_scales[e, a] = scales[4 * a : P, cols]
 
-        held, rounded_of = {}, {}
-
-        def multiply(step, wc, ws):
+        def expert_pass(step):
             e, a = divmod(step, PASSES)
+            w_bf = rounded.tile([P, N * PACK], BF16, name="w_bf", align_bytes=64)
+            dst = w_bf[:].rearrange("p (j u i r) -> p u j r i", j=PACK, i=RUN, r=PACK)
+            src = raw[step][:].rearrange("p r (u j i) -> p u j r i", j=PACK, i=RUN)
+            if step == 0:
+                for j in range(PACK):
+                    nc.scalar.activation(dst[:, :, j], src[:, :, j], COPY)
+            else:
+                engines = ROUNDED_BY.get(step, "S")
+                for h, engine in enumerate(engines):
+                    us = slice(h * GROUPS // len(engines), (h + 1) * GROUPS // len(engines))
+                    if engine == "V":
+                        nc.vector.tensor_copy(out=dst[:, us], in_=src[:, us])
+                    else:
+                        nc.scalar.copy(out=dst[:, us], in_=src[:, us])
+            w_codes = codes.tile([P, N], U32, name="w_codes", align_bytes=64)
+            w_scales = codes.tile([P, N], U8, name="w_scales", align_bytes=64)
+            nc.vector.quantize_mx(out=w_codes[:].bitcast(FP8X4), scales=w_scales[:], in_=w_bf[:])
             if a == 0:
-                banks[e] = [ybanks.tile([P, C], F32, name="ybank") for j in range(PACK)]
+                sums[e] = [sum_banks.tile([P, C], F32, name="sum_bank") for j in range(PACK)]
             for j in range(PACK):
                 cols = slice(j * P, (j + 1) * P)
                 nc.tensor.matmul_mx(
-                    out=banks[e][j][:],
-                    lhsT=wc[:, cols].bitcast(FP8X4),
-                    lhsT_scale=ws[:, cols],
-                    rhs=words[e, a].bitcast(FP8X4),
-                    rhs_scale=planes[e, a],
+                    out=sums[e][j][:],
+                    lhsT=w_codes[:, cols].bitcast(FP8X4),
+                    lhsT_scale=w_scales[:, cols],
+                    rhs=slot_words[e, a].bitcast(FP8X4),
+                    rhs_scale=slot_scales[e, a],
                     start=(a == 0),
                     stop=(a == PASSES - 1),
                 )
 
-        def expert_pass(step):
-            e, a = divmod(step, PASSES)
-            parts = 2 if (e, a) in SPLIT else 1
-            who = CAST.get((e, a), "S" * parts)
-            if step in QPAIR:
-                both = rounded2.tile([P, 2 * N * PACK], BF16, name="wb2", align_bytes=64)
-                held[step + 1] = both
-                wb = both[:, : N * PACK]
-            elif step in held:
-                wb = held[step][:, N * PACK :]
-            else:
-                one = rounded.tile([P, N * PACK], BF16, name="wb", align_bytes=64)
-                wb = one[:]
-            rounded_of[step] = wb
-            dst = wb.rearrange("p (j u i r) -> p u j r i", j=PACK, i=PAIR, r=PACK)
-            src = raw[e, a][:].rearrange("p r (u j i) -> p u j r i", j=PACK, i=PAIR)
-            for h in range(parts):
-                us = slice(h * GROUPS // parts, (h + 1) * GROUPS // parts)
-                if who[h] == "V":
-                    nc.vector.tensor_copy(out=dst[:, us], in_=src[:, us])
-                else:
-                    nc.scalar.copy(out=dst[:, us], in_=src[:, us])
-            if step in QPAIR:
-                return
-            if step in held:
-                wc = codes2.tile([P, 2 * N], U32, name="wc2", align_bytes=64)
-                ws = codes2.tile([P, 2 * N], U8, name="ws2", align_bytes=64)
-                nc.vector.quantize_mx(out=wc[:].bitcast(FP8X4), scales=ws[:], in_=held[step][:])
-                multiply(step - 1, wc[:, :N], ws[:, :N])
-                multiply(step, wc[:, N:], ws[:, N:])
-            else:
-                wc = codes.tile([P, N], U32, name="wc", align_bytes=64)
-                ws = codes.tile([P, N], U8, name="ws", align_bytes=64)
-                nc.vector.quantize_mx(out=wc[:].bitcast(FP8X4), scales=ws[:], in_=wb)
-                multiply(step, wc[:], ws[:])
-
         def quantise_wp():
-            wpb = keep.tile([P, M * PACK], BF16, name="wpb", align_bytes=64)
+            wp_bf = keep.tile([P, M * PACK], BF16, name="wp_bf", align_bytes=64)
             nc.vector.tensor_copy(
-                out=wpb[:].rearrange("p (f i j) -> p f j i", i=2, j=PACK),
-                in_=wp_raw[:].rearrange("p j (f i) -> p f j i", i=2),
+                out=wp_bf[:].rearrange("p (f i j) -> p f j i", i=PAIR, j=PACK),
+                in_=wp_raw[:].rearrange("p j (f i) -> p f j i", i=PAIR),
             )
-            nc.vector.quantize_mx(out=wp_codes[:].bitcast(FP8X4), scales=wp_scales[:], in_=wpb[:])
+            nc.vector.quantize_mx(out=wp_codes[:].bitcast(FP8X4), scales=wp_scales[:], in_=wp_bf[:])
 
-        def spent(step, name):
-            if step < STEPS:
-                return raw[divmod(step, PASSES)]
-            return work.tile([P, PACK, N], F32, name=name)
-
-        team_of = {e: team for team in TEAMS for e in team}
-        sums = {}
-
-        def project(e, step):
-            team = team_of[e]
-            width = C * len(team)
-            if e == team[0]:
-                sums[e] = spent(step, "late")[:, :, :width]
-            y = sums[team[0]]
-            c0 = (e - team[0]) * C
-            for j in range(PACK):
-                nc.scalar.activation(y[:, j, c0 : c0 + C], banks[e][j][:], IDENTITY, bias=bias[:, j, e : e + 1])
-
-        def gate_and_project(e, step):
-            team = team_of[e]
-            width = C * len(team)
-            if e != team[-1]:
-                return
-            y = sums[team[0]]
-            if e in GATE_ON_POOL and step < STEPS:
-                cb = rounded_of[step][:, : width * PACK]
+        def project(e):
+            if PROJECT_STEP[e] <= LAST:
+                y = raw[PROJECT_STEP[e]][:, :, :C]
             else:
-                own = work.tile([P, width * PACK], BF16, name="cb", align_bytes=64)
-                cb = own[:]
-            engine = nc.gpsimd if e in GATE_ON_POOL else nc.vector
-            gated = gates[:, team[0] * C : team[0] * C + width].rearrange("p (s i) -> p s i", i=2)
-            engine.tensor_tensor(
-                cb.rearrange("p (s i j) -> p s j i", i=2, j=PACK),
-                y.rearrange("p j (s i) -> p s j i", i=2),
-                gated.unsqueeze(2).to_broadcast([P, width // 2, PACK, 2]),
+                y = keep.tile([P, PACK, C], F32, name="y_last")
+            biased[e] = y
+            for j in range(PACK):
+                nc.scalar.activation(y[:, j, :], sums[e][j][:], IDENTITY, bias=bias[:, j, e : e + 1])
+            c_bf = cwork.tile([P, C * PACK], BF16, name="c_bf", align_bytes=64)
+            slot_gates = gates[:, e * C : (e + 1) * C].rearrange("p (s i) -> p s i", i=PAIR)
+            nc.vector.tensor_tensor(
+                c_bf[:].rearrange("p (s i j) -> p s j i", i=PAIR, j=PACK),
+                y[:, :, :].rearrange("p j (s i) -> p s j i", i=PAIR),
+                slot_gates.unsqueeze(2).to_broadcast([P, C // PAIR, PACK, PAIR]),
                 MULT,
             )
-            cc = work.tile([P, width], U32, name="cc", align_bytes=64)
-            cs = work.tile([P, width], U8, name="cs", align_bytes=64)
-            nc.vector.quantize_mx(out=cc[:].bitcast(FP8X4), scales=cs[:], in_=cb)
-            if len(team) == 1:
-                obank = obanks.tile([P, M // P, C], F32, name="obank")
-                projected[e] = [obank[:, m, :] for m in range(M // P)] + [obank[:]]
-            else:
-                pair = [obanks.tile([P, width], F32, name="obank") for m in range(M // P)]
-                projected[e] = [bank[:] for bank in pair]
-            for m in range(M // P):
+            c_codes = cwork.tile([P, C], U32, name="c_codes", align_bytes=64)
+            c_scales = cwork.tile([P, C], U8, name="c_scales", align_bytes=64)
+            nc.vector.quantize_mx(out=c_codes[:].bitcast(FP8X4), scales=c_scales[:], in_=c_bf[:])
+            projected[e] = out_banks.tile([P, OUT_TILES, C], F32, name="out_bank")
+            for m in range(OUT_TILES):
                 cols = slice(m * P, (m + 1) * P)
                 nc.tensor.matmul_mx(
-                    out=projected[e][m],
+                    out=projected[e][:, m, :],
                     lhsT=wp_codes[:, cols].bitcast(FP8X4),
                     lhsT_scale=wp_scales[:, cols],
-                    rhs=cc[:].bitcast(FP8X4),
-                    rhs_scale=cs[:],
+                    rhs=c_codes[:].bitcast(FP8X4),
+                    rhs_scale=c_scales[:],
                     start=True,
                     stop=True,
                 )
 
-        def scatter(e, step):
-            team = team_of[e]
-            if e != team[-1]:
-                return
-            width = C * len(team)
-            o = spent(step, "late")[:, : M // P, N - width :]
-            whole = len(team) == 1 and e not in OUT_SPLIT
-            if whole:
-                nc.scalar.copy(out=o, in_=projected[e][M // P])
-            for m in range(M // P):
-                if not whole:
-                    nc.scalar.copy(out=o[:, m, :], in_=projected[e][m])
-                nc.vector.tensor_copy(result[m][:].indirect(picks(team[0], len(team))), o[:, m, :])
+        def scatter(e):
+            if SCATTER_STEP[e] <= LAST:
+                staged = raw[SCATTER_STEP[e]][:, :OUT_TILES, C:]
+            elif e < E - 1:
+                staged = biased[E - 1][:, :OUT_TILES, :]
+            else:
+                staged = keep.tile([P, OUT_TILES, C], F32, name="staged_last")
+            if e not in COPIED_BY_TILE:
+                nc.scalar.copy(out=staged[:, :, :], in_=projected[e][:])
+            for m in range(OUT_TILES):
+                if e in COPIED_BY_TILE:
+                    nc.scalar.copy(out=staged[:, m, :], in_=projected[e][:, m, :])
+                nc.vector.tensor_copy(result[m][:].indirect(slots_of(e)), staged[:, m, :])
 
-        for step in range(STEPS + max(OUT_LAG)):
-            if step < STEPS:
-                e, a = divmod(step, PASSES)
-                if a == 0 and e % GW == 0:
-                    gather(e)
+        for step in range(SCATTER_STEP[-1] + 1):
+            if step <= LAST:
+                if step % (HALF * PASSES) == 0:
+                    gather_tokens(step // PASSES)
                 expert_pass(step)
                 if step == PASSES - 1:
                     quantise_wp()
-            for e in range(E):
-                if step == PASSES * e + PASSES - 1 + OUT_LAG[e]:
-                    scatter(e, step)
-            for e in range(E):
-                if step == PASSES * e + PASSES - 1 + BIAS_LAG[e]:
-                    project(e, step)
-                if step == PASSES * e + PASSES - 1 + GATE_LAG[e]:
-                    gate_and_project(e, step)
+            if step in SCATTER_STEP:
+                scatter(SCATTER_STEP.index(step))
+            if step in PROJECT_STEP:
+                project(PROJECT_STEP.index(step))
 
-        for m in range(M // P):
+        for m in range(OUT_TILES):
             nc.sync.dma_start(out=out[m * P : (m + 1) * P, :], in_=result[m][:])

@@ -17,6 +17,7 @@ FP8X4 = mybir.dt.float8_e4m3fn_x4
 COPY = mybir.ActivationFunctionType.Copy
 IDENTITY = mybir.ActivationFunctionType.Identity
 MULT = mybir.AluOpType.mult
+ADD = mybir.AluOpType.add
 
 PACK = 4
 RUN = 4
@@ -31,16 +32,20 @@ OUT_TILES = M // P
 LIST_COLS = C // 16
 HALF = E // 2
 
-LOADS_BEHIND = {-1: ["x2"], 0: ["scales", "x0"], 3: ["x1"], 4: ["wp", "gate0"], 8: ["gate1"]}
-ROUNDED_BY = {5: "V", 8: "SV", 10: "SV", 11: "VV", 14: "SV", 16: "VS", 17: "SS"}
-PROJECT_STEP = [4, 6, 10, 13, 14, 18]
-SCATTER_STEP = [6, 9, 14, 17, 19, 25]
-COPIED_BY_TILE = (3, 4)
 
-RAW_BUFS = 11
-ROUNDED_BUFS = 6
-CODE_BUFS = 9
-C_BUFS = 3
+BIAS_LAG = 0
+COPY_LAG = 3
+POOL_STEPS = [6,9,12,15]
+VECTOR_STEPS = []
+SPLIT_STEPS = []
+LARGE = ["x0","x1","s","w","w","x2","w"]
+SMALL_FROM = 5
+LATE = {2: "w_first2"}
+GATE1_AT = 12
+RAW_BUFS = 15
+ROUNDED_BUFS = 4
+CODE_BUFS = 6
+C_BUFS = 2
 SUM_BANKS = 6
 
 
@@ -48,50 +53,30 @@ def tile_moe_nxt_lin_bias_kernel(tc, x_words, x_scales, w, b, wp, gate, offs, ou
     nc = tc.nc
     with ExitStack() as ctx:
         keep = ctx.enter_context(tc.tile_pool(name="keep", bufs=1))
-        raws = ctx.enter_context(tc.tile_pool(name="raws", bufs=RAW_BUFS))
-        rounded = ctx.enter_context(tc.tile_pool(name="rounded", bufs=ROUNDED_BUFS))
-        codes = ctx.enter_context(tc.tile_pool(name="codes", bufs=CODE_BUFS))
-        cwork = ctx.enter_context(tc.tile_pool(name="cwork", bufs=C_BUFS))
-        sum_banks = ctx.enter_context(tc.psum_pool(name="sum_banks", bufs=SUM_BANKS))
-        out_banks = ctx.enter_context(tc.psum_pool(name="out_banks", bufs=8 - SUM_BANKS))
+        banks = ctx.enter_context(tc.psum_pool(name="banks", bufs=1))
 
         offsets = keep.tile([P, T // 16], U16, name="offsets")
         nc.sync.dma_start(offsets[:], offs)
 
         token_scales = keep.tile([P, T // 4], I32, name="token_scales", align_bytes=64)
-        nc.gpsimd.memset(token_scales[:], 0)
-        bias = keep.tile([P, PACK, E], F32, name="bias")
-        b_rows = b.rearrange("(u j i) e -> i u j e", j=PACK, i=RUN)
-        for i in range(RUN):
-            nc.scalar.dma_start(out=bias[i:P:RUN, :, :], in_=b_rows[i])
+        nc.vector.memset(token_scales[:], 0)
 
+        bias = keep.tile([P, PACK, E], F32, name="bias")
         token_words = [keep.tile([P, T], I32, name="token_words%d" % a, align_bytes=64) for a in range(PASSES)]
-        gates = keep.tile([P, E * C], F32, name="gates")
+        gates = [keep.tile([P, HALF * C], F32, name="gates%d" % h) for h in range(2)]
         wp_raw = keep.tile([P, PACK, M], F32, name="wp_raw")
         result = [keep.tile([P, T], F32, name="result%d" % m) for m in range(OUT_TILES)]
 
-        def load_other(item):
-            if item == "scales":
-                for q in range(QUADRANTS):
-                    nc.sync.dma_start(
-                        out=token_scales[32 * q : 32 * q + 4 * PASSES, :],
-                        in_=x_scales[:, 4 * q : 4 * q + 4, :].bitcast(I32),
-                    )
-            elif item == "wp":
-                wp_rows = wp.rearrange("(u j i) f -> i u j f", j=PACK, i=RUN)
-                for i in range(RUN):
-                    nc.sync.dma_start(out=wp_raw[i:P:RUN, :, :], in_=wp_rows[i])
-            elif item.startswith("gate"):
-                cols = slice(int(item[-1]) * HALF * C, (int(item[-1]) + 1) * HALF * C)
-                nc.sync.dma_start(out=gates[:, cols], in_=gate[:P, cols])
-            else:
-                a = int(item[-1])
-                nc.sync.dma_start(out=token_words[a][:], in_=x_words[a].rearrange("p t r -> p (t r)").bitcast(I32))
+        b_rows = b.rearrange("(u j i) e -> i u j e", j=PACK, i=RUN)
+        wp_rows = wp.rearrange("(u j i) f -> i u j f", j=PACK, i=RUN)
+        small = [(bias[i:P:RUN, :, :], b_rows[i]) for i in range(RUN)]
+        small = small[:2] + [(gates[0][:], gate[:P, : HALF * C])] + small[2:]
+        small = small + [(wp_raw[i:P:RUN, :, :], wp_rows[i]) for i in range(RUN)]
 
         def load_weights(step):
             e, a = divmod(step, PASSES)
             rows = w[e, a * KP : (a + 1) * KP, :].rearrange("(p r) n -> p r n", r=PACK)
-            tile = raws.tile([P, PACK, N], F32, name="raw")
+            tile = keep.tile([P, PACK, N], F32, name="raw%d" % (step % RAW_BUFS))
             parts = 2 if step == LAST else 1
             for h in range(parts):
                 cols = slice(h * N // parts, (h + 1) * N // parts)
@@ -99,22 +84,42 @@ def tile_moe_nxt_lin_bias_kernel(tc, x_words, x_scales, w, b, wp, gate, offs, ou
             return tile
 
         raw = []
-        for step in range(-1, STEPS):
-            if step >= 0:
-                raw.append(load_weights(step))
-            for item in LOADS_BEHIND.get(step, []):
-                load_other(item)
+        large = LARGE + ["w"] * (STEPS - len([item for item in LARGE if item == "w"]))
+        for place, item in enumerate(large):
+            if item == "w":
+                raw.append(load_weights(len(raw)))
+            elif item == "s":
+                for q in range(QUADRANTS):
+                    nc.sync.dma_start(
+                        out=token_scales[32 * q : 32 * q + 4 * PASSES, :],
+                        in_=x_scales[:, 4 * q : 4 * q + 4, :].bitcast(I32),
+                    )
+            else:
+                a = int(item[-1])
+                nc.sync.dma_start(out=token_words[a][:], in_=x_words[a].rearrange("p t r -> p (t r)").bitcast(I32))
+            if place == GATE1_AT:
+                nc.sync.dma_start(out=gates[1][:], in_=gate[:P, HALF * C :])
+            if place >= SMALL_FROM:
+                for dst, src in small[:2]:
+                    nc.sync.dma_start(out=dst, in_=src)
+                small = small[2:]
 
         wp_codes = keep.tile([P, M], U32, name="wp_codes", align_bytes=64)
         wp_scales = keep.tile([P, M], U8, name="wp_scales", align_bytes=64)
-        slot_words, slot_scales, sums, biased, projected = {}, {}, {}, {}, {}
+        slot_words, slot_scales, sums, biased, projected, w_rounded = {}, {}, {}, {}, {}, {}
+
+        def rounded_tag(step):
+            if "w_first%d" % step in LATE.values():
+                return "w_first%d" % step
+            return "w_bf%d" % (len([s for s in range(step) if s not in POOL_STEPS]) % ROUNDED_BUFS)
 
         def slots_of(e, count=1):
             return offsets[:, e * LIST_COLS : (e + count) * LIST_COLS]
 
         def gather_tokens(e0):
             words = [
-                keep.tile([P, HALF * C], U32, name="slot_words%d_%d" % (e0, a), align_bytes=64) for a in range(PASSES)
+                keep.tile([P, HALF * C], U32, name=(LATE[a] if e0 and a in LATE else "slot_words%d_%d" % (e0, a)), align_bytes=64)
+                for a in range(PASSES)
             ]
             scales = keep.tile([P, HALF * C], U8, name="slot_scales%d" % e0, align_bytes=64)
             picks = slots_of(e0, HALF)
@@ -130,25 +135,41 @@ def tile_moe_nxt_lin_bias_kernel(tc, x_words, x_scales, w, b, wp, gate, offs, ou
 
         def expert_pass(step):
             e, a = divmod(step, PASSES)
-            w_bf = rounded.tile([P, N * PACK], BF16, name="w_bf", align_bytes=64)
+            if step in POOL_STEPS:
+                w_bf = w_rounded[step - 1]
+            else:
+                w_bf = keep.tile([P, N * PACK], BF16, name=rounded_tag(step), align_bytes=64)
+            w_rounded[step] = w_bf
             dst = w_bf[:].rearrange("p (j u i r) -> p u j r i", j=PACK, i=RUN, r=PACK)
             src = raw[step][:].rearrange("p r (u j i) -> p u j r i", j=PACK, i=RUN)
             if step == 0:
                 for j in range(PACK):
                     nc.scalar.activation(dst[:, :, j], src[:, :, j], COPY)
+            elif step in POOL_STEPS:
+                for j in range(PACK):
+                    nc.gpsimd.tensor_scalar(
+                        dst[:, :, j].rearrange("p u r i -> p u i r"),
+                        src[:, :, j].rearrange("p u r i -> p u i r"),
+                        1.0,
+                        0.0,
+                        MULT,
+                        ADD,
+                    )
+            elif step in VECTOR_STEPS:
+                nc.vector.tensor_copy(out=dst, in_=src)
+            elif step in SPLIT_STEPS:
+                nc.scalar.copy(out=dst[:, : GROUPS // 2], in_=src[:, : GROUPS // 2])
+                nc.vector.tensor_copy(out=dst[:, GROUPS // 2 :], in_=src[:, GROUPS // 2 :])
+            elif step == LAST:
+                nc.scalar.copy(out=dst[:, : GROUPS // 2], in_=src[:, : GROUPS // 2])
+                nc.scalar.copy(out=dst[:, GROUPS // 2 :], in_=src[:, GROUPS // 2 :])
             else:
-                engines = ROUNDED_BY.get(step, "S")
-                for h, engine in enumerate(engines):
-                    us = slice(h * GROUPS // len(engines), (h + 1) * GROUPS // len(engines))
-                    if engine == "V":
-                        nc.vector.tensor_copy(out=dst[:, us], in_=src[:, us])
-                    else:
-                        nc.scalar.copy(out=dst[:, us], in_=src[:, us])
-            w_codes = codes.tile([P, N], U32, name="w_codes", align_bytes=64)
-            w_scales = codes.tile([P, N], U8, name="w_scales", align_bytes=64)
+                nc.scalar.copy(out=dst, in_=src)
+            w_codes = keep.tile([P, N], U32, name="w_codes%d" % (step % CODE_BUFS), align_bytes=64)
+            w_scales = keep.tile([P, N], U8, name="w_scales%d" % (step % CODE_BUFS), align_bytes=64)
             nc.vector.quantize_mx(out=w_codes[:].bitcast(FP8X4), scales=w_scales[:], in_=w_bf[:])
             if a == 0:
-                sums[e] = [sum_banks.tile([P, C], F32, name="sum_bank") for j in range(PACK)]
+                sums[e] = [banks.tile([P, C], F32, name="sum_bank%d" % ((PACK * e + j) % SUM_BANKS)) for j in range(PACK)]
             for j in range(PACK):
                 cols = slice(j * P, (j + 1) * P)
                 nc.tensor.matmul_mx(
@@ -170,25 +191,26 @@ def tile_moe_nxt_lin_bias_kernel(tc, x_words, x_scales, w, b, wp, gate, offs, ou
             nc.vector.quantize_mx(out=wp_codes[:].bitcast(FP8X4), scales=wp_scales[:], in_=wp_bf[:])
 
         def project(e):
-            if PROJECT_STEP[e] <= LAST:
-                y = raw[PROJECT_STEP[e]][:, :, :C]
+            step = PASSES * e + PASSES - 1 + BIAS_LAG
+            if step <= LAST:
+                y = raw[step][:, :, :C]
             else:
                 y = keep.tile([P, PACK, C], F32, name="y_last")
             biased[e] = y
             for j in range(PACK):
                 nc.scalar.activation(y[:, j, :], sums[e][j][:], IDENTITY, bias=bias[:, j, e : e + 1])
-            c_bf = cwork.tile([P, C * PACK], BF16, name="c_bf", align_bytes=64)
-            slot_gates = gates[:, e * C : (e + 1) * C].rearrange("p (s i) -> p s i", i=PAIR)
+            c_bf = keep.tile([P, C * PACK], BF16, name=("c_first" if e == 0 else "c_bf%d" % (e % C_BUFS)), align_bytes=64)
+            slot_gates = gates[e // HALF][:, e % HALF * C : (e % HALF + 1) * C].rearrange("p (s i) -> p s i", i=PAIR)
             nc.vector.tensor_tensor(
                 c_bf[:].rearrange("p (s i j) -> p s j i", i=PAIR, j=PACK),
                 y[:, :, :].rearrange("p j (s i) -> p s j i", i=PAIR),
                 slot_gates.unsqueeze(2).to_broadcast([P, C // PAIR, PACK, PAIR]),
                 MULT,
             )
-            c_codes = cwork.tile([P, C], U32, name="c_codes", align_bytes=64)
-            c_scales = cwork.tile([P, C], U8, name="c_scales", align_bytes=64)
+            c_codes = keep.tile([P, C], U32, name="c_codes%d" % (e % C_BUFS), align_bytes=64)
+            c_scales = keep.tile([P, C], U8, name="c_scales%d" % (e % C_BUFS), align_bytes=64)
             nc.vector.quantize_mx(out=c_codes[:].bitcast(FP8X4), scales=c_scales[:], in_=c_bf[:])
-            projected[e] = out_banks.tile([P, OUT_TILES, C], F32, name="out_bank")
+            projected[e] = banks.tile([P, OUT_TILES, C], F32, name="out_bank%d" % (e % 2))
             for m in range(OUT_TILES):
                 cols = slice(m * P, (m + 1) * P)
                 nc.tensor.matmul_mx(
@@ -201,31 +223,36 @@ def tile_moe_nxt_lin_bias_kernel(tc, x_words, x_scales, w, b, wp, gate, offs, ou
                     stop=True,
                 )
 
-        def scatter(e):
-            if SCATTER_STEP[e] <= LAST:
-                staged = raw[SCATTER_STEP[e]][:, :OUT_TILES, C:]
-            elif e < E - 1:
+        def scatter(e, tiles):
+            step = min(PASSES * e + PASSES - 1 + COPY_LAG, LAST)
+            if e == E - 1:
+                staged = keep.tile([P, OUT_TILES, C], F32, name="staged_last")
+            elif step == LAST and tiles[0] > 0:
                 staged = biased[E - 1][:, :OUT_TILES, :]
             else:
-                staged = keep.tile([P, OUT_TILES, C], F32, name="staged_last")
-            if e not in COPIED_BY_TILE:
+                staged = raw[step][:, :OUT_TILES, C:]
+            if len(tiles) == OUT_TILES and e < E - 1:
                 nc.scalar.copy(out=staged[:, :, :], in_=projected[e][:])
-            for m in range(OUT_TILES):
-                if e in COPIED_BY_TILE:
+            for m in tiles:
+                if len(tiles) < OUT_TILES or e == E - 1:
                     nc.scalar.copy(out=staged[:, m, :], in_=projected[e][:, m, :])
                 nc.vector.tensor_copy(result[m][:].indirect(slots_of(e)), staged[:, m, :])
 
-        for step in range(SCATTER_STEP[-1] + 1):
-            if step <= LAST:
-                if step % (HALF * PASSES) == 0:
-                    gather_tokens(step // PASSES)
-                expert_pass(step)
-                if step == PASSES - 1:
-                    quantise_wp()
-            if step in SCATTER_STEP:
-                scatter(SCATTER_STEP.index(step))
-            if step in PROJECT_STEP:
-                project(PROJECT_STEP.index(step))
+        for step in range(STEPS):
+            if step % (HALF * PASSES) == 0:
+                gather_tokens(step // PASSES)
+            expert_pass(step)
+            if step == PASSES - 1:
+                quantise_wp()
+            e, a = divmod(step + 1 - COPY_LAG, PASSES)
+            if a == 0 and e >= 1:
+                scatter(e - 1, [0] if step == LAST else [0, 1])
+            e, a = divmod(step + 1 - BIAS_LAG, PASSES)
+            if a == 0 and e >= 1 and e < E:
+                project(e - 1)
+        project(E - 1)
+        scatter(E - 2, [1])
+        scatter(E - 1, [0, 1])
 
         for m in range(OUT_TILES):
             nc.sync.dma_start(out=out[m * P : (m + 1) * P, :], in_=result[m][:])

@@ -1,6 +1,7 @@
 from contextlib import ExitStack
 
 import concourse.mybir as mybir
+from concourse.masks import make_identity
 
 K, T, E, C, N, M = 1536, 1536, 6, 256, 512, 256
 P = 128
@@ -33,19 +34,18 @@ LIST_COLS = C // 16
 HALF = E // 2
 
 
-BIAS_LAG = 0
-COPY_LAG = 3
-POOL_STEPS = [6,9,12,15]
-VECTOR_STEPS = []
-SPLIT_STEPS = []
-LARGE = ["x0","x1","s","w","w","x2","w"]
-SMALL_FROM = 5
-LATE = {2: "w_first2"}
-GATE1_AT = 12
-RAW_BUFS = 15
-ROUNDED_BUFS = 4
-CODE_BUFS = 6
-C_BUFS = 2
+QUARTER = P * PACK
+POOL_FROM = 2
+POOL_TILES = 4
+REST_ON = "V"
+LARGE = ["x0","x1","s","w","w","w","x2"]
+SMALL_FROM = 6
+SMALL_EACH = 4
+GATE_AT = [3]
+LATE = {1: 2, 2: 2}
+SPLIT = [4]
+RAW_BUFS = 16
+CODE_BUFS = 4
 SUM_BANKS = 6
 
 
@@ -55,39 +55,47 @@ def tile_moe_nxt_lin_bias_kernel(tc, x_words, x_scales, w, b, wp, gate, offs, ou
         keep = ctx.enter_context(tc.tile_pool(name="keep", bufs=1))
         banks = ctx.enter_context(tc.psum_pool(name="banks", bufs=1))
 
+        def tile(shape, dtype, name, tag=None):
+            return keep.tile(shape, dtype, name=name, tag=tag or name, align_bytes=64)
+
+        def slot(step):
+            return "slot%d" % (step % RAW_BUFS)
+
         offsets = keep.tile([P, T // 16], U16, name="offsets")
         nc.sync.dma_start(offsets[:], offs)
 
-        token_scales = keep.tile([P, T // 4], I32, name="token_scales", align_bytes=64)
+        token_scales = tile([P, T // 4], I32, "token_scales")
         nc.vector.memset(token_scales[:], 0)
-
-        bias = keep.tile([P, PACK, E], F32, name="bias")
-        token_words = [keep.tile([P, T], I32, name="token_words%d" % a, align_bytes=64) for a in range(PASSES)]
-        gates = [keep.tile([P, HALF * C], F32, name="gates%d" % h) for h in range(2)]
-        wp_raw = keep.tile([P, PACK, M], F32, name="wp_raw")
-        result = [keep.tile([P, T], F32, name="result%d" % m) for m in range(OUT_TILES)]
+        bias = tile([P, PACK, E], F32, "bias")
+        token_words = [tile([P, T], I32, "token_words%d" % a) for a in range(PASSES)]
+        identity = tile([P, P], F32, "identity")
+        make_identity(nc, identity[:])
+        gate_rows = tile([P, P], F32, "gate_rows")
+        nc.gpsimd.memset(gate_rows[:], 0.0)
+        wp_raw = tile([P, PACK, M], F32, "wp_raw")
+        result = [tile([P, T], F32, "result%d" % m) for m in range(OUT_TILES)]
 
         b_rows = b.rearrange("(u j i) e -> i u j e", j=PACK, i=RUN)
-        wp_rows = wp.rearrange("(u j i) f -> i u j f", j=PACK, i=RUN)
+        wp_rows = wp.rearrange("(u j i) f -> j u i f", j=PACK, i=RUN)
         small = [(bias[i:P:RUN, :, :], b_rows[i]) for i in range(RUN)]
-        small = small[:2] + [(gates[0][:], gate[:P, : HALF * C])] + small[2:]
-        small = small + [(wp_raw[i:P:RUN, :, :], wp_rows[i]) for i in range(RUN)]
+        small = small + [(wp_raw[:, j, :], wp_rows[j]) for j in range(PACK)]
+        small = small[RUN:] + small[:RUN]
+
+        raw = {}
 
         def load_weights(step):
             e, a = divmod(step, PASSES)
             rows = w[e, a * KP : (a + 1) * KP, :].rearrange("(p r) n -> p r n", r=PACK)
-            tile = keep.tile([P, PACK, N], F32, name="raw%d" % (step % RAW_BUFS))
+            raw[step] = tile([P, PACK, N], F32, "raw", slot(step))
             parts = 2 if step == LAST else 1
             for h in range(parts):
                 cols = slice(h * N // parts, (h + 1) * N // parts)
-                nc.sync.dma_start(out=tile[:, :, cols], in_=rows[:, :, cols])
-            return tile
+                nc.sync.dma_start(out=raw[step][:, :, cols], in_=rows[:, :, cols])
 
-        raw = []
-        large = LARGE + ["w"] * (STEPS - len([item for item in LARGE if item == "w"]))
+        large = LARGE + ["w"] * (RAW_BUFS - len([item for item in LARGE if item == "w"]))
         for place, item in enumerate(large):
             if item == "w":
-                raw.append(load_weights(len(raw)))
+                load_weights(len(raw))
             elif item == "s":
                 for q in range(QUADRANTS):
                     nc.sync.dma_start(
@@ -97,56 +105,55 @@ def tile_moe_nxt_lin_bias_kernel(tc, x_words, x_scales, w, b, wp, gate, offs, ou
             else:
                 a = int(item[-1])
                 nc.sync.dma_start(out=token_words[a][:], in_=x_words[a].rearrange("p t r -> p (t r)").bitcast(I32))
-            if place == GATE1_AT:
-                nc.sync.dma_start(out=gates[1][:], in_=gate[:P, HALF * C :])
+            if place == GATE_AT[0]:
+                nc.sync.dma_start(out=gate_rows[: T // P, :], in_=gate[0].rearrange("(c s) -> c s", s=P))
             if place >= SMALL_FROM:
-                for dst, src in small[:2]:
+                for dst, src in small[:SMALL_EACH]:
                     nc.sync.dma_start(out=dst, in_=src)
-                small = small[2:]
+                small = small[SMALL_EACH:]
 
-        wp_codes = keep.tile([P, M], U32, name="wp_codes", align_bytes=64)
-        wp_scales = keep.tile([P, M], U8, name="wp_scales", align_bytes=64)
-        slot_words, slot_scales, sums, biased, projected, w_rounded = {}, {}, {}, {}, {}, {}
+        turned = banks.tile([P, C], F32, name="out_bank0")
+        nc.tensor.transpose(turned[:, :P], gate_rows[:], identity[:])
+        slot_gate = tile([P, T // P], F32, "slot_gate")
+        nc.scalar.copy(out=slot_gate[:], in_=turned[:, : T // P])
 
-        def rounded_tag(step):
-            if "w_first%d" % step in LATE.values():
-                return "w_first%d" % step
-            return "w_bf%d" % (len([s for s in range(step) if s not in POOL_STEPS]) % ROUNDED_BUFS)
+        wp_codes = tile([P, M], U32, "wp_codes")
+        wp_scales = tile([P, M], U8, "wp_scales")
+        w_middle = tile([P, N * PACK], BF16, "w_middle")
+        slot_words, slot_scales, sums, biased, projected, rounded = {}, {}, {}, {}, {}, {}
 
         def slots_of(e, count=1):
             return offsets[:, e * LIST_COLS : (e + count) * LIST_COLS]
 
-        def gather_tokens(e0):
-            words = [
-                keep.tile([P, HALF * C], U32, name=(LATE[a] if e0 and a in LATE else "slot_words%d_%d" % (e0, a)), align_bytes=64)
-                for a in range(PASSES)
-            ]
-            scales = keep.tile([P, HALF * C], U8, name="slot_scales%d" % e0, align_bytes=64)
-            picks = slots_of(e0, HALF)
-            nc.vector.tensor_copy(words[0][:], token_words[0][:].bitcast(U32).indirect(picks))
-            nc.vector.tensor_copy(scales[:], token_scales[:].bitcast(U8).indirect(picks))
-            for a in range(1, PASSES):
-                nc.vector.tensor_copy(words[a][:], token_words[a][:].bitcast(U32).indirect(picks))
+        def gather_words(e0, a, tag=None):
+            words = tile([P, HALF * C], U32, "slot_words%d_%d" % (e0, a), tag)
+            nc.vector.tensor_copy(words[:], token_words[a][:].bitcast(U32).indirect(slots_of(e0, HALF)))
             for e in range(e0, e0 + HALF):
-                cols = slice((e - e0) * C, (e - e0 + 1) * C)
-                for a in range(PASSES):
-                    slot_words[e, a] = words[a][:, cols]
-                    slot_scales[e, a] = scales[4 * a : P, cols]
+                slot_words[e, a] = words[:, (e - e0) * C : (e - e0 + 1) * C]
 
-        def expert_pass(step):
+        def gather_scales(e0):
+            scales = tile([P, HALF * C], U8, "slot_scales%d" % e0)
+            nc.vector.tensor_copy(scales[:], token_scales[:].bitcast(U8).indirect(slots_of(e0, HALF)))
+            for e in range(e0, e0 + HALF):
+                for a in range(PASSES):
+                    slot_scales[e, a] = scales[4 * a : P, (e - e0) * C : (e - e0 + 1) * C]
+
+        def round_weights(step):
             e, a = divmod(step, PASSES)
-            if step in POOL_STEPS:
-                w_bf = w_rounded[step - 1]
+            if a == 1:
+                w_bf = w_middle[:]
+            elif step in LATE.values():
+                w_bf = tile([P, N * PACK], BF16, "w_bf", "late%d" % step)[:]
             else:
-                w_bf = keep.tile([P, N * PACK], BF16, name=rounded_tag(step), align_bytes=64)
-            w_rounded[step] = w_bf
-            dst = w_bf[:].rearrange("p (j u i r) -> p u j r i", j=PACK, i=RUN, r=PACK)
+                w_bf = tile([P, N * PACK], BF16, "w_bf", "w_bf%d" % (a // 2 + 2 * (e % 2)))[:]
+            rounded[step] = w_bf
+            dst = w_bf.rearrange("p (j u i r) -> p u j r i", j=PACK, i=RUN, r=PACK)
             src = raw[step][:].rearrange("p r (u j i) -> p u j r i", j=PACK, i=RUN)
             if step == 0:
                 for j in range(PACK):
                     nc.scalar.activation(dst[:, :, j], src[:, :, j], COPY)
-            elif step in POOL_STEPS:
-                for j in range(PACK):
+            elif a == 1 and e >= POOL_FROM:
+                for j in range(POOL_TILES):
                     nc.gpsimd.tensor_scalar(
                         dst[:, :, j].rearrange("p u r i -> p u i r"),
                         src[:, :, j].rearrange("p u r i -> p u i r"),
@@ -155,9 +162,13 @@ def tile_moe_nxt_lin_bias_kernel(tc, x_words, x_scales, w, b, wp, gate, offs, ou
                         MULT,
                         ADD,
                     )
-            elif step in VECTOR_STEPS:
+                if POOL_TILES < PACK and REST_ON == "S":
+                    nc.scalar.copy(out=dst[:, :, POOL_TILES:], in_=src[:, :, POOL_TILES:])
+                if POOL_TILES < PACK and REST_ON == "V":
+                    nc.vector.tensor_copy(out=dst[:, :, POOL_TILES:], in_=src[:, :, POOL_TILES:])
+            elif step in []:
                 nc.vector.tensor_copy(out=dst, in_=src)
-            elif step in SPLIT_STEPS:
+            elif step in SPLIT:
                 nc.scalar.copy(out=dst[:, : GROUPS // 2], in_=src[:, : GROUPS // 2])
                 nc.vector.tensor_copy(out=dst[:, GROUPS // 2 :], in_=src[:, GROUPS // 2 :])
             elif step == LAST:
@@ -165,15 +176,25 @@ def tile_moe_nxt_lin_bias_kernel(tc, x_words, x_scales, w, b, wp, gate, offs, ou
                 nc.scalar.copy(out=dst[:, GROUPS // 2 :], in_=src[:, GROUPS // 2 :])
             else:
                 nc.scalar.copy(out=dst, in_=src)
-            w_codes = keep.tile([P, N], U32, name="w_codes%d" % (step % CODE_BUFS), align_bytes=64)
-            w_scales = keep.tile([P, N], U8, name="w_scales%d" % (step % CODE_BUFS), align_bytes=64)
-            nc.vector.quantize_mx(out=w_codes[:].bitcast(FP8X4), scales=w_scales[:], in_=w_bf[:])
+
+        def multiply(step, tag=None):
+            e, a = divmod(step, PASSES)
+            w_codes = tile([P, N], U32, "w_codes", tag or "w_codes%d" % (step % CODE_BUFS))
+            w_scales = tile([P, N], U8, "w_scales", "w_scales%d" % (step % CODE_BUFS))
+            nc.vector.quantize_mx(out=w_codes[:].bitcast(FP8X4), scales=w_scales[:], in_=rounded[step])
             if a == 0:
-                sums[e] = [banks.tile([P, C], F32, name="sum_bank%d" % ((PACK * e + j) % SUM_BANKS)) for j in range(PACK)]
+                sums[e] = [
+                    banks.tile([P, 2 * C], F32, name="sum_bank%d" % ((PACK * e + j) % SUM_BANKS)) for j in range(PACK)
+                ]
+                for h in range(C // P):
+                    column = slot_gate[:, e * C // P + h : e * C // P + h + 1]
+                    nc.tensor.transpose(
+                        sums[e][3][:, C + h * P : C + (h + 1) * P], column.to_broadcast([P, P]), identity[:]
+                    )
             for j in range(PACK):
                 cols = slice(j * P, (j + 1) * P)
                 nc.tensor.matmul_mx(
-                    out=sums[e][j][:],
+                    out=sums[e][j][:, :C],
                     lhsT=w_codes[:, cols].bitcast(FP8X4),
                     lhsT_scale=w_scales[:, cols],
                     rhs=slot_words[e, a].bitcast(FP8X4),
@@ -183,38 +204,35 @@ def tile_moe_nxt_lin_bias_kernel(tc, x_words, x_scales, w, b, wp, gate, offs, ou
                 )
 
         def quantise_wp():
-            wp_bf = keep.tile([P, M * PACK], BF16, name="wp_bf", align_bytes=64)
+            wp_bf = tile([P, M * PACK], BF16, "wp_bf")
             nc.vector.tensor_copy(
                 out=wp_bf[:].rearrange("p (f i j) -> p f j i", i=PAIR, j=PACK),
                 in_=wp_raw[:].rearrange("p j (f i) -> p f j i", i=PAIR),
             )
             nc.vector.quantize_mx(out=wp_codes[:].bitcast(FP8X4), scales=wp_scales[:], in_=wp_bf[:])
 
-        def project(e):
-            step = PASSES * e + PASSES - 1 + BIAS_LAG
-            if step <= LAST:
-                y = raw[step][:, :, :C]
-            else:
-                y = keep.tile([P, PACK, C], F32, name="y_last")
+        def add_bias(e, y):
             biased[e] = y
             for j in range(PACK):
-                nc.scalar.activation(y[:, j, :], sums[e][j][:], IDENTITY, bias=bias[:, j, e : e + 1])
-            c_bf = keep.tile([P, C * PACK], BF16, name=("c_first" if e == 0 else "c_bf%d" % (e % C_BUFS)), align_bytes=64)
-            slot_gates = gates[e // HALF][:, e % HALF * C : (e % HALF + 1) * C].rearrange("p (s i) -> p s i", i=PAIR)
+                nc.scalar.activation(biased[e][:, j, :], sums[e][j][:, :C], IDENTITY, bias=bias[:, j, e : e + 1])
+
+        def project(e):
+            c_bf = tile([P, C * PACK], BF16, "c_bf", "c_bf%d" % (e % 2))
+            slot_gates = sums[e][3][:, C:].rearrange("p (s i) -> p s i", i=PAIR)
             nc.vector.tensor_tensor(
                 c_bf[:].rearrange("p (s i j) -> p s j i", i=PAIR, j=PACK),
-                y[:, :, :].rearrange("p j (s i) -> p s j i", i=PAIR),
+                biased[e].rearrange("p j (s i) -> p s j i", i=PAIR),
                 slot_gates.unsqueeze(2).to_broadcast([P, C // PAIR, PACK, PAIR]),
                 MULT,
             )
-            c_codes = keep.tile([P, C], U32, name="c_codes%d" % (e % C_BUFS), align_bytes=64)
-            c_scales = keep.tile([P, C], U8, name="c_scales%d" % (e % C_BUFS), align_bytes=64)
+            c_codes = tile([P, C], U32, "c_codes", "c_codes%d" % (e % 2))
+            c_scales = tile([P, C], U8, "c_scales", "c_scales%d" % (e % 2))
             nc.vector.quantize_mx(out=c_codes[:].bitcast(FP8X4), scales=c_scales[:], in_=c_bf[:])
-            projected[e] = banks.tile([P, OUT_TILES, C], F32, name="out_bank%d" % (e % 2))
+            projected[e] = [banks.tile([P, C], F32, name="out_bank%d" % m) for m in range(OUT_TILES)]
             for m in range(OUT_TILES):
                 cols = slice(m * P, (m + 1) * P)
                 nc.tensor.matmul_mx(
-                    out=projected[e][:, m, :],
+                    out=projected[e][m][:],
                     lhsT=wp_codes[:, cols].bitcast(FP8X4),
                     lhsT_scale=wp_scales[:, cols],
                     rhs=c_codes[:].bitcast(FP8X4),
@@ -223,36 +241,41 @@ def tile_moe_nxt_lin_bias_kernel(tc, x_words, x_scales, w, b, wp, gate, offs, ou
                     stop=True,
                 )
 
-        def scatter(e, tiles):
-            step = min(PASSES * e + PASSES - 1 + COPY_LAG, LAST)
-            if e == E - 1:
-                staged = keep.tile([P, OUT_TILES, C], F32, name="staged_last")
-            elif step == LAST and tiles[0] > 0:
-                staged = biased[E - 1][:, :OUT_TILES, :]
-            else:
-                staged = raw[step][:, :OUT_TILES, C:]
-            if len(tiles) == OUT_TILES and e < E - 1:
-                nc.scalar.copy(out=staged[:, :, :], in_=projected[e][:])
-            for m in tiles:
-                if len(tiles) < OUT_TILES or e == E - 1:
-                    nc.scalar.copy(out=staged[:, m, :], in_=projected[e][:, m, :])
+        def scatter(e, staged):
+            for m in range(OUT_TILES):
+                nc.scalar.copy(out=staged[:, m, :], in_=projected[e][m][:])
                 nc.vector.tensor_copy(result[m][:].indirect(slots_of(e)), staged[:, m, :])
 
-        for step in range(STEPS):
-            if step % (HALF * PASSES) == 0:
-                gather_tokens(step // PASSES)
-            expert_pass(step)
-            if step == PASSES - 1:
+        for a in range(PASSES):
+            gather_words(0, a)
+            if a not in LATE:
+                gather_words(HALF, a)
+        gather_scales(0)
+        gather_scales(HALF)
+        for e in range(E):
+            first, middle, last = range(PASSES * e, PASSES * (e + 1))
+            round_weights(first)
+            if e > 0:
+                add_bias(e - 1, tile([P, PACK, C], F32, "y")[:])
+            if e == 1:
                 quantise_wp()
-            e, a = divmod(step + 1 - COPY_LAG, PASSES)
-            if a == 0 and e >= 1:
-                scatter(e - 1, [0] if step == LAST else [0, 1])
-            e, a = divmod(step + 1 - BIAS_LAG, PASSES)
-            if a == 0 and e >= 1 and e < E:
+            if e > 0:
                 project(e - 1)
+            multiply(first, "y" if e >= 1 else None)
+            round_weights(middle)
+            multiply(middle)
+            round_weights(last)
+            multiply(last)
+            for a in LATE:
+                if LATE[a] // PASSES == e:
+                    gather_words(HALF, a, "late%d" % LATE[a] if a == PASSES - 1 else slot(last))
+            if e > 0:
+                scatter(e - 1, raw[last][:, :OUT_TILES, :C])
+            for step in range(first + RAW_BUFS, min(last + RAW_BUFS + 1, STEPS)):
+                load_weights(step)
+        add_bias(E - 1, raw[LAST][:, :, C:])
         project(E - 1)
-        scatter(E - 2, [1])
-        scatter(E - 1, [0, 1])
+        scatter(E - 1, tile([P, OUT_TILES, C], F32, "staged_last")[:])
 
         for m in range(OUT_TILES):
             nc.sync.dma_start(out=out[m * P : (m + 1) * P, :], in_=result[m][:])

@@ -21,7 +21,7 @@ MULT = mybir.AluOpType.mult
 ADD = mybir.AluOpType.add
 
 PACK = 4
-RUN = 4
+RUN = 2
 PAIR = 2
 KP = P * PACK
 PASSES = K // KP
@@ -155,8 +155,8 @@ def tile_moe_nxt_lin_bias_kernel(tc, x_words, x_scales, w, b, wp, gate, offs, ou
             elif a == 1 and e >= POOL_FROM:
                 for j in range(POOL_TILES):
                     nc.gpsimd.tensor_scalar(
-                        dst[:, :, j].rearrange("p u r i -> p u i r"),
-                        src[:, :, j].rearrange("p u r i -> p u i r"),
+                        dst[:, :, j],
+                        src[:, :, j],
                         1.0,
                         0.0,
                         MULT,

@@ -38,12 +38,12 @@ QUARTER = P * PACK
 POOL_FROM = 2
 POOL_TILES = 4
 REST_ON = "V"
-LARGE = ["x0","x1","s","w","w","w","x2"]
+LARGE = ["s","x0","x1","w","w","w","x2"]
 SMALL_FROM = 6
 SMALL_EACH = 4
 GATE_AT = [3]
 LATE = {1: 2, 2: 2}
-SPLIT = [4]
+SPLIT = []
 RAW_BUFS = 16
 CODE_BUFS = 4
 SUM_BANKS = 6
@@ -66,18 +66,19 @@ def tile_moe_nxt_lin_bias_kernel(tc, x_words, x_scales, w, b, wp, gate, offs, ou
 
         token_scales = tile([P, T // 4], I32, "token_scales")
         nc.vector.memset(token_scales[:], 0)
-        bias = tile([P, PACK, E], F32, "bias")
+        bias_run = ((PACK - 1) * RUN + 1) * E
+        bias = tile([P, bias_run], F32, "bias")
         token_words = [tile([P, T], I32, "token_words%d" % a) for a in range(PASSES)]
         identity = tile([P, P], F32, "identity")
         make_identity(nc, identity[:])
         gate_rows = tile([P, P], F32, "gate_rows")
-        nc.gpsimd.memset(gate_rows[:], 0.0)
+        nc.vector.memset(gate_rows[:], 0.0)
         wp_raw = tile([P, PACK, M], F32, "wp_raw")
         result = [tile([P, T], F32, "result%d" % m) for m in range(OUT_TILES)]
 
-        b_rows = b.rearrange("(u j i) e -> i u j e", j=PACK, i=RUN)
+        b_groups = b.rearrange("(u x) e -> u (x e)", x=PACK * RUN)
         wp_rows = wp.rearrange("(u j i) f -> j u i f", j=PACK, i=RUN)
-        small = [(bias[i:P:RUN, :, :], b_rows[i]) for i in range(RUN)]
+        small = [(bias[i:P:RUN, :], b_groups[:, i * E : i * E + bias_run]) for i in range(RUN)]
         small = small + [(wp_raw[:, j, :], wp_rows[j]) for j in range(PACK)]
         small = small[RUN:] + small[:RUN]
 
@@ -98,7 +99,7 @@ def tile_moe_nxt_lin_bias_kernel(tc, x_words, x_scales, w, b, wp, gate, offs, ou
                 load_weights(len(raw))
             elif item == "s":
                 for q in range(QUADRANTS):
-                    nc.sync.dma_start(
+                    nc.gpsimd.dma_start(
                         out=token_scales[32 * q : 32 * q + 4 * PASSES, :],
                         in_=x_scales[:, 4 * q : 4 * q + 4, :].bitcast(I32),
                     )
@@ -119,7 +120,7 @@ def tile_moe_nxt_lin_bias_kernel(tc, x_words, x_scales, w, b, wp, gate, offs, ou
 
         wp_codes = tile([P, M], U32, "wp_codes")
         wp_scales = tile([P, M], U8, "wp_scales")
-        w_middle = tile([P, N * PACK], BF16, "w_middle")
+        w_pair = [tile([P, N * PACK], BF16, "w_pair%d" % h) for h in range(2)]
         slot_words, slot_scales, sums, biased, projected, rounded = {}, {}, {}, {}, {}, {}
 
         def slots_of(e, count=1):
@@ -138,10 +139,16 @@ def tile_moe_nxt_lin_bias_kernel(tc, x_words, x_scales, w, b, wp, gate, offs, ou
                 for a in range(PASSES):
                     slot_scales[e, a] = scales[4 * a : P, (e - e0) * C : (e - e0 + 1) * C]
 
+        def pool_tiles(step):
+            e, a = divmod(step, PASSES)
+            if e >= POOL_FROM:
+                return [1,4,0][a]
+            return {3: 1}.get(step, 0)
+
         def round_weights(step):
             e, a = divmod(step, PASSES)
-            if a == 1:
-                w_bf = w_middle[:]
+            if a < PASSES - 1:
+                w_bf = w_pair[(e + a) % 2][:]
             elif step in LATE.values():
                 w_bf = tile([P, N * PACK], BF16, "w_bf", "late%d" % step)[:]
             else:
@@ -152,21 +159,12 @@ def tile_moe_nxt_lin_bias_kernel(tc, x_words, x_scales, w, b, wp, gate, offs, ou
             if step == 0:
                 for j in range(PACK):
                     nc.scalar.activation(dst[:, :, j], src[:, :, j], COPY)
-            elif a == 1 and e >= POOL_FROM:
-                for j in range(POOL_TILES):
-                    nc.gpsimd.tensor_scalar(
-                        dst[:, :, j],
-                        src[:, :, j],
-                        1.0,
-                        0.0,
-                        MULT,
-                        ADD,
-                    )
-                if POOL_TILES < PACK and REST_ON == "S":
-                    nc.scalar.copy(out=dst[:, :, POOL_TILES:], in_=src[:, :, POOL_TILES:])
-                if POOL_TILES < PACK and REST_ON == "V":
-                    nc.vector.tensor_copy(out=dst[:, :, POOL_TILES:], in_=src[:, :, POOL_TILES:])
-            elif step in []:
+            elif pool_tiles(step):
+                for j in range(pool_tiles(step)):
+                    nc.gpsimd.tensor_scalar(dst[:, :, j], src[:, :, j], 1.0, 0.0, MULT, ADD)
+                if pool_tiles(step) < PACK:
+                    nc.scalar.copy(out=dst[:, :, pool_tiles(step) :], in_=src[:, :, pool_tiles(step) :])
+            elif step in [4]:
                 nc.vector.tensor_copy(out=dst, in_=src)
             elif step in SPLIT:
                 nc.scalar.copy(out=dst[:, : GROUPS // 2], in_=src[:, : GROUPS // 2])
@@ -205,16 +203,16 @@ def tile_moe_nxt_lin_bias_kernel(tc, x_words, x_scales, w, b, wp, gate, offs, ou
 
         def quantise_wp():
             wp_bf = tile([P, M * PACK], BF16, "wp_bf")
-            nc.vector.tensor_copy(
-                out=wp_bf[:].rearrange("p (f i j) -> p f j i", i=PAIR, j=PACK),
-                in_=wp_raw[:].rearrange("p j (f i) -> p f j i", i=PAIR),
+            nc.scalar.copy(
+                out=wp_bf[:].rearrange("p (f i j) -> p f j i", i=RUN, j=PACK),
+                in_=wp_raw[:].rearrange("p j (f i) -> p f j i", i=RUN),
             )
             nc.vector.quantize_mx(out=wp_codes[:].bitcast(FP8X4), scales=wp_scales[:], in_=wp_bf[:])
 
         def add_bias(e, y):
             biased[e] = y
             for j in range(PACK):
-                nc.scalar.activation(biased[e][:, j, :], sums[e][j][:, :C], IDENTITY, bias=bias[:, j, e : e + 1])
+                nc.scalar.activation(biased[e][:, j, :], sums[e][j][:, :C], IDENTITY, bias=bias[:, j * RUN * E + e : j * RUN * E + e + 1])
 
         def project(e):
             c_bf = tile([P, C * PACK], BF16, "c_bf", "c_bf%d" % (e % 2))
@@ -241,10 +239,9 @@ def tile_moe_nxt_lin_bias_kernel(tc, x_words, x_scales, w, b, wp, gate, offs, ou
                     stop=True,
                 )
 
-        def scatter(e, staged):
-            for m in range(OUT_TILES):
-                nc.scalar.copy(out=staged[:, m, :], in_=projected[e][m][:])
-                nc.vector.tensor_copy(result[m][:].indirect(slots_of(e)), staged[:, m, :])
+        def scatter(e, m, staged):
+            nc.scalar.copy(out=staged, in_=projected[e][m][:])
+            nc.vector.tensor_copy(result[m][:].indirect(slots_of(e)), staged)
 
         for a in range(PASSES):
             gather_words(0, a)
@@ -269,13 +266,16 @@ def tile_moe_nxt_lin_bias_kernel(tc, x_words, x_scales, w, b, wp, gate, offs, ou
             for a in LATE:
                 if LATE[a] // PASSES == e:
                     gather_words(HALF, a, "late%d" % LATE[a] if a == PASSES - 1 else slot(last))
-            if e > 0:
-                scatter(e - 1, raw[last][:, :OUT_TILES, :C])
+            for m in range(OUT_TILES if e < E - 1 else 2):
+                if e > 0:
+                    scatter(e - 1, m, raw[last][:, m, :C])
             for step in range(first + RAW_BUFS, min(last + RAW_BUFS + 1, STEPS)):
                 load_weights(step)
         add_bias(E - 1, raw[LAST][:, :, C:])
         project(E - 1)
-        scatter(E - 1, tile([P, OUT_TILES, C], F32, "staged_last")[:])
+        staged_last = tile([P, OUT_TILES, C], F32, "staged_last")
+        for m in range(OUT_TILES):
+            scatter(E - 1, m, staged_last[:, m, :])
 
         for m in range(OUT_TILES):
             nc.sync.dma_start(out=out[m * P : (m + 1) * P, :], in_=result[m][:])

@@ -35,18 +35,13 @@ HALF = E // 2
 
 
 QUARTER = P * PACK
-POOL_FROM = 2
-POOL_TILES = 4
-REST_ON = "V"
-LARGE = ["s","x0","x1","w","w","w","x2"]
-SMALL_FROM = 6
-SMALL_EACH = 4
-GATE_AT = [3]
-LATE = {1: 2, 2: 2}
-SPLIT = []
+LOW, HIGH, ALL = [0, 1], [2, 3], [0, 1, 2, 3]
+SHARE = 16
 RAW_BUFS = 16
 CODE_BUFS = 4
 SUM_BANKS = 6
+POOL_TILES = {3: 1, 4: 3, 6: 1, 7: 3, 9: 1, 10: 3, 12: 1, 13: 3, 15: 1, 16: 3}
+ORDER = ["x0", "g", "w", "b", "x1", "w", "x2", "w", "w", "p", "w"]
 
 
 def tile_moe_nxt_lin_bias_kernel(tc, x_words, x_scales, w, b, wp, gate, offs, out):
@@ -65,22 +60,24 @@ def tile_moe_nxt_lin_bias_kernel(tc, x_words, x_scales, w, b, wp, gate, offs, ou
         nc.sync.dma_start(offsets[:], offs)
 
         token_scales = tile([P, T // 4], I32, "token_scales")
+        gate_rows = tile([P, P], F32, "gate_rows")
+        nc.vector.memset(gate_rows[:], 0.0)
         nc.vector.memset(token_scales[:], 0)
+        for q in range(QUADRANTS):
+            nc.gpsimd.dma_start(
+                out=token_scales[32 * q : 32 * q + 4 * PASSES, :],
+                in_=x_scales[:, 4 * q : 4 * q + 4, :].bitcast(I32),
+            )
         bias_run = ((PACK - 1) * RUN + 1) * E
         bias = tile([P, bias_run], F32, "bias")
         token_words = [tile([P, T], I32, "token_words%d" % a) for a in range(PASSES)]
         identity = tile([P, P], F32, "identity")
         make_identity(nc, identity[:])
-        gate_rows = tile([P, P], F32, "gate_rows")
-        nc.vector.memset(gate_rows[:], 0.0)
         wp_raw = tile([P, PACK, M], F32, "wp_raw")
         result = [tile([P, T], F32, "result%d" % m) for m in range(OUT_TILES)]
 
         b_groups = b.rearrange("(u x) e -> u (x e)", x=PACK * RUN)
         wp_rows = wp.rearrange("(u j i) f -> j u i f", j=PACK, i=RUN)
-        small = [(bias[i:P:RUN, :], b_groups[:, i * E : i * E + bias_run]) for i in range(RUN)]
-        small = small + [(wp_raw[:, j, :], wp_rows[j]) for j in range(PACK)]
-        small = small[RUN:] + small[:RUN]
 
         raw = {}
 
@@ -93,112 +90,120 @@ def tile_moe_nxt_lin_bias_kernel(tc, x_words, x_scales, w, b, wp, gate, offs, ou
                 cols = slice(h * N // parts, (h + 1) * N // parts)
                 nc.sync.dma_start(out=raw[step][:, :, cols], in_=rows[:, :, cols])
 
-        large = LARGE + ["w"] * (RAW_BUFS - len([item for item in LARGE if item == "w"]))
-        for place, item in enumerate(large):
+        for item in ORDER + ["w"] * (RAW_BUFS - len([item for item in ORDER if item == "w"])):
             if item == "w":
                 load_weights(len(raw))
-            elif item == "s":
-                for q in range(QUADRANTS):
-                    nc.gpsimd.dma_start(
-                        out=token_scales[32 * q : 32 * q + 4 * PASSES, :],
-                        in_=x_scales[:, 4 * q : 4 * q + 4, :].bitcast(I32),
-                    )
+            elif item == "b":
+                for i in range(RUN):
+                    nc.sync.dma_start(out=bias[i:P:RUN, :], in_=b_groups[:, i * E : i * E + bias_run])
+            elif item == "g":
+                gate_chunks = gate[0].rearrange("(c s) -> c s", s=P)
+                nc.sync.dma_start(out=gate_rows[:8, :], in_=gate_chunks[:8])
+                nc.sync.dma_start(out=gate_rows[8:12, :], in_=gate_chunks[8:])
+            elif item == "p":
+                for j in range(PACK):
+                    nc.sync.dma_start(out=wp_raw[:, j, :], in_=wp_rows[j])
             else:
                 a = int(item[-1])
                 nc.sync.dma_start(out=token_words[a][:], in_=x_words[a].rearrange("p t r -> p (t r)").bitcast(I32))
-            if place == GATE_AT[0]:
-                nc.sync.dma_start(out=gate_rows[: T // P, :], in_=gate[0].rearrange("(c s) -> c s", s=P))
-            if place >= SMALL_FROM:
-                for dst, src in small[:SMALL_EACH]:
-                    nc.sync.dma_start(out=dst, in_=src)
-                small = small[SMALL_EACH:]
 
         turned = banks.tile([P, C], F32, name="out_bank0")
         nc.tensor.transpose(turned[:, :P], gate_rows[:], identity[:])
         slot_gate = tile([P, T // P], F32, "slot_gate")
         nc.scalar.copy(out=slot_gate[:], in_=turned[:, : T // P])
+        expert_bias = [tile([P, PACK], F32, "expert_bias%d" % e) for e in range(E)]
+        for e in range(E):
+            nc.scalar.copy(out=expert_bias[e][:], in_=bias[:, e : bias_run : RUN * E])
 
         wp_codes = tile([P, M], U32, "wp_codes")
         wp_scales = tile([P, M], U8, "wp_scales")
-        w_pair = [tile([P, N * PACK], BF16, "w_pair%d" % h) for h in range(2)]
-        slot_words, slot_scales, sums, biased, projected, rounded = {}, {}, {}, {}, {}, {}
+        w_ends = [tile([P, (2 * PACK - 1) * QUARTER], BF16, "w_ends%d" % h) for h in range(2)]
+        w_middle = tile([P, N * PACK], BF16, "w_middle")
+        slot_words, slot_scales, sums, biased, projected, rounded, gated = {}, {}, {}, {}, {}, {}, {}
+
+        whole = []
 
         def slots_of(e, count=1):
             return offsets[:, e * LIST_COLS : (e + count) * LIST_COLS]
 
-        def gather_words(e0, a, tag=None):
-            words = tile([P, HALF * C], U32, "slot_words%d_%d" % (e0, a), tag)
-            nc.vector.tensor_copy(words[:], token_words[a][:].bitcast(U32).indirect(slots_of(e0, HALF)))
+        def gather_words(e0, a, words=None):
+            if words is None:
+                words = tile([P, HALF * C], U32, "slot_words%d_%d" % (e0, a))[:]
+            nc.vector.tensor_copy(words, token_words[a][:].bitcast(U32).indirect(slots_of(e0, HALF)))
+            whole.append(words)
             for e in range(e0, e0 + HALF):
                 slot_words[e, a] = words[:, (e - e0) * C : (e - e0 + 1) * C]
 
-        def gather_scales(e0):
-            scales = tile([P, HALF * C], U8, "slot_scales%d" % e0)
+        def gather_scales(e0, tag=None):
+            scales = tile([P, HALF * C], U8, "slot_scales%d" % e0, tag)
             nc.vector.tensor_copy(scales[:], token_scales[:].bitcast(U8).indirect(slots_of(e0, HALF)))
+            whole.append(scales)
             for e in range(e0, e0 + HALF):
                 for a in range(PASSES):
                     slot_scales[e, a] = scales[4 * a : P, (e - e0) * C : (e - e0 + 1) * C]
 
-        def pool_tiles(step):
-            e, a = divmod(step, PASSES)
-            if e >= POOL_FROM:
-                return [1,4,0][a]
-            return {3: 1}.get(step, 0)
-
         def round_weights(step):
             e, a = divmod(step, PASSES)
-            if a < PASSES - 1:
-                w_bf = w_pair[(e + a) % 2][:]
-            elif step in LATE.values():
-                w_bf = tile([P, N * PACK], BF16, "w_bf", "late%d" % step)[:]
+            if a == 0:
+                w_bf = w_ends[(e + 1) % 2][:, : N * PACK]
+            elif a == 1:
+                w_bf = w_middle[:]
             else:
-                w_bf = tile([P, N * PACK], BF16, "w_bf", "w_bf%d" % (a // 2 + 2 * (e % 2)))[:]
+                w_bf = w_ends[e % 2][:, (PACK - 1) * QUARTER :]
             rounded[step] = w_bf
             dst = w_bf.rearrange("p (j u i r) -> p u j r i", j=PACK, i=RUN, r=PACK)
             src = raw[step][:].rearrange("p r (u j i) -> p u j r i", j=PACK, i=RUN)
+            pool = POOL_TILES.get(step, 0)
             if step == 0:
                 for j in range(PACK):
                     nc.scalar.activation(dst[:, :, j], src[:, :, j], COPY)
-            elif pool_tiles(step):
-                for j in range(pool_tiles(step)):
-                    nc.gpsimd.tensor_scalar(dst[:, :, j], src[:, :, j], 1.0, 0.0, MULT, ADD)
-                if pool_tiles(step) < PACK:
-                    nc.scalar.copy(out=dst[:, :, pool_tiles(step) :], in_=src[:, :, pool_tiles(step) :])
-            elif step in [4]:
-                nc.vector.tensor_copy(out=dst, in_=src)
-            elif step in SPLIT:
-                nc.scalar.copy(out=dst[:, : GROUPS // 2], in_=src[:, : GROUPS // 2])
-                nc.vector.tensor_copy(out=dst[:, GROUPS // 2 :], in_=src[:, GROUPS // 2 :])
-            elif step == LAST:
+            elif a == PASSES - 1:
                 nc.scalar.copy(out=dst[:, : GROUPS // 2], in_=src[:, : GROUPS // 2])
                 nc.scalar.copy(out=dst[:, GROUPS // 2 :], in_=src[:, GROUPS // 2 :])
             else:
-                nc.scalar.copy(out=dst, in_=src)
+                for j in range(PACK - pool, PACK):
+                    nc.gpsimd.tensor_scalar(dst[:, :, j], src[:, :, j], 1.0, 0.0, MULT, ADD)
+                if a == 1 and e > 0:
+                    nc.gpsimd.tensor_scalar(dst[:, :SHARE, 0], src[:, :SHARE, 0], 1.0, 0.0, MULT, ADD)
+                    nc.scalar.copy(out=dst[:, SHARE:, 0], in_=src[:, SHARE:, 0])
+                elif pool < PACK:
+                    nc.scalar.copy(out=dst[:, :, : PACK - pool], in_=src[:, :, : PACK - pool])
 
-        def multiply(step, tag=None):
+        codes, added = {}, {}
+
+        def quantise(step, tiles, scales=None):
+            ring = "%d_%d" % (step % CODE_BUFS, tiles[0])
+            w_codes = tile([P, len(tiles) * P], U32, "w_codes", "w_codes" + ring)
+            w_scales = scales if scales is not None else tile([P, len(tiles) * P], U8, "w_scales", "w_scales" + ring)[:]
+            values = rounded[step][:, tiles[0] * QUARTER : (tiles[-1] + 1) * QUARTER]
+            nc.vector.quantize_mx(out=w_codes[:].bitcast(FP8X4), scales=w_scales, in_=values)
+            for place, j in enumerate(tiles):
+                cols = slice(place * P, (place + 1) * P)
+                codes[step, j] = (w_codes[:, cols], w_scales[:, cols])
+
+        def open_sums(e):
+            sums[e] = [
+                banks.tile([P, 2 * C], F32, name="sum_bank%d" % ((PACK * e + j) % SUM_BANKS)) for j in range(PACK)
+            ]
+            for h in range(C // P):
+                column = slot_gate[:, e * C // P + h : e * C // P + h + 1]
+                nc.tensor.transpose(
+                    sums[e][3][:, C + h * P : C + (h + 1) * P], column.to_broadcast([P, P]), identity[:]
+                )
+
+        def multiply(step, tiles):
             e, a = divmod(step, PASSES)
-            w_codes = tile([P, N], U32, "w_codes", tag or "w_codes%d" % (step % CODE_BUFS))
-            w_scales = tile([P, N], U8, "w_scales", "w_scales%d" % (step % CODE_BUFS))
-            nc.vector.quantize_mx(out=w_codes[:].bitcast(FP8X4), scales=w_scales[:], in_=rounded[step])
-            if a == 0:
-                sums[e] = [
-                    banks.tile([P, 2 * C], F32, name="sum_bank%d" % ((PACK * e + j) % SUM_BANKS)) for j in range(PACK)
-                ]
-                for h in range(C // P):
-                    column = slot_gate[:, e * C // P + h : e * C // P + h + 1]
-                    nc.tensor.transpose(
-                        sums[e][3][:, C + h * P : C + (h + 1) * P], column.to_broadcast([P, P]), identity[:]
-                    )
-            for j in range(PACK):
-                cols = slice(j * P, (j + 1) * P)
+            for j in tiles:
+                w_codes, w_scales = codes[step, j]
+                added[e, j] = added.get((e, j), 0) + 1
                 nc.tensor.matmul_mx(
                     out=sums[e][j][:, :C],
-                    lhsT=w_codes[:, cols].bitcast(FP8X4),
-                    lhsT_scale=w_scales[:, cols],
+                    lhsT=w_codes.bitcast(FP8X4),
+                    lhsT_scale=w_scales,
                     rhs=slot_words[e, a].bitcast(FP8X4),
                     rhs_scale=slot_scales[e, a],
-                    start=(a == 0),
-                    stop=(a == PASSES - 1),
+                    start=(added[e, j] == 1),
+                    stop=(added[e, j] == PASSES),
                 )
 
         def quantise_wp():
@@ -209,13 +214,32 @@ def tile_moe_nxt_lin_bias_kernel(tc, x_words, x_scales, w, b, wp, gate, offs, ou
             )
             nc.vector.quantize_mx(out=wp_codes[:].bitcast(FP8X4), scales=wp_scales[:], in_=wp_bf[:])
 
-        def add_bias(e, y):
+        def add_bias(e, y, on_scalar=PACK):
             biased[e] = y
             for j in range(PACK):
-                nc.scalar.activation(biased[e][:, j, :], sums[e][j][:, :C], IDENTITY, bias=bias[:, j * RUN * E + e : j * RUN * E + e + 1])
+                column = expert_bias[e][:, j : j + 1]
+                if j < on_scalar:
+                    nc.scalar.activation(y[:, j, :], sums[e][j][:, :C], IDENTITY, bias=column)
+                else:
+                    nc.vector.tensor_scalar(y[:, j, :], sums[e][j][:, :C], column, None, ADD)
 
-        def project(e):
+        def warm_up(e):
+            w_codes, w_scales = codes[PASSES * e - 1, 0]
+            for turn in range(4):
+                unread = banks.tile([P, 2 * C], F32, name="sum_bank%d" % ((PACK * (e - 1) + 0) % SUM_BANKS))
+                nc.tensor.matmul_mx(
+                    out=unread[:],
+                    lhsT=w_codes.bitcast(FP8X4),
+                    lhsT_scale=w_scales,
+                    rhs=gathered_words[:, : 2 * C].bitcast(FP8X4),
+                    rhs_scale=gathered_scales[:, : 2 * C],
+                    start=True,
+                    stop=True,
+                )
+
+        def apply_gate(e):
             c_bf = tile([P, C * PACK], BF16, "c_bf", "c_bf%d" % (e % 2))
+            gated[e] = c_bf
             slot_gates = sums[e][3][:, C:].rearrange("p (s i) -> p s i", i=PAIR)
             nc.vector.tensor_tensor(
                 c_bf[:].rearrange("p (s i j) -> p s j i", i=PAIR, j=PACK),
@@ -223,9 +247,11 @@ def tile_moe_nxt_lin_bias_kernel(tc, x_words, x_scales, w, b, wp, gate, offs, ou
                 slot_gates.unsqueeze(2).to_broadcast([P, C // PAIR, PACK, PAIR]),
                 MULT,
             )
+
+        def project(e):
             c_codes = tile([P, C], U32, "c_codes", "c_codes%d" % (e % 2))
             c_scales = tile([P, C], U8, "c_scales", "c_scales%d" % (e % 2))
-            nc.vector.quantize_mx(out=c_codes[:].bitcast(FP8X4), scales=c_scales[:], in_=c_bf[:])
+            nc.vector.quantize_mx(out=c_codes[:].bitcast(FP8X4), scales=c_scales[:], in_=gated[e][:])
             projected[e] = [banks.tile([P, C], F32, name="out_bank%d" % m) for m in range(OUT_TILES)]
             for m in range(OUT_TILES):
                 cols = slice(m * P, (m + 1) * P)
@@ -243,36 +269,57 @@ def tile_moe_nxt_lin_bias_kernel(tc, x_words, x_scales, w, b, wp, gate, offs, ou
             nc.scalar.copy(out=staged, in_=projected[e][m][:])
             nc.vector.tensor_copy(result[m][:].indirect(slots_of(e)), staged)
 
-        for a in range(PASSES):
-            gather_words(0, a)
-            if a not in LATE:
-                gather_words(HALF, a)
+        gather_words(0, 0)
+        gathered_words = whole[0]
+        gather_words(HALF, 0)
         gather_scales(0)
+        gathered_scales = whole[-1]
         gather_scales(HALF)
+        gather_words(0, 1)
+        gather_words(0, 2)
         for e in range(E):
             first, middle, last = range(PASSES * e, PASSES * (e + 1))
             round_weights(first)
             if e > 0:
                 add_bias(e - 1, tile([P, PACK, C], F32, "y")[:])
-            if e == 1:
-                quantise_wp()
-            if e > 0:
+                apply_gate(e - 1)
+                if e == E - 1:
+                    warm_up(e)
+                quantise(first, HIGH, tile([P, 2 * P], U8, "early_scales", "expert_bias%d" % (e - 1))[:])
+                if e == 1:
+                    quantise_wp()
                 project(e - 1)
-            multiply(first, "y" if e >= 1 else None)
+                late_scales = tile([P, 2 * P + N], U8, "late_scales", "y")
+                quantise(first, LOW, late_scales[:, : 2 * P])
+                open_sums(e)
+                multiply(first, LOW)
+            else:
+                quantise(first, ALL)
+                open_sums(e)
+                multiply(first, ALL)
             round_weights(middle)
-            multiply(middle)
+            quantise(middle, ALL, late_scales[:, 2 * P :] if e > 0 else None)
+            multiply(middle, ALL)
+            if e > 0:
+                multiply(first, HIGH)
             round_weights(last)
-            multiply(last)
-            for a in LATE:
-                if LATE[a] // PASSES == e:
-                    gather_words(HALF, a, "late%d" % LATE[a] if a == PASSES - 1 else slot(last))
-            for m in range(OUT_TILES if e < E - 1 else 2):
+            quantise(last, ALL)
+            multiply(last, ALL)
+            if e == 0:
+                held_words = tile([P, 2, HALF * C], U32, "held_words", slot(last))
+                for a in range(1, PASSES):
+                    gather_words(HALF, a, held_words[:, a - 1, :])
+            for m in range(OUT_TILES if e < E - 1 else 1):
                 if e > 0:
-                    scatter(e - 1, m, raw[last][:, m, :C])
+                    scatter(e - 1, m, raw[last][:, m, C:] if last == LAST else raw[last][:, m, :C])
             for step in range(first + RAW_BUFS, min(last + RAW_BUFS + 1, STEPS)):
                 load_weights(step)
-        add_bias(E - 1, raw[LAST][:, :, C:])
+        add_bias(E - 1, tile([P, PACK, C], F32, "y_last")[:], PACK - 1)
+        apply_gate(E - 1)
+        held = tile([P, C], F32, "held", "expert_bias%d" % (E - 1))
+        nc.vector.tensor_copy(out=held[:], in_=projected[E - 2][1][:])
         project(E - 1)
+        nc.vector.tensor_copy(result[1][:].indirect(slots_of(E - 2)), held[:])
         staged_last = tile([P, OUT_TILES, C], F32, "staged_last")
         for m in range(OUT_TILES):
             scatter(E - 1, m, staged_last[:, m, :])

@@ -41,7 +41,7 @@ RAW_BUFS = 16
 CODE_BUFS = 4
 SUM_BANKS = 6
 POOL_TILES = {3: 1, 4: 3, 6: 1, 7: 3, 9: 1, 10: 3, 12: 1, 13: 3, 15: 1, 16: 3}
-ORDER = ["x0", "g", "w", "b", "x1", "w", "x2", "w", "w", "p", "w"]
+ORDER = ["x0", "x1", "w", "g", "w", "w", "x2", "p", "w", "b"]
 
 
 def tile_moe_nxt_lin_bias_kernel(tc, x_words, x_scales, w, b, wp, gate, offs, out):
@@ -97,9 +97,7 @@ def tile_moe_nxt_lin_bias_kernel(tc, x_words, x_scales, w, b, wp, gate, offs, ou
                 for i in range(RUN):
                     nc.sync.dma_start(out=bias[i:P:RUN, :], in_=b_groups[:, i * E : i * E + bias_run])
             elif item == "g":
-                gate_chunks = gate[0].rearrange("(c s) -> c s", s=P)
-                nc.sync.dma_start(out=gate_rows[:8, :], in_=gate_chunks[:8])
-                nc.sync.dma_start(out=gate_rows[8:12, :], in_=gate_chunks[8:])
+                nc.sync.dma_start(out=gate_rows[: T // P, :], in_=gate[0].rearrange("(c s) -> c s", s=P))
             elif item == "p":
                 for j in range(PACK):
                     nc.sync.dma_start(out=wp_raw[:, j, :], in_=wp_rows[j])

@@ -221,20 +221,6 @@ def tile_moe_nxt_lin_bias_kernel(tc, x_words, x_scales, w, b, wp, gate, offs, ou
                 else:
                     nc.vector.tensor_scalar(y[:, j, :], sums[e][j][:, :C], column, None, ADD)
 
-        def warm_up(e):
-            w_codes, w_scales = codes[PASSES * e - 1, 0]
-            for turn in range(4):
-                unread = banks.tile([P, 2 * C], F32, name="sum_bank%d" % ((PACK * (e - 1) + 0) % SUM_BANKS))
-                nc.tensor.matmul_mx(
-                    out=unread[:],
-                    lhsT=w_codes.bitcast(FP8X4),
-                    lhsT_scale=w_scales,
-                    rhs=gathered_words[:, : 2 * C].bitcast(FP8X4),
-                    rhs_scale=gathered_scales[:, : 2 * C],
-                    start=True,
-                    stop=True,
-                )
-
         def apply_gate(e):
             c_bf = tile([P, C * PACK], BF16, "c_bf", "c_bf%d" % (e % 2))
             gated[e] = c_bf
@@ -268,10 +254,8 @@ def tile_moe_nxt_lin_bias_kernel(tc, x_words, x_scales, w, b, wp, gate, offs, ou
             nc.vector.tensor_copy(result[m][:].indirect(slots_of(e)), staged)
 
         gather_words(0, 0)
-        gathered_words = whole[0]
         gather_words(HALF, 0)
         gather_scales(0)
-        gathered_scales = whole[-1]
         gather_scales(HALF)
         gather_words(0, 1)
         gather_words(0, 2)
@@ -281,8 +265,6 @@ def tile_moe_nxt_lin_bias_kernel(tc, x_words, x_scales, w, b, wp, gate, offs, ou
             if e > 0:
                 add_bias(e - 1, tile([P, PACK, C], F32, "y")[:])
                 apply_gate(e - 1)
-                if e == E - 1:
-                    warm_up(e)
                 quantise(first, HIGH, tile([P, 2 * P], U8, "early_scales", "expert_bias%d" % (e - 1))[:])
                 if e == 1:
                     quantise_wp()

@@ -6,7 +6,7 @@ from concourse.masks import make_identity
 K, T, E, C, N, M = 1536, 1536, 6, 256, 512, 256
 P = 128
 FLOPS = 2 * K * N * E * C + 2 * N * M * T
-BYTES = K * T + K * T // 32 + 4 * (E * K * N + N * E + N * M + P * E * C + M * T) + 2 * P * (T // 16)
+BYTES = K * T + K * T // 32 + 4 * (E * K * N + N * E + N * M + E * C + M * T) + 2 * P * (T // 16)
 
 F32 = mybir.dt.float32
 BF16 = mybir.dt.bfloat16
@@ -26,22 +26,21 @@ PAIR = 2
 KP = P * PACK
 PASSES = K // KP
 STEPS = E * PASSES
-LAST = STEPS - 1
 GROUPS = N // (PACK * RUN)
 QUADRANTS = P // 32
+SCALE_ROWS = 4
 OUT_TILES = M // P
 LIST_COLS = C // 16
 HALF = E // 2
-
-
 QUARTER = P * PACK
-LOW, HIGH, ALL = [0, 1], [2, 3], [0, 1, 2, 3]
-SHARE = 16
+ALL_SLOTS = slice(0, C)
+LOW, HIGH = [0, 1], [2, 3]
+SLOT_HALVES = [slice(0, C // 2), slice(C // 2, C)]
 RAW_BUFS = 16
 CODE_BUFS = 4
 SUM_BANKS = 6
-POOL_TILES = {3: 1, 4: 3, 6: 1, 7: 3, 9: 1, 10: 3, 12: 1, 13: 3, 15: 1, 16: 3}
-ORDER = ["x0", "x1", "w", "g", "w", "w", "x2", "p", "w", "b"]
+POOL_TILES = 2
+POOL_GROUPS = GROUPS // 2
 
 
 def tile_moe_nxt_lin_bias_kernel(tc, x_words, x_scales, w, b, wp, gate, offs, out):
@@ -53,8 +52,8 @@ def tile_moe_nxt_lin_bias_kernel(tc, x_words, x_scales, w, b, wp, gate, offs, ou
         def tile(shape, dtype, name, tag=None):
             return keep.tile(shape, dtype, name=name, tag=tag or name, align_bytes=64)
 
-        def slot(step):
-            return "slot%d" % (step % RAW_BUFS)
+        def raw_tag(step):
+            return "raw%d" % (step % RAW_BUFS)
 
         offsets = keep.tile([P, T // 16], U16, name="offsets")
         nc.sync.dma_start(offsets[:], offs)
@@ -65,114 +64,112 @@ def tile_moe_nxt_lin_bias_kernel(tc, x_words, x_scales, w, b, wp, gate, offs, ou
         nc.vector.memset(token_scales[:], 0)
         for q in range(QUADRANTS):
             nc.gpsimd.dma_start(
-                out=token_scales[32 * q : 32 * q + 4 * PASSES, :],
-                in_=x_scales[:, 4 * q : 4 * q + 4, :].bitcast(I32),
+                out=token_scales[32 * q : 32 * q + SCALE_ROWS * PASSES, :],
+                in_=x_scales[:, SCALE_ROWS * q : SCALE_ROWS * (q + 1), :].bitcast(I32),
             )
-        bias_run = ((PACK - 1) * RUN + 1) * E
-        bias = tile([P, bias_run], F32, "bias")
-        token_words = [tile([P, T], I32, "token_words%d" % a) for a in range(PASSES)]
         identity = tile([P, P], F32, "identity")
         make_identity(nc, identity[:])
-        wp_raw = tile([P, PACK, M], F32, "wp_raw")
-        result = [tile([P, T], F32, "result%d" % m) for m in range(OUT_TILES)]
 
-        b_groups = b.rearrange("(u x) e -> u (x e)", x=PACK * RUN)
-        wp_rows = wp.rearrange("(u j i) f -> j u i f", j=PACK, i=RUN)
-
+        token_words = [tile([P, T], I32, "token_words%d" % a) for a in range(PASSES)]
         raw = {}
+
+        def load_tokens(a):
+            nc.sync.dma_start(out=token_words[a][:], in_=x_words[a].rearrange("p t r -> p (t r)").bitcast(I32))
 
         def load_weights(step):
             e, a = divmod(step, PASSES)
-            rows = w[e, a * KP : (a + 1) * KP, :].rearrange("(p r) n -> p r n", r=PACK)
-            raw[step] = tile([P, PACK, N], F32, "raw", slot(step))
-            parts = 2 if step == LAST else 1
-            for h in range(parts):
-                cols = slice(h * N // parts, (h + 1) * N // parts)
-                nc.sync.dma_start(out=raw[step][:, :, cols], in_=rows[:, :, cols])
+            raw[step] = tile([P, PACK, N], F32, "raw", raw_tag(step))
+            nc.sync.dma_start(
+                out=raw[step][:], in_=w[e, a * KP : (a + 1) * KP, :].rearrange("(p r) n -> p r n", r=PACK)
+            )
 
-        for item in ORDER + ["w"] * (RAW_BUFS - len([item for item in ORDER if item == "w"])):
-            if item == "w":
-                load_weights(len(raw))
-            elif item == "b":
-                for i in range(RUN):
-                    nc.sync.dma_start(out=bias[i:P:RUN, :], in_=b_groups[:, i * E : i * E + bias_run])
-            elif item == "g":
-                nc.sync.dma_start(out=gate_rows[: T // P, :], in_=gate[0].rearrange("(c s) -> c s", s=P))
-            elif item == "p":
-                for j in range(PACK):
-                    nc.sync.dma_start(out=wp_raw[:, j, :], in_=wp_rows[j])
-            else:
-                a = int(item[-1])
-                nc.sync.dma_start(out=token_words[a][:], in_=x_words[a].rearrange("p t r -> p (t r)").bitcast(I32))
+        load_tokens(0)
+        load_tokens(1)
+        load_weights(0)
+        nc.sync.dma_start(out=gate_rows[: T // P, :], in_=gate[0].rearrange("(c s) -> c s", s=P))
+        load_weights(1)
+        load_weights(2)
+        load_tokens(2)
+        wp_raw = tile([P, PACK, M], F32, "wp_raw")
+        wp_rows = wp.rearrange("(u j i) f -> j u i f", j=PACK, i=RUN)
+        for j in range(PACK):
+            nc.sync.dma_start(out=wp_raw[:, j, :], in_=wp_rows[j])
+        load_weights(PASSES)
+        bias_run = ((PACK - 1) * RUN + 1) * E
+        bias = tile([P, bias_run], F32, "bias")
+        b_groups = b.rearrange("(u x) e -> u (x e)", x=PACK * RUN)
+        for i in range(RUN):
+            nc.sync.dma_start(out=bias[i:P:RUN, :], in_=b_groups[:, i * E : i * E + bias_run])
+        for step in range(PASSES + 1, RAW_BUFS):
+            load_weights(step)
 
         turned = banks.tile([P, C], F32, name="out_bank0")
         nc.tensor.transpose(turned[:, :P], gate_rows[:], identity[:])
         slot_gate = tile([P, T // P], F32, "slot_gate")
         nc.scalar.copy(out=slot_gate[:], in_=turned[:, : T // P])
-        expert_bias = [tile([P, PACK], F32, "expert_bias%d" % e) for e in range(E)]
-        for e in range(E):
-            nc.scalar.copy(out=expert_bias[e][:], in_=bias[:, e : bias_run : RUN * E])
 
+        def bias_columns(e, name):
+            columns = tile([P, PACK], F32, name)
+            nc.scalar.copy(out=columns[:], in_=bias[:, e : bias_run : RUN * E])
+            return columns
+
+        expert_bias = [bias_columns(e, "expert_bias%d" % e) for e in range(E)]
+        early_bias = bias_columns(E - 1, "early_bias")
+
+        result = [tile([P, T], F32, "result%d" % m) for m in range(OUT_TILES)]
         wp_codes = tile([P, M], U32, "wp_codes")
         wp_scales = tile([P, M], U8, "wp_scales")
-        w_ends = [tile([P, (2 * PACK - 1) * QUARTER], BF16, "w_ends%d" % h) for h in range(2)]
+        w_ends = [tile([P, (2 * PACK - POOL_TILES) * QUARTER], BF16, "w_ends%d" % h) for h in range(2)]
         w_middle = tile([P, N * PACK], BF16, "w_middle")
-        slot_words, slot_scales, sums, biased, projected, rounded, gated = {}, {}, {}, {}, {}, {}, {}
-
-        whole = []
+        slot_words, slot_scales, rounded, codes = {}, {}, {}, {}
+        sums, gates, projected = {}, {}, {}
 
         def slots_of(e, count=1):
             return offsets[:, e * LIST_COLS : (e + count) * LIST_COLS]
 
-        def gather_words(e0, a, words=None):
-            if words is None:
-                words = tile([P, HALF * C], U32, "slot_words%d_%d" % (e0, a))[:]
+        def gather_words(e0, a, words):
             nc.vector.tensor_copy(words, token_words[a][:].bitcast(U32).indirect(slots_of(e0, HALF)))
-            whole.append(words)
             for e in range(e0, e0 + HALF):
                 slot_words[e, a] = words[:, (e - e0) * C : (e - e0 + 1) * C]
 
-        def gather_scales(e0, tag=None):
-            scales = tile([P, HALF * C], U8, "slot_scales%d" % e0, tag)
+        def gather_scales(e0):
+            scales = tile([P, HALF * C], U8, "slot_scales%d" % e0)
             nc.vector.tensor_copy(scales[:], token_scales[:].bitcast(U8).indirect(slots_of(e0, HALF)))
-            whole.append(scales)
             for e in range(e0, e0 + HALF):
                 for a in range(PASSES):
-                    slot_scales[e, a] = scales[4 * a : P, (e - e0) * C : (e - e0 + 1) * C]
+                    slot_scales[e, a] = scales[SCALE_ROWS * a : P, (e - e0) * C : (e - e0 + 1) * C]
 
         def round_weights(step):
             e, a = divmod(step, PASSES)
             if a == 0:
                 w_bf = w_ends[(e + 1) % 2][:, : N * PACK]
-            elif a == 1:
+            elif a < PASSES - 1:
                 w_bf = w_middle[:]
             else:
-                w_bf = w_ends[e % 2][:, (PACK - 1) * QUARTER :]
+                w_bf = w_ends[e % 2][:, (PACK - POOL_TILES) * QUARTER :]
             rounded[step] = w_bf
             dst = w_bf.rearrange("p (j u i r) -> p u j r i", j=PACK, i=RUN, r=PACK)
             src = raw[step][:].rearrange("p r (u j i) -> p u j r i", j=PACK, i=RUN)
-            pool = POOL_TILES.get(step, 0)
             if step == 0:
                 for j in range(PACK):
                     nc.scalar.activation(dst[:, :, j], src[:, :, j], COPY)
-            elif a == PASSES - 1:
-                nc.scalar.copy(out=dst[:, : GROUPS // 2], in_=src[:, : GROUPS // 2])
-                nc.scalar.copy(out=dst[:, GROUPS // 2 :], in_=src[:, GROUPS // 2 :])
-            else:
-                for j in range(PACK - pool, PACK):
+            elif a < PASSES - 1:
+                on_scalar = PACK - POOL_TILES if e > 0 else PACK
+                for j in range(on_scalar, PACK):
                     nc.gpsimd.tensor_scalar(dst[:, :, j], src[:, :, j], 1.0, 0.0, MULT, ADD)
-                if a == 1 and e > 0:
-                    nc.gpsimd.tensor_scalar(dst[:, :SHARE, 0], src[:, :SHARE, 0], 1.0, 0.0, MULT, ADD)
-                    nc.scalar.copy(out=dst[:, SHARE:, 0], in_=src[:, SHARE:, 0])
-                elif pool < PACK:
-                    nc.scalar.copy(out=dst[:, :, : PACK - pool], in_=src[:, :, : PACK - pool])
+                nc.scalar.copy(out=dst[:, :, :on_scalar], in_=src[:, :, :on_scalar])
+            else:
+                on_scalar = PACK - 1 if e > 0 else PACK
+                for j in range(on_scalar, PACK):
+                    nc.gpsimd.tensor_scalar(dst[:, :POOL_GROUPS, j], src[:, :POOL_GROUPS, j], 1.0, 0.0, MULT, ADD)
+                nc.scalar.copy(out=dst[:, :POOL_GROUPS, :on_scalar], in_=src[:, :POOL_GROUPS, :on_scalar])
+                nc.scalar.copy(out=dst[:, POOL_GROUPS:], in_=src[:, POOL_GROUPS:])
 
-        codes, added = {}, {}
-
-        def quantise(step, tiles, scales=None):
+        def quantise(step, tiles, w_scales=None):
             ring = "%d_%d" % (step % CODE_BUFS, tiles[0])
             w_codes = tile([P, len(tiles) * P], U32, "w_codes", "w_codes" + ring)
-            w_scales = scales if scales is not None else tile([P, len(tiles) * P], U8, "w_scales", "w_scales" + ring)[:]
+            if w_scales is None:
+                w_scales = tile([P, len(tiles) * P], U8, "w_scales", "w_scales" + ring)[:]
             values = rounded[step][:, tiles[0] * QUARTER : (tiles[-1] + 1) * QUARTER]
             nc.vector.quantize_mx(out=w_codes[:].bitcast(FP8X4), scales=w_scales, in_=values)
             for place, j in enumerate(tiles):
@@ -183,126 +180,156 @@ def tile_moe_nxt_lin_bias_kernel(tc, x_words, x_scales, w, b, wp, gate, offs, ou
             sums[e] = [
                 banks.tile([P, 2 * C], F32, name="sum_bank%d" % ((PACK * e + j) % SUM_BANKS)) for j in range(PACK)
             ]
+            if e < E - 1:
+                gates[e] = sums[e][PACK - 1][:, C:]
+            else:
+                gates[e] = banks.tile([P, C], F32, name="sum_bank0")[:]
             for h in range(C // P):
                 column = slot_gate[:, e * C // P + h : e * C // P + h + 1]
-                nc.tensor.transpose(
-                    sums[e][3][:, C + h * P : C + (h + 1) * P], column.to_broadcast([P, P]), identity[:]
-                )
+                nc.tensor.transpose(gates[e][:, h * P : (h + 1) * P], column.to_broadcast([P, P]), identity[:])
 
         def multiply(step, tiles):
             e, a = divmod(step, PASSES)
             for j in tiles:
                 w_codes, w_scales = codes[step, j]
-                added[e, j] = added.get((e, j), 0) + 1
                 nc.tensor.matmul_mx(
                     out=sums[e][j][:, :C],
                     lhsT=w_codes.bitcast(FP8X4),
                     lhsT_scale=w_scales,
                     rhs=slot_words[e, a].bitcast(FP8X4),
                     rhs_scale=slot_scales[e, a],
-                    start=(added[e, j] == 1),
-                    stop=(added[e, j] == PASSES),
+                    start=(a == 0),
+                    stop=(a == PASSES - 1),
                 )
 
         def quantise_wp():
             wp_bf = tile([P, M * PACK], BF16, "wp_bf")
             nc.scalar.copy(
-                out=wp_bf[:].rearrange("p (f i j) -> p f j i", i=RUN, j=PACK),
-                in_=wp_raw[:].rearrange("p j (f i) -> p f j i", i=RUN),
+                out=wp_bf[:].rearrange("p (f i j) -> p f j i", i=PAIR, j=PACK),
+                in_=wp_raw[:].rearrange("p j (f i) -> p f j i", i=PAIR),
             )
             nc.vector.quantize_mx(out=wp_codes[:].bitcast(FP8X4), scales=wp_scales[:], in_=wp_bf[:])
 
-        def add_bias(e, y, on_scalar=PACK):
-            biased[e] = y
-            for j in range(PACK):
-                column = expert_bias[e][:, j : j + 1]
-                if j < on_scalar:
-                    nc.scalar.activation(y[:, j, :], sums[e][j][:, :C], IDENTITY, bias=column)
-                else:
-                    nc.vector.tensor_scalar(y[:, j, :], sums[e][j][:, :C], column, None, ADD)
-
-        def apply_gate(e):
-            c_bf = tile([P, C * PACK], BF16, "c_bf", "c_bf%d" % (e % 2))
-            gated[e] = c_bf
-            slot_gates = sums[e][3][:, C:].rearrange("p (s i) -> p s i", i=PAIR)
+        def apply_gate(e, cols, y, c_bf):
+            slot_gates = gates[e][:, cols].rearrange("p (s i) -> p s i", i=PAIR)
             nc.vector.tensor_tensor(
-                c_bf[:].rearrange("p (s i j) -> p s j i", i=PAIR, j=PACK),
-                biased[e].rearrange("p j (s i) -> p s j i", i=PAIR),
-                slot_gates.unsqueeze(2).to_broadcast([P, C // PAIR, PACK, PAIR]),
+                c_bf[:, cols.start * PACK : cols.stop * PACK].rearrange("p (s i j) -> p s j i", i=PAIR, j=PACK),
+                y.rearrange("p j (s i) -> p s j i", i=PAIR),
+                slot_gates.unsqueeze(2).to_broadcast([P, (cols.stop - cols.start) // PAIR, PACK, PAIR]),
                 MULT,
             )
 
-        def project(e):
+        def quantise_c(cols, c_bf, c_codes, c_scales):
+            nc.vector.quantize_mx(
+                out=c_codes[:, cols].bitcast(FP8X4),
+                scales=c_scales[:, cols],
+                in_=c_bf[:, cols.start * PACK : cols.stop * PACK],
+            )
+
+        def project(m, bank, c_codes, c_scales):
+            rows = slice(m * P, (m + 1) * P)
+            nc.tensor.matmul_mx(
+                out=bank[:],
+                lhsT=wp_codes[:, rows].bitcast(FP8X4),
+                lhsT_scale=wp_scales[:, rows],
+                rhs=c_codes.bitcast(FP8X4),
+                rhs_scale=c_scales,
+                start=True,
+                stop=True,
+            )
+
+        def c_tiles(e, tag):
+            c_bf = tile([P, C * PACK], BF16, "c_bf", tag)
             c_codes = tile([P, C], U32, "c_codes", "c_codes%d" % (e % 2))
             c_scales = tile([P, C], U8, "c_scales", "c_scales%d" % (e % 2))
-            nc.vector.quantize_mx(out=c_codes[:].bitcast(FP8X4), scales=c_scales[:], in_=gated[e][:])
+            return c_bf, c_codes, c_scales
+
+        def bias_and_gate(e):
+            y = tile([P, PACK, C], F32, "y")
+            for j in range(PACK):
+                nc.scalar.activation(y[:, j, :], sums[e][j][:, :C], IDENTITY, bias=expert_bias[e][:, j : j + 1])
+            c_parts = c_tiles(e, "c_bf")
+            apply_gate(e, ALL_SLOTS, y[:], c_parts[0])
+            return c_parts
+
+        def project_all(e, c_bf, c_codes, c_scales):
+            quantise_c(ALL_SLOTS, c_bf, c_codes, c_scales)
             projected[e] = [banks.tile([P, C], F32, name="out_bank%d" % m) for m in range(OUT_TILES)]
             for m in range(OUT_TILES):
-                cols = slice(m * P, (m + 1) * P)
-                nc.tensor.matmul_mx(
-                    out=projected[e][m][:],
-                    lhsT=wp_codes[:, cols].bitcast(FP8X4),
-                    lhsT_scale=wp_scales[:, cols],
-                    rhs=c_codes[:].bitcast(FP8X4),
-                    rhs_scale=c_scales[:],
-                    start=True,
-                    stop=True,
-                )
+                project(m, projected[e][m], c_codes[:], c_scales[:])
 
         def scatter(e, m, staged):
-            nc.scalar.copy(out=staged, in_=projected[e][m][:])
             nc.vector.tensor_copy(result[m][:].indirect(slots_of(e)), staged)
 
-        gather_words(0, 0)
-        gather_words(HALF, 0)
-        gather_scales(0)
-        gather_scales(HALF)
-        gather_words(0, 1)
-        gather_words(0, 2)
+        everything = list(range(PACK))
+        for e0 in (0, HALF):
+            gather_words(e0, 0, tile([P, HALF * C], U32, "slot_words%d_0" % e0)[:])
+        for e0 in (0, HALF):
+            gather_scales(e0)
+        for a in range(1, PASSES):
+            gather_words(0, a, tile([P, HALF * C], U32, "slot_words0_%d" % a)[:])
         for e in range(E):
             first, middle, last = range(PASSES * e, PASSES * (e + 1))
             round_weights(first)
-            if e > 0:
-                add_bias(e - 1, tile([P, PACK, C], F32, "y")[:])
-                apply_gate(e - 1)
+            if e == 0:
+                middle_scales = None
+                quantise(first, everything)
+                open_sums(e)
+                multiply(first, everything)
+            else:
+                c_parts = bias_and_gate(e - 1)
                 quantise(first, HIGH, tile([P, 2 * P], U8, "early_scales", "expert_bias%d" % (e - 1))[:])
                 if e == 1:
                     quantise_wp()
-                project(e - 1)
-                late_scales = tile([P, 2 * P + N], U8, "late_scales", "y")
-                quantise(first, LOW, late_scales[:, : 2 * P])
+                project_all(e - 1, *c_parts)
+                planes = tile([P, 2 * P + N], U8, "late_scales", "y")
+                middle_scales = planes[:, 2 * P :]
+                quantise(first, LOW, planes[:, : 2 * P])
                 open_sums(e)
-                multiply(first, LOW)
-            else:
-                quantise(first, ALL)
-                open_sums(e)
-                multiply(first, ALL)
+                multiply(first, HIGH + LOW)
             round_weights(middle)
-            quantise(middle, ALL, late_scales[:, 2 * P :] if e > 0 else None)
-            multiply(middle, ALL)
-            if e > 0:
-                multiply(first, HIGH)
+            quantise(middle, everything, middle_scales)
+            multiply(middle, everything)
             round_weights(last)
-            quantise(last, ALL)
-            multiply(last, ALL)
+            for tiles in [everything] if e < E - 1 else [LOW, HIGH]:
+                quantise(last, tiles)
+                multiply(last, tiles)
             if e == 0:
-                held_words = tile([P, 2, HALF * C], U32, "held_words", slot(last))
+                held_words = tile([P, PASSES - 1, HALF * C], U32, "held_words", raw_tag(last))
                 for a in range(1, PASSES):
                     gather_words(HALF, a, held_words[:, a - 1, :])
-            for m in range(OUT_TILES if e < E - 1 else 1):
-                if e > 0:
-                    scatter(e - 1, m, raw[last][:, m, C:] if last == LAST else raw[last][:, m, :C])
+            else:
+                for m in range(OUT_TILES if e < E - 1 else 1):
+                    nc.scalar.copy(out=raw[last][:, m, :C], in_=projected[e - 1][m][:])
+                    scatter(e - 1, m, raw[last][:, m, :C])
             for step in range(first + RAW_BUFS, min(last + RAW_BUFS + 1, STEPS)):
                 load_weights(step)
-        add_bias(E - 1, tile([P, PACK, C], F32, "y_last")[:], PACK - 1)
-        apply_gate(E - 1)
-        held = tile([P, C], F32, "held", "expert_bias%d" % (E - 1))
-        nc.vector.tensor_copy(out=held[:], in_=projected[E - 2][1][:])
-        project(E - 1)
-        nc.vector.tensor_copy(result[1][:].indirect(slots_of(E - 2)), held[:])
-        staged_last = tile([P, OUT_TILES, C], F32, "staged_last")
+
+        e = E - 1
+        c_bf, c_codes, c_scales = c_tiles(e, "wp_bf")
+        y_halves = []
+        for h, cols in enumerate(SLOT_HALVES):
+            y_halves.append(tile([P, PACK, C // 2], F32, "y_half", ("c_bf", "early_bias")[h]))
+            for j in range(PACK):
+                columns = early_bias if h == 0 and j < PACK - 1 else expert_bias[e]
+                nc.scalar.activation(y_halves[h][:, j, :], sums[e][j][:, cols], IDENTITY, bias=columns[:, j : j + 1])
+        for h, cols in enumerate(SLOT_HALVES):
+            apply_gate(e, cols, y_halves[h][:], c_bf)
+        for h, cols in enumerate(SLOT_HALVES):
+            if h == 1:
+                held = tile([P, C], F32, "held", "expert_bias%d" % e)
+                nc.vector.tensor_copy(out=held[:], in_=projected[e - 1][1][:])
+            quantise_c(cols, c_bf, c_codes, c_scales)
+            for m in range(OUT_TILES):
+                name = (("out_bank0", "sum_bank1"), ("sum_bank0", "out_bank1"))[h][m]
+                projected[e, h, m] = banks.tile([P, C // 2], F32, name=name)
+                project(m, projected[e, h, m], c_codes[:, cols], c_scales[:, cols])
+        scatter(e - 1, 1, held[:])
+        staged = tile([P, OUT_TILES, C], F32, "staged", "wp_raw")
         for m in range(OUT_TILES):
-            scatter(E - 1, m, staged_last[:, m, :])
+            for h, cols in enumerate(SLOT_HALVES):
+                nc.scalar.copy(out=staged[:, m, cols], in_=projected[e, h, m][:])
+            scatter(e, m, staged[:, m, :])
 
         for m in range(OUT_TILES):
             nc.sync.dma_start(out=out[m * P : (m + 1) * P, :], in_=result[m][:])

@@ -50,7 +50,7 @@ def tile_moe_nxt_lin_bias_kernel(tc, x_words, x_scales, w, b, wp, gate, offs, ou
         banks = ctx.enter_context(tc.psum_pool(name="banks", bufs=1))
 
         def tile(shape, dtype, name, tag=None):
-            return keep.tile(shape, dtype, name=name, tag=tag or name, align_bytes=64)
+            return keep.tile(shape, dtype, name=name, tag=tag or name, align_bytes=256)
 
         def raw_tag(step):
             return "raw%d" % (step % RAW_BUFS)
@@ -80,7 +80,8 @@ def tile_moe_nxt_lin_bias_kernel(tc, x_words, x_scales, w, b, wp, gate, offs, ou
             e, a = divmod(step, PASSES)
             raw[step] = tile([P, PACK, N], F32, "raw", raw_tag(step))
             nc.sync.dma_start(
-                out=raw[step][:], in_=w[e, a * KP : (a + 1) * KP, :].rearrange("(p r) n -> p r n", r=PACK)
+                out=raw[step][:].rearrange("p r n -> p (r n)"),
+                in_=w[e, a * KP : (a + 1) * KP, :].rearrange("(p r) n -> p (r n)", r=PACK),
             )
 
         load_tokens(0)

@@ -109,21 +109,20 @@ def tile_moe_nxt_lin_bias_kernel(tc, x_words, x_scales, w, b, wp, gate, offs, ou
         slot_gate = tile([P, T // P], F32, "slot_gate")
         nc.scalar.copy(out=slot_gate[:], in_=turned[:, : T // P])
 
-        def bias_columns(e, name):
-            columns = tile([P, PACK], F32, name)
-            nc.scalar.copy(out=columns[:], in_=bias[:, e : bias_run : RUN * E])
+        def bias_columns(e, name, count):
+            columns = tile([P, count], F32, name)
+            nc.scalar.copy(out=columns[:], in_=bias[:, e : bias_run : RUN * E][:, :count])
             return columns
 
-        expert_bias = [bias_columns(e, "expert_bias%d" % e) for e in range(E)]
-        early_bias = bias_columns(E - 1, "early_bias")
+        expert_bias = [bias_columns(e, "expert_bias%d" % e, PACK) for e in range(E)]
+        early_bias = bias_columns(E - 1, "early_bias", PACK - 1)
 
         result = [tile([P, T], F32, "result%d" % m) for m in range(OUT_TILES)]
         wp_codes = tile([P, M], U32, "wp_codes")
-        wp_scales = tile([P, M], U8, "wp_scales")
         w_ends = [tile([P, (2 * PACK - POOL_TILES) * QUARTER], BF16, "w_ends%d" % h) for h in range(2)]
         w_middle = tile([P, N * PACK], BF16, "w_middle")
         slot_words, slot_scales, rounded, codes = {}, {}, {}, {}
-        sums, gates, projected = {}, {}, {}
+        sums, gates, projected, early_scales = {}, {}, {}, {}
 
         def slots_of(e, count=1):
             return offsets[:, e * LIST_COLS : (e + count) * LIST_COLS]
@@ -203,13 +202,13 @@ def tile_moe_nxt_lin_bias_kernel(tc, x_words, x_scales, w, b, wp, gate, offs, ou
                     stop=(a == PASSES - 1),
                 )
 
-        def quantise_wp():
+        def quantise_wp(wp_scales):
             wp_bf = tile([P, M * PACK], BF16, "wp_bf")
             nc.scalar.copy(
                 out=wp_bf[:].rearrange("p (f i j) -> p f j i", i=PAIR, j=PACK),
                 in_=wp_raw[:].rearrange("p j (f i) -> p f j i", i=PAIR),
             )
-            nc.vector.quantize_mx(out=wp_codes[:].bitcast(FP8X4), scales=wp_scales[:], in_=wp_bf[:])
+            nc.vector.quantize_mx(out=wp_codes[:].bitcast(FP8X4), scales=wp_scales, in_=wp_bf[:])
 
         def apply_gate(e, cols, y, c_bf):
             slot_gates = gates[e][:, cols].rearrange("p (s i) -> p s i", i=PAIR)
@@ -232,7 +231,7 @@ def tile_moe_nxt_lin_bias_kernel(tc, x_words, x_scales, w, b, wp, gate, offs, ou
             nc.tensor.matmul_mx(
                 out=bank[:],
                 lhsT=wp_codes[:, rows].bitcast(FP8X4),
-                lhsT_scale=wp_scales[:, rows],
+                lhsT_scale=early_scales[1][:, 2 * P :][:, rows],
                 rhs=c_codes.bitcast(FP8X4),
                 rhs_scale=c_scales,
                 start=True,
@@ -279,9 +278,11 @@ def tile_moe_nxt_lin_bias_kernel(tc, x_words, x_scales, w, b, wp, gate, offs, ou
                 multiply(first, everything)
             else:
                 c_parts = bias_and_gate(e - 1)
-                quantise(first, HIGH, tile([P, 2 * P], U8, "early_scales", "expert_bias%d" % (e - 1))[:])
+                width = 2 * P + (M if e == 1 else 0)
+                early_scales[e] = tile([P, width], U8, "early_scales", "expert_bias%d" % (e - 1))
+                quantise(first, HIGH, early_scales[e][:, : 2 * P])
                 if e == 1:
-                    quantise_wp()
+                    quantise_wp(early_scales[e][:, 2 * P :])
                 project_all(e - 1, *c_parts)
                 planes = tile([P, 2 * P + N], U8, "late_scales", "y")
                 middle_scales = planes[:, 2 * P :]
@@ -307,7 +308,7 @@ def tile_moe_nxt_lin_bias_kernel(tc, x_words, x_scales, w, b, wp, gate, offs, ou
                 load_weights(step)
 
         e = E - 1
-        c_bf, c_codes, c_scales = c_tiles(e, "wp_bf")
+        c_parts = c_tiles(e, "wp_bf")
         y_halves = []
         for h, cols in enumerate(SLOT_HALVES):
             y_halves.append(tile([P, PACK, C // 2], F32, "y_half", ("c_bf", "early_bias")[h]))
@@ -315,21 +316,14 @@ def tile_moe_nxt_lin_bias_kernel(tc, x_words, x_scales, w, b, wp, gate, offs, ou
                 columns = early_bias if h == 0 and j < PACK - 1 else expert_bias[e]
                 nc.scalar.activation(y_halves[h][:, j, :], sums[e][j][:, cols], IDENTITY, bias=columns[:, j : j + 1])
         for h, cols in enumerate(SLOT_HALVES):
-            apply_gate(e, cols, y_halves[h][:], c_bf)
-        for h, cols in enumerate(SLOT_HALVES):
-            if h == 1:
-                held = tile([P, C], F32, "held", "expert_bias%d" % e)
-                nc.vector.tensor_copy(out=held[:], in_=projected[e - 1][1][:])
-            quantise_c(cols, c_bf, c_codes, c_scales)
-            for m in range(OUT_TILES):
-                name = (("out_bank0", "sum_bank1"), ("sum_bank0", "out_bank1"))[h][m]
-                projected[e, h, m] = banks.tile([P, C // 2], F32, name=name)
-                project(m, projected[e, h, m], c_codes[:, cols], c_scales[:, cols])
+            apply_gate(e, cols, y_halves[h][:], c_parts[0])
+        held = tile([P, C], F32, "held", "expert_bias%d" % e)
+        nc.vector.tensor_copy(out=held[:], in_=projected[e - 1][1][:])
+        project_all(e, *c_parts)
         scatter(e - 1, 1, held[:])
         staged = tile([P, OUT_TILES, C], F32, "staged", "wp_raw")
         for m in range(OUT_TILES):
-            for h, cols in enumerate(SLOT_HALVES):
-                nc.scalar.copy(out=staged[:, m, cols], in_=projected[e, h, m][:])
+            nc.scalar.copy(out=staged[:, m, :], in_=projected[e][m][:])
             scatter(e, m, staged[:, m, :])
 
         for m in range(OUT_TILES):

@@ -21,12 +21,10 @@ MULT = mybir.AluOpType.mult
 ADD = mybir.AluOpType.add
 
 PACK = 4
-RUN = 2
 PAIR = 2
 KP = P * PACK
 PASSES = K // KP
 STEPS = E * PASSES
-GROUPS = N // (PACK * RUN)
 QUADRANTS = P // 32
 SCALE_ROWS = 4
 OUT_TILES = M // P
@@ -36,11 +34,13 @@ QUARTER = P * PACK
 ALL_SLOTS = slice(0, C)
 LOW, HIGH = [0, 1], [2, 3]
 SLOT_HALVES = [slice(0, C // 2), slice(C // 2, C)]
+EARLY_SLOTS = 192
 RAW_BUFS = 16
 CODE_BUFS = 4
 SUM_BANKS = 6
 POOL_TILES = 2
-POOL_GROUPS = GROUPS // 2
+POOL_COLUMNS = P // 4
+LATE_COLUMNS = 80
 
 
 def tile_moe_nxt_lin_bias_kernel(tc, x_words, x_scales, w, b, wp, gate, offs, out):
@@ -92,15 +92,10 @@ def tile_moe_nxt_lin_bias_kernel(tc, x_words, x_scales, w, b, wp, gate, offs, ou
         load_weights(2)
         load_tokens(2)
         wp_raw = tile([P, PACK, M], F32, "wp_raw")
-        wp_rows = wp.rearrange("(u j i) f -> j u i f", j=PACK, i=RUN)
-        for j in range(PACK):
-            nc.sync.dma_start(out=wp_raw[:, j, :], in_=wp_rows[j])
+        nc.sync.dma_start(out=wp_raw[:].rearrange("p j f -> p (j f)"), in_=wp.rearrange("(p j) f -> p (j f)", j=PACK))
         load_weights(PASSES)
-        bias_run = ((PACK - 1) * RUN + 1) * E
-        bias = tile([P, bias_run], F32, "bias")
-        b_groups = b.rearrange("(u x) e -> u (x e)", x=PACK * RUN)
-        for i in range(RUN):
-            nc.sync.dma_start(out=bias[i:P:RUN, :], in_=b_groups[:, i * E : i * E + bias_run])
+        bias = tile([P, PACK * E], F32, "bias")
+        nc.sync.dma_start(out=bias[:], in_=b.rearrange("(p j) e -> p (j e)", j=PACK))
         for step in range(PASSES + 1, RAW_BUFS):
             load_weights(step)
 
@@ -109,13 +104,22 @@ def tile_moe_nxt_lin_bias_kernel(tc, x_words, x_scales, w, b, wp, gate, offs, ou
         slot_gate = tile([P, T // P], F32, "slot_gate")
         nc.scalar.copy(out=slot_gate[:], in_=turned[:, : T // P])
 
+        def spread_gates(e, bank):
+            for h in range(C // P):
+                column = slot_gate[:, e * C // P + h : e * C // P + h + 1]
+                nc.tensor.transpose(bank[:, h * P : (h + 1) * P], column.to_broadcast([P, P]), identity[:])
+
+        spread = banks.tile([P, C], F32, name="out_bank1")
+        spread_gates(E - 1, spread)
+        last_gates = tile([P, C], F32, "last_gates")
+        nc.scalar.copy(out=last_gates[:], in_=spread[:])
+
         def bias_columns(e, name, count):
             columns = tile([P, count], F32, name)
-            nc.scalar.copy(out=columns[:], in_=bias[:, e : bias_run : RUN * E][:, :count])
+            nc.scalar.copy(out=columns[:], in_=bias[:, e::E][:, :count])
             return columns
 
         expert_bias = [bias_columns(e, "expert_bias%d" % e, PACK) for e in range(E)]
-        early_bias = bias_columns(E - 1, "early_bias", PACK - 1)
 
         result = [tile([P, T], F32, "result%d" % m) for m in range(OUT_TILES)]
         wp_codes = tile([P, M], U32, "wp_codes")
@@ -139,6 +143,19 @@ def tile_moe_nxt_lin_bias_kernel(tc, x_words, x_scales, w, b, wp, gate, offs, ou
                 for a in range(PASSES):
                     slot_scales[e, a] = scales[SCALE_ROWS * a : P, (e - e0) * C : (e - e0 + 1) * C]
 
+        def pair_views(step, tiles, values, cols=slice(0, P)):
+            dst = values.rearrange("p (j c r) -> p c r j", j=len(tiles), r=PACK)
+            src = raw[step][:].rearrange("p r (c j) -> p c r j", j=PACK)
+            return dst[:, cols], src[:, cols, :, tiles[0] : tiles[-1] + 1]
+
+        def round_on_scalar(step, tiles, values, cols=slice(0, P)):
+            dst, src = pair_views(step, tiles, values, cols)
+            nc.scalar.copy(out=dst, in_=src)
+
+        def round_on_gpsimd(step, tiles, values, cols=slice(0, P)):
+            dst, src = pair_views(step, tiles, values, cols)
+            nc.gpsimd.tensor_scalar(dst, src, 1.0, 0.0, MULT, ADD)
+
         def round_weights(step):
             e, a = divmod(step, PASSES)
             if a == 0:
@@ -148,29 +165,29 @@ def tile_moe_nxt_lin_bias_kernel(tc, x_words, x_scales, w, b, wp, gate, offs, ou
             else:
                 w_bf = w_ends[e % 2][:, (PACK - POOL_TILES) * QUARTER :]
             rounded[step] = w_bf
-            dst = w_bf.rearrange("p (j u i r) -> p u j r i", j=PACK, i=RUN, r=PACK)
-            src = raw[step][:].rearrange("p r (u j i) -> p u j r i", j=PACK, i=RUN)
+            low, high = w_bf[:, : 2 * QUARTER], w_bf[:, 2 * QUARTER :]
             if step == 0:
-                for j in range(PACK):
-                    nc.scalar.activation(dst[:, :, j], src[:, :, j], COPY)
+                nc.scalar.activation(*pair_views(step, LOW, low), COPY)
+                nc.scalar.activation(*pair_views(step, HIGH, high), COPY)
+            elif e == 0:
+                round_on_scalar(step, LOW, low)
+                round_on_scalar(step, HIGH, high)
             elif a < PASSES - 1:
-                on_scalar = PACK - POOL_TILES if e > 0 else PACK
-                for j in range(on_scalar, PACK):
-                    nc.gpsimd.tensor_scalar(dst[:, :, j], src[:, :, j], 1.0, 0.0, MULT, ADD)
-                nc.scalar.copy(out=dst[:, :, :on_scalar], in_=src[:, :, :on_scalar])
+                round_on_gpsimd(step, HIGH, high)
+                round_on_scalar(step, LOW, low)
             else:
-                on_scalar = PACK - 1 if e > 0 else PACK
-                for j in range(on_scalar, PACK):
-                    nc.gpsimd.tensor_scalar(dst[:, :POOL_GROUPS, j], src[:, :POOL_GROUPS, j], 1.0, 0.0, MULT, ADD)
-                nc.scalar.copy(out=dst[:, :POOL_GROUPS, :on_scalar], in_=src[:, :POOL_GROUPS, :on_scalar])
-                nc.scalar.copy(out=dst[:, POOL_GROUPS:], in_=src[:, POOL_GROUPS:])
+                round_on_gpsimd(step, HIGH, high, slice(0, POOL_COLUMNS))
+                round_on_scalar(step, LOW, low, slice(0, P // 2))
+                round_on_scalar(step, HIGH, high, slice(POOL_COLUMNS, P))
+                round_on_scalar(step, LOW, low, slice(P // 2, P))
 
-        def quantise(step, tiles, w_scales=None):
+        def quantise(step, tiles, w_scales=None, values=None):
             ring = "%d_%d" % (step % CODE_BUFS, tiles[0])
             w_codes = tile([P, len(tiles) * P], U32, "w_codes", "w_codes" + ring)
             if w_scales is None:
                 w_scales = tile([P, len(tiles) * P], U8, "w_scales", "w_scales" + ring)[:]
-            values = rounded[step][:, tiles[0] * QUARTER : (tiles[-1] + 1) * QUARTER]
+            if values is None:
+                values = rounded[step][:, tiles[0] * QUARTER : (tiles[-1] + 1) * QUARTER]
             nc.vector.quantize_mx(out=w_codes[:].bitcast(FP8X4), scales=w_scales, in_=values)
             for place, j in enumerate(tiles):
                 cols = slice(place * P, (place + 1) * P)
@@ -182,11 +199,7 @@ def tile_moe_nxt_lin_bias_kernel(tc, x_words, x_scales, w, b, wp, gate, offs, ou
             ]
             if e < E - 1:
                 gates[e] = sums[e][PACK - 1][:, C:]
-            else:
-                gates[e] = banks.tile([P, C], F32, name="sum_bank0")[:]
-            for h in range(C // P):
-                column = slot_gate[:, e * C // P + h : e * C // P + h + 1]
-                nc.tensor.transpose(gates[e][:, h * P : (h + 1) * P], column.to_broadcast([P, P]), identity[:])
+                spread_gates(e, gates[e])
 
         def multiply(step, tiles):
             e, a = divmod(step, PASSES)
@@ -244,22 +257,29 @@ def tile_moe_nxt_lin_bias_kernel(tc, x_words, x_scales, w, b, wp, gate, offs, ou
             c_scales = tile([P, C], U8, "c_scales", "c_scales%d" % (e % 2))
             return c_bf, c_codes, c_scales
 
-        def bias_and_gate(e):
+        def add_bias(e):
             y = tile([P, PACK, C], F32, "y")
             for j in range(PACK):
                 nc.scalar.activation(y[:, j, :], sums[e][j][:, :C], IDENTITY, bias=expert_bias[e][:, j : j + 1])
+            return y
+
+        def bias_and_gate(e):
+            y = add_bias(e)
             c_parts = c_tiles(e, "c_bf")
             apply_gate(e, ALL_SLOTS, y[:], c_parts[0])
             return c_parts
 
-        def project_all(e, c_bf, c_codes, c_scales):
+        def project_all(e, c_bf, c_codes, c_scales, names=("out_bank0", "out_bank1")):
             quantise_c(ALL_SLOTS, c_bf, c_codes, c_scales)
-            projected[e] = [banks.tile([P, C], F32, name="out_bank%d" % m) for m in range(OUT_TILES)]
+            projected[e] = [banks.tile([P, C], F32, name=name) for name in names]
             for m in range(OUT_TILES):
                 project(m, projected[e][m], c_codes[:], c_scales[:])
 
-        def scatter(e, m, staged):
-            nc.vector.tensor_copy(result[m][:].indirect(slots_of(e)), staged)
+        def listed(e, cols):
+            return slots_of(e)[:, cols.start // 16 : cols.stop // 16]
+
+        def scatter(e, m, staged, cols=ALL_SLOTS):
+            nc.vector.tensor_copy(result[m][:].indirect(listed(e, cols)), staged)
 
         everything = list(range(PACK))
         for e0 in (0, HALF):
@@ -268,7 +288,7 @@ def tile_moe_nxt_lin_bias_kernel(tc, x_words, x_scales, w, b, wp, gate, offs, ou
             gather_scales(e0)
         for a in range(1, PASSES):
             gather_words(0, a, tile([P, HALF * C], U32, "slot_words0_%d" % a)[:])
-        for e in range(E):
+        for e in range(E - 1):
             first, middle, last = range(PASSES * e, PASSES * (e + 1))
             round_weights(first)
             if e == 0:
@@ -293,38 +313,83 @@ def tile_moe_nxt_lin_bias_kernel(tc, x_words, x_scales, w, b, wp, gate, offs, ou
             quantise(middle, everything, middle_scales)
             multiply(middle, everything)
             round_weights(last)
-            for tiles in [everything] if e < E - 1 else [LOW, HIGH]:
-                quantise(last, tiles)
-                multiply(last, tiles)
+            quantise(last, everything)
+            multiply(last, everything)
             if e == 0:
                 held_words = tile([P, PASSES - 1, HALF * C], U32, "held_words", raw_tag(last))
                 for a in range(1, PASSES):
                     gather_words(HALF, a, held_words[:, a - 1, :])
             else:
-                for m in range(OUT_TILES if e < E - 1 else 1):
-                    nc.scalar.copy(out=raw[last][:, m, :C], in_=projected[e - 1][m][:])
-                    scatter(e - 1, m, raw[last][:, m, :C])
+                for m in range(OUT_TILES):
+                    cols = slice(0, EARLY_SLOTS) if e == E - 2 else ALL_SLOTS
+                    nc.scalar.copy(out=raw[last][:, m, cols], in_=projected[e - 1][m][:, cols])
+                    scatter(e - 1, m, raw[last][:, m, cols], cols)
             for step in range(first + RAW_BUFS, min(last + RAW_BUFS + 1, STEPS)):
                 load_weights(step)
 
         e = E - 1
-        c_parts = c_tiles(e, "wp_bf")
-        y_halves = []
-        for h, cols in enumerate(SLOT_HALVES):
-            y_halves.append(tile([P, PACK, C // 2], F32, "y_half", ("c_bf", "early_bias")[h]))
-            for j in range(PACK):
-                columns = early_bias if h == 0 and j < PACK - 1 else expert_bias[e]
-                nc.scalar.activation(y_halves[h][:, j, :], sums[e][j][:, cols], IDENTITY, bias=columns[:, j : j + 1])
-        for h, cols in enumerate(SLOT_HALVES):
-            apply_gate(e, cols, y_halves[h][:], c_parts[0])
-        held = tile([P, C], F32, "held", "expert_bias%d" % e)
-        nc.vector.tensor_copy(out=held[:], in_=projected[e - 1][1][:])
-        project_all(e, *c_parts)
-        scatter(e - 1, 1, held[:])
-        staged = tile([P, OUT_TILES, C], F32, "staged", "wp_raw")
+        first, middle, last = range(PASSES * e, PASSES * (e + 1))
+        round_weights(first)
+        y = add_bias(e - 1)
+        quantise(first, everything)
+        open_sums(e)
+        multiply(first, everything)
+        middle_low = w_middle[:, : len(LOW) * QUARTER]
+        start = PACK * QUARTER - LATE_COLUMNS * PACK
+        middle_high = w_ends[(e + 1) % 2][:, start : start + len(HIGH) * QUARTER]
+        round_on_gpsimd(middle, HIGH, middle_high, slice(LATE_COLUMNS, P))
+        round_on_gpsimd(middle, HIGH, middle_high, slice(0, LATE_COLUMNS))
+        round_on_scalar(middle, LOW, middle_low)
+        c_parts = c_tiles(e - 1, raw_tag(first))
+        apply_gate(e - 1, ALL_SLOTS, y[:], c_parts[0])
+        quantise(middle, LOW, tile([P, N // 2], U8, "late_scales", "expert_bias%d" % (e - 1))[:], middle_low)
+        project_all(e - 1, *c_parts, names=("sum_bank0", "sum_bank1"))
+        multiply(middle, LOW)
+        quantise(middle, HIGH, values=middle_high)
+        multiply(middle, HIGH)
+        for tiles in (LOW, HIGH):
+            values = tile([P, len(tiles) * QUARTER], BF16, "last_rounded", raw_tag(PASSES + tiles[0]))
+            if tiles == LOW:
+                round_on_scalar(last, tiles, values[:])
+            else:
+                round_on_scalar(last, tiles, values[:], slice(0, P // 2))
+                dst, src = pair_views(last, tiles, values[:], slice(P // 2, P))
+                nc.vector.tensor_copy(out=dst, in_=src)
+            quantise(last, tiles, values=values[:])
+            multiply(last, tiles)
+        rest = C - EARLY_SLOTS
+        across = slots_of(e - 2, 2)[:, EARLY_SLOTS // 16 :]
         for m in range(OUT_TILES):
-            nc.scalar.copy(out=staged[:, m, :], in_=projected[e][m][:])
-            scatter(e, m, staged[:, m, :])
+            nc.scalar.copy(out=raw[last][:, m, :rest], in_=projected[e - 2][m][:, EARLY_SLOTS:])
+            copy_out = nc.vector.tensor_copy if m else nc.scalar.copy
+            copy_out(out=raw[last][:, m, rest : rest + C], in_=projected[e - 1][m][:])
+        for m in range(OUT_TILES):
+            nc.scalar.activation(result[m][:].indirect(across), raw[last][:, m, : rest + C], COPY)
+
+        c_planes = tile([P, PACK, C], BF16, "c_planes", "c_bf")
+        for j, cols in [(j, ALL_SLOTS) for j in LOW] + [(j, cols) for cols in SLOT_HALVES for j in HIGH]:
+            nc.vector.scalar_tensor_tensor(
+                c_planes[:, j, cols], sums[e][j][:, cols], expert_bias[e][:, j : j + 1], last_gates[:, cols], ADD, MULT
+            )
+        c_bf, c_codes, c_scales = c_tiles(e, "wp_bf")
+        for h, cols in enumerate(SLOT_HALVES):
+            nc.vector.tensor_copy(
+                out=c_bf[:, cols.start * PACK : cols.stop * PACK].rearrange("p (s i j) -> p s j i", i=PACK, j=PACK),
+                in_=c_planes[:, :, cols].rearrange("p j (s i) -> p s j i", i=PACK),
+            )
+        for cols in SLOT_HALVES:
+            quantise_c(cols, c_bf, c_codes, c_scales)
+        staged = tile([P, OUT_TILES, C], F32, "staged", "wp_raw")
+        halves = [banks.tile([P, C // 2], F32, name=name) for name in ("out_bank0", "sum_bank0")]
+        for bank, cols in zip(halves, SLOT_HALVES):
+            project(0, bank, c_codes[:, cols], c_scales[:, cols])
+        second = banks.tile([P, C], F32, name="out_bank1")
+        project(1, second, c_codes[:], c_scales[:])
+        for bank, cols in zip(halves, SLOT_HALVES):
+            nc.vector.tensor_copy(out=staged[:, 0, cols], in_=bank[:])
+        nc.vector.tensor_copy(out=staged[:, 1, :], in_=second[:])
+        scatter(e, 0, staged[:, 0, :])
+        scatter(e, 1, staged[:, 1, :])
 
         for m in range(OUT_TILES):
             nc.sync.dma_start(out=out[m * P : (m + 1) * P, :], in_=result[m][:])

from contextlib import ExitStack

import concourse.mybir as mybir
from concourse.masks import make_identity

K, T, E, C, N, M = 1536, 1536, 6, 256, 512, 256
P = 128
FLOPS = 2 * K * N * E * C + 2 * N * M * T
BYTES = K * T + K * T // 32 + 4 * (E * K * N + N * E + N * M + E * C + M * T) + 2 * P * (T // 16)

F32 = mybir.dt.float32
BF16 = mybir.dt.bfloat16
I32 = mybir.dt.int32
U32 = mybir.dt.uint32
U16 = mybir.dt.uint16
U8 = mybir.dt.uint8
FP8X4 = mybir.dt.float8_e4m3fn_x4
COPY = mybir.ActivationFunctionType.Copy
IDENTITY = mybir.ActivationFunctionType.Identity
MULT = mybir.AluOpType.mult
ADD = mybir.AluOpType.add

PACK = 4
PAIR = 2
KP = P * PACK
PASSES = K // KP
STEPS = E * PASSES
QUADRANTS = P // 32
SCALE_ROWS = 4
OUT_TILES = M // P
LIST_COLS = C // 16
HALF = E // 2
QUARTER = P * PACK
ALL_SLOTS = slice(0, C)
LOW, HIGH = [0, 1], [2, 3]
SLOT_HALVES = [slice(0, C // 2), slice(C // 2, C)]
EARLY_SLOTS = 192
RAW_BUFS = 16
CODE_BUFS = 4
SUM_BANKS = 6
POOL_TILES = 2
POOL_COLUMNS = P // 4
LATE_COLUMNS = 80


def tile_moe_nxt_lin_bias_kernel(tc, x_words, x_scales, w, b, wp, gate, offs, out):
    nc = tc.nc
    with ExitStack() as ctx:
        keep = ctx.enter_context(tc.tile_pool(name="keep", bufs=1))
        banks = ctx.enter_context(tc.psum_pool(name="banks", bufs=1))

        def tile(shape, dtype, name, tag=None):
            return keep.tile(shape, dtype, name=name, tag=tag or name, align_bytes=256)

        def raw_tag(step):
            return "raw%d" % (step % RAW_BUFS)

        offsets = keep.tile([P, T // 16], U16, name="offsets")
        nc.sync.dma_start(offsets[:], offs)

        token_scales = tile([P, T // 4], I32, "token_scales")
        gate_rows = tile([P, P], F32, "gate_rows")
        nc.vector.memset(gate_rows[:], 0.0)
        nc.vector.memset(token_scales[:], 0)
        for q in range(QUADRANTS):
            nc.gpsimd.dma_start(
                out=token_scales[32 * q : 32 * q + SCALE_ROWS * PASSES, :],
                in_=x_scales[:, SCALE_ROWS * q : SCALE_ROWS * (q + 1), :].bitcast(I32),
            )
        identity = tile([P, P], F32, "identity")
        make_identity(nc, identity[:])

        token_words = [tile([P, T], I32, "token_words%d" % a) for a in range(PASSES)]
        raw = {}

        def load_tokens(a):
            nc.sync.dma_start(out=token_words[a][:], in_=x_words[a].rearrange("p t r -> p (t r)").bitcast(I32))

        def load_weights(step):
            e, a = divmod(step, PASSES)
            raw[step] = tile([P, PACK, N], F32, "raw", raw_tag(step))
            nc.sync.dma_start(
                out=raw[step][:].rearrange("p r n -> p (r n)"),
                in_=w[e, a * KP : (a + 1) * KP, :].rearrange("(p r) n -> p (r n)", r=PACK),
            )

        load_tokens(0)
        load_tokens(1)
        load_weights(0)
        nc.sync.dma_start(out=gate_rows[: T // P, :], in_=gate[0].rearrange("(c s) -> c s", s=P))
        load_weights(1)
        load_weights(2)
        load_tokens(2)
        wp_raw = tile([P, PACK, M], F32, "wp_raw")
        nc.sync.dma_start(out=wp_raw[:].rearrange("p j f -> p (j f)"), in_=wp.rearrange("(p j) f -> p (j f)", j=PACK))
        load_weights(PASSES)
        bias = tile([P, PACK * E], F32, "bias")
        nc.sync.dma_start(out=bias[:], in_=b.rearrange("(p j) e -> p (j e)", j=PACK))
        for step in range(PASSES + 1, RAW_BUFS):
            load_weights(step)

        turned = banks.tile([P, C], F32, name="out_bank0")
        nc.tensor.transpose(turned[:, :P], gate_rows[:], identity[:])
        slot_gate = tile([P, T // P], F32, "slot_gate")
        nc.scalar.copy(out=slot_gate[:], in_=turned[:, : T // P])

        def spread_gates(e, bank):
            for h in range(C // P):
                column = slot_gate[:, e * C // P + h : e * C // P + h + 1]
                nc.tensor.transpose(bank[:, h * P : (h + 1) * P], column.to_broadcast([P, P]), identity[:])

        spread = banks.tile([P, C], F32, name="out_bank1")
        spread_gates(E - 1, spread)
        last_gates = tile([P, C], F32, "last_gates")
        nc.scalar.copy(out=last_gates[:], in_=spread[:])

        def bias_columns(e, name, count):
            columns = tile([P, count], F32, name)
            nc.scalar.copy(out=columns[:], in_=bias[:, e::E][:, :count])
            return columns

        expert_bias = [bias_columns(e, "expert_bias%d" % e, PACK) for e in range(E)]

        result = [tile([P, T], F32, "result%d" % m) for m in range(OUT_TILES)]
        wp_codes = tile([P, M], U32, "wp_codes")
        w_ends = [tile([P, (2 * PACK - POOL_TILES) * QUARTER], BF16, "w_ends%d" % h) for h in range(2)]
        w_middle = tile([P, N * PACK], BF16, "w_middle")
        slot_words, slot_scales, rounded, codes = {}, {}, {}, {}
        sums, gates, projected, early_scales = {}, {}, {}, {}

        def slots_of(e, count=1):
            return offsets[:, e * LIST_COLS : (e + count) * LIST_COLS]

        def gather_words(e0, a, words):
            nc.vector.tensor_copy(words, token_words[a][:].bitcast(U32).indirect(slots_of(e0, HALF)))
            for e in range(e0, e0 + HALF):
                slot_words[e, a] = words[:, (e - e0) * C : (e - e0 + 1) * C]

        def gather_scales(e0):
            scales = tile([P, HALF * C], U8, "slot_scales%d" % e0)
            nc.vector.tensor_copy(scales[:], token_scales[:].bitcast(U8).indirect(slots_of(e0, HALF)))
            for e in range(e0, e0 + HALF):
                for a in range(PASSES):
                    slot_scales[e, a] = scales[SCALE_ROWS * a : P, (e - e0) * C : (e - e0 + 1) * C]

        def pair_views(step, tiles, values, cols=slice(0, P)):
            dst = values.rearrange("p (j c r) -> p c r j", j=len(tiles), r=PACK)
            src = raw[step][:].rearrange("p r (c j) -> p c r j", j=PACK)
            return dst[:, cols], src[:, cols, :, tiles[0] : tiles[-1] + 1]

        def round_on_scalar(step, tiles, values, cols=slice(0, P)):
            dst, src = pair_views(step, tiles, values, cols)
            nc.scalar.copy(out=dst, in_=src)

        def round_on_gpsimd(step, tiles, values, cols=slice(0, P)):
            dst, src = pair_views(step, tiles, values, cols)
            nc.gpsimd.tensor_scalar(dst, src, 1.0, 0.0, MULT, ADD)

        def round_weights(step):
            e, a = divmod(step, PASSES)
            if a == 0:
                w_bf = w_ends[(e + 1) % 2][:, : N * PACK]
            elif a < PASSES - 1:
                w_bf = w_middle[:]
            else:
                w_bf = w_ends[e % 2][:, (PACK - POOL_TILES) * QUARTER :]
            rounded[step] = w_bf
            low, high = w_bf[:, : 2 * QUARTER], w_bf[:, 2 * QUARTER :]
            if step == 0:
                nc.scalar.activation(*pair_views(step, LOW, low), COPY)
                nc.scalar.activation(*pair_views(step, HIGH, high), COPY)
            elif e == 0:
                round_on_scalar(step, LOW, low)
                round_on_scalar(step, HIGH, high)
            elif a < PASSES - 1:
                round_on_gpsimd(step, HIGH, high)
                round_on_scalar(step, LOW, low)
            else:
                round_on_gpsimd(step, HIGH, high, slice(0, POOL_COLUMNS))
                round_on_scalar(step, LOW, low, slice(0, P // 2))
                round_on_scalar(step, HIGH, high, slice(POOL_COLUMNS, P))
                round_on_scalar(step, LOW, low, slice(P // 2, P))

        def quantise(step, tiles, w_scales=None, values=None):
            ring = "%d_%d" % (step % CODE_BUFS, tiles[0])
            w_codes = tile([P, len(tiles) * P], U32, "w_codes", "w_codes" + ring)
            if w_scales is None:
                w_scales = tile([P, len(tiles) * P], U8, "w_scales", "w_scales" + ring)[:]
            if values is None:
                values = rounded[step][:, tiles[0] * QUARTER : (tiles[-1] + 1) * QUARTER]
            nc.vector.quantize_mx(out=w_codes[:].bitcast(FP8X4), scales=w_scales, in_=values)
            for place, j in enumerate(tiles):
                cols = slice(place * P, (place + 1) * P)
                codes[step, j] = (w_codes[:, cols], w_scales[:, cols])

        def open_sums(e):
            sums[e] = [
                banks.tile([P, 2 * C], F32, name="sum_bank%d" % ((PACK * e + j) % SUM_BANKS)) for j in range(PACK)
            ]
            if e < E - 1:
                gates[e] = sums[e][PACK - 1][:, C:]
                spread_gates(e, gates[e])

        def multiply(step, tiles):
            e, a = divmod(step, PASSES)
            for j in tiles:
                w_codes, w_scales = codes[step, j]
                nc.tensor.matmul_mx(
                    out=sums[e][j][:, :C],
                    lhsT=w_codes.bitcast(FP8X4),
                    lhsT_scale=w_scales,
                    rhs=slot_words[e, a].bitcast(FP8X4),
                    rhs_scale=slot_scales[e, a],
                    start=(a == 0),
                    stop=(a == PASSES - 1),
                )

        def quantise_wp(wp_scales):
            wp_bf = tile([P, M * PACK], BF16, "wp_bf")
            nc.scalar.copy(
                out=wp_bf[:].rearrange("p (f i j) -> p f j i", i=PAIR, j=PACK),
                in_=wp_raw[:].rearrange("p j (f i) -> p f j i", i=PAIR),
            )
            nc.vector.quantize_mx(out=wp_codes[:].bitcast(FP8X4), scales=wp_scales, in_=wp_bf[:])

        def apply_gate(e, cols, y, c_bf):
            slot_gates = gates[e][:, cols].rearrange("p (s i) -> p s i", i=PAIR)
            nc.vector.tensor_tensor(
                c_bf[:, cols.start * PACK : cols.stop * PACK].rearrange("p (s i j) -> p s j i", i=PAIR, j=PACK),
                y.rearrange("p j (s i) -> p s j i", i=PAIR),
                slot_gates.unsqueeze(2).to_broadcast([P, (cols.stop - cols.start) // PAIR, PACK, PAIR]),
                MULT,
            )

        def quantise_c(cols, c_bf, c_codes, c_scales):
            nc.vector.quantize_mx(
                out=c_codes[:, cols].bitcast(FP8X4),
                scales=c_scales[:, cols],
                in_=c_bf[:, cols.start * PACK : cols.stop * PACK],
            )

        def project(m, bank, c_codes, c_scales):
            rows = slice(m * P, (m + 1) * P)
            nc.tensor.matmul_mx(
                out=bank[:],
                lhsT=wp_codes[:, rows].bitcast(FP8X4),
                lhsT_scale=early_scales[1][:, 2 * P :][:, rows],
                rhs=c_codes.bitcast(FP8X4),
                rhs_scale=c_scales,
                start=True,
                stop=True,
            )

        def c_tiles(e, tag):
            c_bf = tile([P, C * PACK], BF16, "c_bf", tag)
            c_codes = tile([P, C], U32, "c_codes", "c_codes%d" % (e % 2))
            c_scales = tile([P, C], U8, "c_scales", "c_scales%d" % (e % 2))
            return c_bf, c_codes, c_scales

        def add_bias(e):
            y = tile([P, PACK, C], F32, "y")
            for j in range(PACK):
                nc.scalar.activation(y[:, j, :], sums[e][j][:, :C], IDENTITY, bias=expert_bias[e][:, j : j + 1])
            return y

        def bias_and_gate(e):
            y = add_bias(e)
            c_parts = c_tiles(e, "c_bf")
            apply_gate(e, ALL_SLOTS, y[:], c_parts[0])
            return c_parts

        def project_all(e, c_bf, c_codes, c_scales, names=("out_bank0", "out_bank1")):
            quantise_c(ALL_SLOTS, c_bf, c_codes, c_scales)
            projected[e] = [banks.tile([P, C], F32, name=name) for name in names]
            for m in range(OUT_TILES):
                project(m, projected[e][m], c_codes[:], c_scales[:])

        def listed(e, cols):
            return slots_of(e)[:, cols.start // 16 : cols.stop // 16]

        def scatter(e, m, staged, cols=ALL_SLOTS):
            nc.vector.tensor_copy(result[m][:].indirect(listed(e, cols)), staged)

        everything = list(range(PACK))
        for e0 in (0, HALF):
            gather_words(e0, 0, tile([P, HALF * C], U32, "slot_words%d_0" % e0)[:])
        for e0 in (0, HALF):
            gather_scales(e0)
        for a in range(1, PASSES):
            gather_words(0, a, tile([P, HALF * C], U32, "slot_words0_%d" % a)[:])
        for e in range(E - 1):
            first, middle, last = range(PASSES * e, PASSES * (e + 1))
            round_weights(first)
            if e == 0:
                middle_scales = None
                quantise(first, everything)
                open_sums(e)
                multiply(first, everything)
            else:
                c_parts = bias_and_gate(e - 1)
                width = 2 * P + (M if e == 1 else 0)
                early_scales[e] = tile([P, width], U8, "early_scales", "expert_bias%d" % (e - 1))
                quantise(first, HIGH, early_scales[e][:, : 2 * P])
                if e == 1:
                    quantise_wp(early_scales[e][:, 2 * P :])
                project_all(e - 1, *c_parts)
                planes = tile([P, 2 * P + N], U8, "late_scales", "y")
                middle_scales = planes[:, 2 * P :]
                quantise(first, LOW, planes[:, : 2 * P])
                open_sums(e)
                multiply(first, HIGH + LOW)
            round_weights(middle)
            quantise(middle, everything, middle_scales)
            multiply(middle, everything)
            round_weights(last)
            quantise(last, everything)
            multiply(last, everything)
            if e == 0:
                held_words = tile([P, PASSES - 1, HALF * C], U32, "held_words", raw_tag(last))
                for a in range(1, PASSES):
                    gather_words(HALF, a, held_words[:, a - 1, :])
            else:
                for m in range(OUT_TILES):
                    cols = slice(0, EARLY_SLOTS) if e == E - 2 else ALL_SLOTS
                    nc.scalar.copy(out=raw[last][:, m, cols], in_=projected[e - 1][m][:, cols])
                    scatter(e - 1, m, raw[last][:, m, cols], cols)
            for step in range(first + RAW_BUFS, min(last + RAW_BUFS + 1, STEPS)):
                load_weights(step)

        e = E - 1
        first, middle, last = range(PASSES * e, PASSES * (e + 1))
        round_weights(first)
        y = add_bias(e - 1)
        quantise(first, everything)
        open_sums(e)
        multiply(first, everything)
        middle_low = w_middle[:, : len(LOW) * QUARTER]
        start = PACK * QUARTER - LATE_COLUMNS * PACK
        middle_high = w_ends[(e + 1) % 2][:, start : start + len(HIGH) * QUARTER]
        round_on_gpsimd(middle, HIGH, middle_high, slice(LATE_COLUMNS, P))
        round_on_gpsimd(middle, HIGH, middle_high, slice(0, LATE_COLUMNS))
        round_on_scalar(middle, LOW, middle_low)
        c_parts = c_tiles(e - 1, raw_tag(first))
        apply_gate(e - 1, ALL_SLOTS, y[:], c_parts[0])
        quantise(middle, LOW, tile([P, N // 2], U8, "late_scales", "expert_bias%d" % (e - 1))[:], middle_low)
        project_all(e - 1, *c_parts, names=("sum_bank0", "sum_bank1"))
        multiply(middle, LOW)
        quantise(middle, HIGH, values=middle_high)
        multiply(middle, HIGH)
        for tiles in (LOW, HIGH):
            values = tile([P, len(tiles) * QUARTER], BF16, "last_rounded", raw_tag(PASSES + tiles[0]))
            if tiles == LOW:
                round_on_scalar(last, tiles, values[:])
            else:
                round_on_scalar(last, tiles, values[:], slice(0, P // 2))
                dst, src = pair_views(last, tiles, values[:], slice(P // 2, P))
                nc.vector.tensor_copy(out=dst, in_=src)
            quantise(last, tiles, values=values[:])
            multiply(last, tiles)
        rest = C - EARLY_SLOTS
        across = slots_of(e - 2, 2)[:, EARLY_SLOTS // 16 :]
        for m in range(OUT_TILES):
            nc.scalar.copy(out=raw[last][:, m, :rest], in_=projected[e - 2][m][:, EARLY_SLOTS:])
            copy_out = nc.vector.tensor_copy if m else nc.scalar.copy
            copy_out(out=raw[last][:, m, rest : rest + C], in_=projected[e - 1][m][:])
        for m in range(OUT_TILES):
            nc.scalar.activation(result[m][:].indirect(across), raw[last][:, m, : rest + C], COPY)

        c_planes = tile([P, PACK, C], BF16, "c_planes", "c_bf")
        for j, cols in [(j, ALL_SLOTS) for j in LOW] + [(j, cols) for cols in SLOT_HALVES for j in HIGH]:
            nc.vector.scalar_tensor_tensor(
                c_planes[:, j, cols], sums[e][j][:, cols], expert_bias[e][:, j : j + 1], last_gates[:, cols], ADD, MULT
            )
        c_bf, c_codes, c_scales = c_tiles(e, "wp_bf")
        for h, cols in enumerate(SLOT_HALVES):
            nc.vector.tensor_copy(
                out=c_bf[:, cols.start * PACK : cols.stop * PACK].rearrange("p (s i j) -> p s j i", i=PACK, j=PACK),
                in_=c_planes[:, :, cols].rearrange("p j (s i) -> p s j i", i=PACK),
            )
        for cols in SLOT_HALVES:
            quantise_c(cols, c_bf, c_codes, c_scales)
        staged = tile([P, OUT_TILES, C], F32, "staged", "wp_raw")
        halves = [banks.tile([P, C // 2], F32, name=name) for name in ("out_bank0", "sum_bank0")]
        for bank, cols in zip(halves, SLOT_HALVES):
            project(0, bank, c_codes[:, cols], c_scales[:, cols])
        second = banks.tile([P, C], F32, name="out_bank1")
        project(1, second, c_codes[:], c_scales[:])
        for bank, cols in zip(halves, SLOT_HALVES):
            nc.vector.tensor_copy(out=staged[:, 0, cols], in_=bank[:])
        nc.vector.tensor_copy(out=staged[:, 1, :], in_=second[:])
        scatter(e, 0, staged[:, 0, :])
        scatter(e, 1, staged[:, 1, :])

        for m in range(OUT_TILES):
            nc.sync.dma_start(out=out[m * P : (m + 1) * P, :], in_=result[m][:])
